import numpy as np, ml_dtypes
CORES = [9,25,41,57]
N = 4
BF = ml_dtypes.bfloat16
def gentries(a):
    return np.ascontiguousarray(a.reshape(8, 16, -1).transpose(0, 2, 1)).reshape(8, -1)
def gtable(e):
    e = np.asarray(e); return np.ascontiguousarray(e.reshape(8, -1, 16).transpose(0, 2, 1)).reshape(128, -1).astype(np.int32)
D, NB, S, NEED, RO = 2048, 256, 16, 3, 4
P = S // 2; M = NB * P; W = D + M
TOP, NEAR = 255, 16
def parts(rng):
    pat = 2 * rng.integers(0, 2, (N, 8, 16, 1)) - 1; sgn = 2 * rng.integers(0, 2, (N, 8, 1, D)) - 1
    amp = rng.random((N, 8, 1, D)) * np.where(rng.random((N, 8, 1, D)) < 0.88, 49.5, 126.5)
    x = np.clip(np.rint(127.5 + pat * sgn * amp + 8.8 * rng.standard_normal((N, 8, 16, D))), 0, TOP).astype(np.int64)
    return x, rng.integers(0, 2 * W, (N, 8, D)), rng.integers(0, 2 * W, (N, 8, D)), rng.integers(0, 2 * W, (N, 8, NB, S)), rng.integers(0, 2, (N, 8, NB))
def pack(x, k0, k1, L, f):
    return {"faces": np.ascontiguousarray(x.reshape(N, 128, D)).astype(np.float32).astype(BF), "kid0": k0.astype(np.int32), "kid1": k1.astype(np.int32),
            "belts": np.stack([gtable(a.reshape(8, -1)) for a in L]), "flip": f.astype(np.int32)}
def planted(rng, z, n, few):
    x, k0, k1, L, f = z; cs = np.array([0, 1, 7, 8, 9, 10, 15, 16])
    hit = np.argsort(np.argsort(rng.random((N, 8, NB, P)), axis=-1), axis=-1) < n[..., None]
    for g in range(8):
        o = rng.permutation(D); sen = rng.integers(0, 2, D); c = np.zeros(D, np.int64); c[o] = cs[(np.arange(D) // 4) % 8]
        bl, fa, pt = o[1::4], o[2::4], o[3::4]; hi = fa[c[fa] >= 9]; lo = fa[c[fa] < 9]; sh = (N, 16, len(fa))
        close = np.where(rng.random(sh) < 0.5, NEAR, rng.integers(0, NEAR + 1, sh)); far = np.where(rng.random(sh) < 0.5, NEAR + 1, rng.integers(NEAR + 1, TOP + 1, sh))
        v = np.where(np.argsort(rng.random(sh), axis=1) < c[fa], close, far)
        y = x[:, g]; y[:, :, fa] = np.where(sen[fa] == 1, TOP - v, v); y[:, :, bl] = TOP * sen[bl]
        def twin(a):
            return 2 * D * ((a < M) & (rng.random(a.shape) < 0.5))
        def good(a):
            return 2 * a + sen[a] + twin(a)
        def some(a):
            return np.full((N, NB, P), a[int(rng.integers(0, len(a)))]) if few[g] else a[rng.integers(0, len(a), (N, NB, P))]
        q0 = k0[:, g]; q1 = k1[:, g]
        q0[:, pt] = good(bl[rng.integers(0, len(bl), (N, len(pt)))]); q1[:, pt] = good(bl[rng.integers(0, len(bl), (N, len(pt)))]) ^ 1
        lh = good(np.where(hit[:, g], some(hi), some(lo))); pk = some(pt); lk = 2 * pk + rng.integers(0, 2, pk.shape) + twin(pk)
        k = (2 * np.arange(P) + f[:, g, :, None]) % S; l = L[:, g]
        np.put_along_axis(l, k, lk, 2); np.put_along_axis(l, (k + 1) % S, lh, 2)
    return x, k0, k1, L, f
def setup_inputs(rng):
    return pack(*parts(rng))
def setup_inputs_spread(rng):
    x, k0, k1, L, f = parts(rng)
    pat = 2 * rng.integers(0, 2, (N, 8, 16, 1)) - 1; sgn = 2 * rng.integers(0, 2, (N, 8, 1, D)) - 1; amp = np.exp2(7.5 * rng.random((N, 8, 1, D)) - 0.5)
    x = np.clip(np.rint(127.5 + pat * sgn * amp + 5.5 * rng.standard_normal((N, 8, 16, D))), 0, TOP).astype(np.int64)
    x = np.where(rng.random((N, 8, 1, D)) < 0.125, rng.integers(0, TOP + 1, x.shape), x)
    z = []
    for a in (k0, k1, L):
        e = np.minimum((2 * W * rng.random(a.shape) ** 3).astype(np.int64), 2 * W - 1); e[:, 1::2] = 2 * W - 1 - e[:, 1::2]; z.append(e)
    f = (rng.random((N, 8, NB)) < 0.1 + 0.8 * rng.random((N, 8, 1))).astype(np.int64)
    return pack(x, z[0], z[1], z[2], f)
def mixends(rng, shape):
    return np.where(rng.random(shape) < 0.75, (2 * W - 1) * rng.integers(0, 2, shape), rng.integers(0, 2 * W, shape))
def setup_inputs_ends(rng):
    kind = rng.integers(0, 3, (N, 8, 1, D)); x = TOP * np.where(kind == 2, rng.integers(0, 2, (N, 8, 16, D)), kind)
    k0 = mixends(rng, (N, 8, D)); k1 = mixends(rng, (N, 8, D)); k0[..., M - 1] = 0; k1[..., 0] = 0
    f = rng.integers(0, 2, (N, 8, NB)); f[..., 0] = 0; f[..., NB - 1] = 1
    for q in (0, 1, N - 1): x[q, :, :, M - 1] = TOP - x[q, :, :, 0]
    L = mixends(rng, (N, 8, NB, S)); ks = ((np.arange(S) - f[..., None]) & 1) == 0; hs = (2 * W - 1) * rng.integers(0, 2, L.shape)
    calm = np.where(ks, 0, hs); wild = np.where(ks, 2 * W - 1, hs); full = np.where(ks, 2 * W - 1, 0)
    L[:, :, NB - 1] = full[:, :, NB - 1]; L[:, :, NB - 2] = 0
    L[0] = calm[0]; L[1] = calm[1]; L[1, 7, NB - 1] = full[1, 7, NB - 1]; L[N - 1] = wild[N - 1]
    return pack(x, k0, k1, L, f)
def setup_inputs_corners(rng):
    x, k0, k1, L, f = parts(rng); own = 2 * np.arange(D)
    for a in (k0, k1):
        w = rng.integers(0, 8, a.shape); e = rng.integers(0, 2, a.shape)
        a[...] = np.where(w == 0, own + e, np.where(w == 1, e, np.where(w == 2, 2 * W - 2 + e, np.where(w == 3, own[::-1] + e, a))))
    w = rng.integers(0, 6, (N, 8, NB, 1)); one = rng.integers(0, 2 * W, (N, 8, NB, 1))
    old = np.where(w == 0, one, np.where(w == 1, 0, np.where(w == 2, 2 * W - 1, L)))
    n = rng.choice(np.array([0, 1, NEED - 1, NEED, NEED + 1, P]), (N, 8, NB)); n[N - 1, 7, NB - 1] = P; n[0, 0, 0] = NEED; n[1, 0, 0] = NEED - 1
    x, k0, k1, L, f = planted(rng, (x, k0, k1, L, f), n, np.zeros(8, np.int64))
    m = rng.random((N, 8, NB, 1)) < 0.25; m[N - 1, 7, NB - 1] = False; m[:2, 0, 0] = False
    return pack(x, k0, k1, np.where(m, old, L), f)
def setup_inputs_crowd(rng):
    n = np.zeros((N, 8, NB), np.int64); low = np.array([0, NEED - 1]); top = np.array([NEED, P])
    for q in range(N):
        n[q] = rng.choice(low if q % 4 < 2 else top, (8, NB))
        if q % 4 == 1: n[q, 7, NB - 1] = P
        if q % 4 == 2: n[q, 7, NB - 1] = NEED - 1
    return pack(*planted(rng, parts(rng), n, 1 - np.arange(8) % 2))
def setup_inputs_stale(rng):
    x, k0, k1, L, f = parts(rng); z = int(rng.integers(0, N)); y = (z + 2) % N
    sh = (N, 16, D)
    for g in range(8):
        o = rng.permutation(D); sen = rng.integers(0, 2, D); bl, h1, h2, al, pt = o[0::5], o[1::5], o[2::5], o[3::5], o[4::5]
        c = rng.choice(np.array([0, 1, 7, 8]), (N, D)); c[:, al] = 16
        c[z, pt] = rng.choice(np.array([10, 16]), len(pt)); c[y, pt] = 9; c[z, h2] = 9; c[y, h1] = 9
        close = np.where(rng.random(sh) < 0.5, NEAR, rng.integers(0, NEAR + 1, sh)); far = np.where(rng.random(sh) < 0.5, NEAR + 1, rng.integers(NEAR + 1, TOP + 1, sh))
        v = np.where(np.argsort(rng.random(sh), axis=1) < c[:, None, :], close, far); v[:, :, bl] = 0
        x[:, g] = np.where(sen == 1, TOP - v, v)
        b0 = bl[rng.integers(0, len(bl), (N, D))]; b1 = bl[rng.integers(0, len(bl), (N, D))]
        k0[:, g] = 2 * b0 + sen[b0]; k1[:, g] = (2 * b1 + sen[b1]) ^ 1
        hp = h2[rng.integers(0, len(h2), (N, NB, P))]; hp[z] = h1[rng.integers(0, len(h1), (NB, P))]
        if 1 <= g <= 5:
            for q in (z, y):
                i = NB - 1 if g == 5 else int(rng.integers(0, NB))
                hp[q, i] = al[rng.integers(0, len(al), P)]
        pk = pt[rng.integers(0, len(pt), (N, NB, P))]
        k = (2 * np.arange(P) + f[:, g, :, None]) % S; l = L[:, g]
        np.put_along_axis(l, k, (2 * pk + sen[pk]) ^ 1, 2); np.put_along_axis(l, (k + 1) % S, 2 * hp + sen[hp], 2)
    return pack(x, k0, k1, L, f)
def check_inputs(d):
    bad = []
    for k, lo, hi in (("faces", 0, TOP), ("kid0", 0, 2 * W - 1), ("kid1", 0, 2 * W - 1), ("belts", 0, 2 * W - 1), ("flip", 0, 1)):
        v = np.asarray(d[k]).astype(np.float64)
        if not (np.min(v) >= lo and np.max(v) <= hi): bad.append("range of " + k)
        if np.any(v != np.floor(v)): bad.append("whole numbers in " + k)
    return bad
def values(x, e):
    v = np.take_along_axis(x, (e >> 1)[:, :, None, :], 3)
    return np.where((e & 1)[:, :, None, :] == 1, TOP - v, v)
def reference(faces, kid0, kid1, belts, flip):
    x = faces.astype(np.float32).astype(np.int32).reshape(N, 8, 16, D); x = np.concatenate([x, x[..., :M]], axis=3)
    k0 = kid0.astype(np.int64); k0 = np.concatenate([k0, k0[..., :M]], axis=2)
    k1 = kid1.astype(np.int64); k1 = np.concatenate([k1, k1[..., :M]], axis=2)
    L = np.stack([gentries(a) for a in belts]).astype(np.int64).reshape(N, 8, NB, S); f = flip.astype(np.int64)
    A = np.zeros(N, np.int64); new = 2 * (D + np.arange(M)).reshape(NB, P)
    for t in range(RO):
        if t > 0:
            L = np.roll(L, 1, axis=0); f = np.roll(f, 1, axis=0)
        k = (2 * np.arange(P) + f[..., None]) % S; h = (k + 1) % S
        lk = np.take_along_axis(L, k, 3); lh = np.take_along_axis(L, h, 3)
        e = lk.reshape(N, 8, M); w = lh.reshape(N, 8, M); odd = (e & 1) == 1
        c0 = np.take_along_axis(k0, e >> 1, 2); c1 = np.take_along_axis(k1, e >> 1, 2)
        a = np.where(odd, c1 ^ 1, c0); b = np.where(odd, c0 ^ 1, c1); u = b ^ 1
        fu = values(x, u); fw = values(x, w)
        near = np.add.reduce((np.abs(fu - fw) <= NEAR).astype(np.int64), axis=2)
        split = (near >= 9 + (A & 1)[:, None, None]).reshape(N, 8, NB, P)
        opens = np.add.reduce(split.astype(np.int64), axis=3) >= NEED
        go = split & opens[..., None]; gm = go.reshape(N, 8, M)
        x = np.concatenate([x[..., :D], np.where(gm[:, :, None, :], (fu + fw) >> 1, x[..., D:])], axis=3)
        k0 = np.concatenate([k0[..., :D], np.where(gm, u, k0[..., D:])], axis=2)
        k1 = np.concatenate([k1[..., :D], np.where(gm, w, k1[..., D:])], axis=2)
        l2 = np.array(L)
        np.put_along_axis(l2, k, np.where(go, a.reshape(N, 8, NB, P), lk), 3); np.put_along_axis(l2, h, np.where(go, new, lh), 3)
        L = np.where(opens[..., None], l2, L ^ 1); f = np.where(opens, f, 1 - f)
        A = np.add.reduce((~opens).astype(np.int64).reshape(N, 8 * NB), axis=1)
    return {"yx": x.reshape(N, 128, W).astype(np.float32).astype(BF), "y0": k0.astype(np.float32), "y1": k1.astype(np.float32),
            "yb": np.stack([gtable(q.reshape(8, -1)) for q in L]).astype(np.float32), "yf": f.astype(np.float32)}

@@ -1,0 +1,498 @@
+from concourse.mybir import AluOpType as ALU, ActivationFunctionType as ACT
+
+F, B, I, U, H16 = "float32", "bfloat16", "int32", "uint16", "float16"
+RO = 4
+MF = ["If", "nIf", "n2If", "Upf", "IUpf", "DnIf", "U16", "E0", "E1", "O0", "O1",
+      "a0", "a1", "b0", "b1", "c0", "c1", "d0", "d1", "FT"]
+MB = ["Ib", "nIb", "n4I", "I2k", "n8I", "DnIb", "IUp8", "Up8", "B8I", "nB4", "EI8", "CC", "GX", "GX0", "GX1",
+      "C16M", "C16", "QT", "N2k", "C20", "C3", "DnI8"]
+SCRATCH = {
+    "TF0": ("sbuf", [128, 10240], B), "TF1": ("sbuf", [128, 10240], B),
+    "TK0": ("sbuf", [128, 6144], B), "TK1": ("sbuf", [128, 6144], B),
+    "G": ("sbuf", [128, 2048], B), "FW": ("sbuf", [128, 2048], B), "D": ("sbuf", [128, 2048], B), "NR": ("sbuf", [128, 2048], B),
+    "IN0": ("sbuf", [128, 2, 192], U), "IN1": ("sbuf", [128, 2, 192], U), "IN2": ("sbuf", [128, 2, 192], U), "IN3": ("sbuf", [128, 2, 192], U),
+    "OUT0": ("sbuf", [128, 384], U), "OUT1": ("sbuf", [128, 384], U), "OUT2": ("sbuf", [128, 384], U),
+    "PH": ("sbuf", [128, 2, 192], F), "R": ("sbuf", [128, 384], F), "R1": ("sbuf", [128, 256], F), "Q": ("sbuf", [128, 256], F),
+    "sK": ("sbuf", [128, 128], B), "Z": ("sbuf", [128, 768], B), "SP": ("sbuf", [128, 128], B), "MK": ("sbuf", [128, 512], B),
+    "p16": ("sbuf", [128, 128], U), "u16": ("sbuf", [128, 128], U), "m16": ("sbuf", [128, 128], U),
+    "sd": ("sbuf", [128, 128], F), "TT": ("sbuf", [128, 128], B),
+    "KS0": ("sbuf", [128, 8, 128], B), "KS1": ("sbuf", [128, 8, 128], B),
+    "EI": ("sbuf", [128, 512], I), "SI": ("sbuf", [128, 512], I), "FI": ("sbuf", [128, 256], I),
+    "P0": ("sbuf", [128, 256], F), "S0": ("sbuf", [128, 256], F), "KP": ("sbuf", [128, 768], B), "FF": ("sbuf", [128, 256], B),
+    "FB": ("sbuf", [128, 256], F), "RR": ("sbuf", [128, 256], F), "KF": ("sbuf", [128, 256], F),
+    "IO": ("sbuf", [128, 64], F), "IO2": ("sbuf", [128, 128], F), "IO3": ("sbuf", [128, 128], F), "IO4": ("sbuf", [128, 128], F),
+    "MS": ("sbuf", [128, 1040], B), "CF": ("sbuf", [128, 128 * len(MF)], F), "CB": ("sbuf", [128, 128 * len(MB)], B),
+    "CH": ("sbuf", [128, 256], H16),
+    "W": ("sbuf", [128, 5 * 144], B), "ZF": ("sbuf", [128, 128], F), "ZB": ("sbuf", [128, 144], B),
+    "ONE": ("sbuf", [128, 512], B), "M4": ("sbuf", [128, 128], B),
+    "COL": ("sbuf", [128, 32], F), "COI": ("sbuf", [128, 16], I), "JK": ("sbuf", [128, 64], F),
+    "EH": ("sbuf", [128, 256], F), "FE": ("sbuf", [128, 256], F), "YB": ("sbuf", [128, 256], F), "YF": ("sbuf", [128, 256], F),
+    "YS": ("sbuf", [128, 256], F),
+    "pA": ("psum", [128, 512], F), "pX": ("psum", [128, 512], F), "pE0": ("psum", [128, 512], F), "pE1": ("psum", [128, 512], F),
+    "pZ": ("psum", [128, 512], F), "pV0": ("psum", [128, 512], F), "pV1": ("psum", [128, 512], F), "pK": ("psum", [128, 8, 128], B),
+}
+DSEM = ["dk", "db", "df", "dp", "dv", "dc0", "dc1", "dc2", "df1", "dn1", "dk1", "dyx", "dy",
+        "ox0", "ox1", "ob0", "ob1", "oy0", "oy1", "of"] + ["kc%d%d" % (t, h) for t in range(4) for h in range(2)]
+SEMAPHORES = ["sV", "sS", "sP", "sG"] + DSEM + ["ls%d%d" % (t, h) for t in range(3) for h in range(2)] \
+    + ["rs%d%d" % (t, h) for t in range(3) for h in range(2)]
+C23 = 12582912.0
+C28 = 402653184.0
+NOM = {"cy": 1.04, "pe": 0.52, "ga": 1.56, "fix": 60.0, "wake": 60.0, "dlat": 1900.0, "rlat": 4000.0, "kb": 4.5}
+ENG = {"g": ["VSSS"] * 4, "m": ["SSSV"] * 4, "k": ["SSSS"] * 4, "kev": "VV", "k0h": "S", "kb": "SVSV"}
+SEQ = "00090a07010b08020q0m03060l040o2f0g0p0h2g0r0k2i0f350u2j140s2k0w0i15161i2h05301g1j1c2x2z2l2y1k0x2m0y1n2v311l0v2w0t113q1m223g201s3a3f1v3i1x21123e1u133j1o0n3r0z3l1w170j3t363b0c24251y181p192a1z1a1q2b1b2c321r2d1d2637442e1e1t271f28291h3c2n454i3k474k41484u4j5a46495r434a4b5v424l3u3d0d3v4c3y4m2o104n2p4t4e4v2q4d5x382r5t0e4f5q4g612u664x2s4o5p4h2t4q3z3w3x6769403s4w3m4y5s686a994p3n34595b3h4r6d4z4s3o5d6u6b3p656c60506f6e6g6h6v566z5752515c545e6i585y7055536o6j5z6k6w6l6r6m6n5f6p716q5u5g6375626s235k735w745n3372645o765j5m6x5l795h5i7c9a7a777b6y787d7j6t7e7f7g7k7h7i7o7q7r8d7s7l9e8e7t8f7v7u9d9m7p9g7w9f7m7n7y7x8183848t7z8u85808h9i8g869o8i879t9n8j9l82888k9u8r8a8s8m8p898n8v8b8q9w8l8c8o8xah9v9x9ya09kaia39zak8w8y39a4ala19ca29qa59h9ba6a88za7a9af9paaabajac90ad9sao95ar9j93aeas91aqap969rat9792am98aw94axazauayanavb0b6agb1b2b3b4b5bbbdbec0bfc1cxbgbhbibcczbjc2blbkbobrbqbmcgcwbnbscyc4c3chd7btc5budcd6c6d5d4b7bvbpddb8deb9babwc7bxciccdjc8bycedhbzcbcke0cacdc9cfdfdid0dgdmdldke1e5cjd2dncle6e2dodrdpdud1dqdadsdxdtcmdve7dwd3eacnebdbe8e9cvd9ecdyctd8cseicoe3cqefcucpegcrehedepejeee4ekdzelemeneoeuexewghfjeygiezf0f1eqf4fkerevesetflf2f7f9fafzfbf3f5fcggfnglgmfdf6fmfogngffpg0fef8gofgfqgpfffsg1fwfrfhgufugqfifvg3hofyftfxgsgrgvgtgxgwgyg4hrgzg2hpg5hsh2h0gjh1h3h7hth4h5g6hqh9g8gchagdgkgehvhuhcgahwhzg9hbhxhygbhki0h6g7i3i4i5hfibi1hdici2hlh8i6i7hgiehei8ihi9iihmidiahjifhhighiimijhniliqikinioip"
+ORDER = [int(SEQ[k:k + 2], 36) for k in range(0, len(SEQ), 2)]
+
+
+def rank_program(g, core, T, topo):
+    rank = T.rank_of(core)
+    if rank is None:
+        return
+    nxt = T.cores[(rank + 1) % len(T.cores)]
+    rid, pid, _se = topo.addr(nxt)
+    rmask = topo.mask(core, nxt)
+    neng = len(topo.engines(core, nxt))
+    ops = []
+    wid = {F: 4, I: 4, B: 2, U: 2, H16: 2}
+
+    def A(n, c0=None, c1=None, st=1, p0=0, p1=128):
+        if c0 is None:
+            c0, c1 = 0, SCRATCH[n][1][-1]
+        ap = T[n][p0:p1, c0:c1] if st == 1 else T[n][p0:p1, c0:c1:st]
+        return (ap, [(n, c0, c1)], (c1 - c0 + st - 1) // st, wid[SCRATCH[n][2]], False)
+
+    def A3(n, h, k, w=1):
+        a, b = 64 * k, 64 * (k + w)
+        if h is None:
+            return (T[n][:, :, a:b], [(n, a, b), (n, 192 + a, 192 + b)], 128 * w, wid[SCRATCH[n][2]], False)
+        return (T[n][:, h, a:b], [(n, 192 * h + a, 192 * h + b)], 64 * w, wid[SCRATCH[n][2]], False)
+
+    def IX(win, off):
+        return (win[0].indirect(off[0]), win[1] + off[1], 16 * off[2], win[3], True)
+
+    def cf(n, c0=0, c1=128, st=1, p1=128):
+        k = 128 * MF.index(n); return A("CF", k + c0, k + c1, st, 0, p1)
+
+    def cb(n, c0=0, c1=128, st=1, p0=0, p1=128):
+        k = 128 * MB.index(n); return A("CB", k + c0, k + c1, st, p0, p1)
+
+    def col(k):
+        return A("COL", 4 * k, 4 * k + 1)
+
+    def op(e, fns, outs, ins, cost, sem=None, n=1, lat=0.0):
+        ops.append({"e": e, "fns": fns, "w": [r for a in outs for r in a[1]], "r": [r for a in ins for r in a[1]],
+                    "sem": sem, "n": n, "c": cost, "lat": lat})
+
+    def sa(x):
+        return x[0] if isinstance(x, tuple) else x
+
+    def aps(*xs):
+        return [x for x in xs if isinstance(x, tuple)]
+
+    def vc(o, i, two=1, fast=True):
+        if i[4]:
+            return NOM["fix"] + NOM["cy"] * NOM["ga"] * i[2]
+        return NOM["fix"] + NOM["cy"] * max(64, i[2] * two * (0.5 if fast and o[3] == 2 and i[3] == 2 else 1))
+
+    def ts(o, i, s1, o0, s2=None, o1=None):
+        if o1 is None:
+            op("V", [lambda: g.vector.tensor_scalar(o[0], i[0], sa(s1), None, o0)], [o], aps(i, s1), vc(o, i))
+        else:
+            op("V", [lambda: g.vector.tensor_scalar(o[0], i[0], sa(s1), sa(s2), o0, o1)], [o], aps(i, s1, s2), vc(o, i))
+
+    def tt(o, a, b, o0):
+        two = 2 if SCRATCH[a[1][0][0]][0] == SCRATCH[b[1][0][0]][0] else 1
+        op("V", [lambda: g.vector.tensor_tensor(o[0], a[0], b[0], o0)], [o], [a, b], vc(o, a, two, b[3] == 2))
+
+    def ms(o, c):
+        op("V", [lambda: g.vector.memset(o[0], c)], [o], [], vc(o, o))
+
+    def act(o, i, scale=1.0, bias=0.0, acc=None):
+        if acc is not None:
+            op("S", [lambda: g.scalar.activation(o[0], i[0], ACT.Identity, accum_out=acc[0])], [o, acc], [i], vc(o, i, 1, False))
+        elif bias == 0.0:
+            op("S", [lambda: g.scalar.activation(o[0], i[0], ACT.Copy, scale=scale)], [o], [i], vc(o, i, 1, False))
+        else:
+            op("S", [lambda: g.scalar.activation(o[0], i[0], ACT.Identity, bias=bias, scale=scale)], [o], [i], vc(o, i, 1, False))
+
+    def cp(o, i, e="V"):
+        if e == "S":
+            act(o, i)
+        else:
+            op("V", [lambda: g.vector.tensor_copy(o[0], i[0])], [o], [i], vc(o, i))
+
+    def flip(o, i, e="V"):
+        if e == "S":
+            act(o, i, -1.0, 255.0)
+        else:
+            ts(o, i, -1.0, ALU.mult, 255.0, ALU.add)
+
+    def mm(o, terms, start=True, stop=True, lock=False):
+        op("P", [lambda l=l, r=r, k=k: g.tensor.matmul(o[0], l[0], r[0], start and k == 0, stop and k == len(terms) - 1)
+                 for k, (l, r) in enumerate(terms)],
+           [o] + ([A("pX", 511, 512)] if lock else []), [a for lr in terms for a in lr], sum(10 + NOM["pe"] * max(min(64, l[2]), r[2]) * (4 if l[3] == 4 else 1) for l, r in terms))
+
+    def dma(o, i, sem, kb, q="Y"):
+        op(q, [lambda: (g.sync if q == "Y" else g.scalar).dma_start(o[0], i[0])], [o], [i], 100.0, sem, 16, NOM["dlat"])
+        ops[-1]["kb"] = kb
+
+    def X(ap):
+        return (ap, [])
+
+    def iota(o, pat, base, cm):
+        op("G", [lambda: g.iota(o[0], pat, base, cm, allow_small_or_imprecise_dtypes=True)], [o], [], 130 + 2 * NOM["cy"] * o[2])
+
+    def sel(o, i, pat, base, fill, cmp=ALU.not_equal, cm=1):
+        op("G", [lambda: g.affine_select(o[0], i[0], pat, cmp, fill, base, cm)], [o], [i], 170 + 2 * NOM["cy"] * o[2])
+
+    dma(A("EI", 256, 512), X(T.belts[:]), "db", 128)
+    dma(A("FI", 0, 256, 1, 0, 8), X(T.flip[:]), "df", 8, "S")
+    dma(A("EI", 0, 256, 1, 0, 64), X(T.kid0[:]), "dk", 64, "S")
+    dma(A("EI", 0, 256, 1, 64, 128), X(T.kid1[:]), "dk", 64)
+    dma(A("TF0", 0, 2048), X(T.faces[:]), "dp", 512)
+    dma(A("TF0", 2048, 4096), X(T.faces[:]), "dv", 512)
+    iota(A("IO2"), [[-1, 128]], 0, 1)
+    iota(A("IO3"), [[-16, 8], [300, 2], [-2, 8]], 0, 1)
+    iota(A("IO4"), [[-1, 8], [300, 2], [0, 8]], 0, 1)
+    iota(A("IO"), [[-1, 8], [-8, 8]], 0, 1)
+    ms(A("MS"), 0.0); ms(A("ZF"), 0.0); ms(A("ZB"), 0.0); ms(A("ONE"), 1.0); ms(A("M4"), -4.0)
+    ts(cf("If"), A("IO2"), 0.0, ALU.is_equal)
+    ts(cf("U16"), A("IO2"), 1.0, ALU.is_equal)
+    ts(cf("U16", 15, 128, 16), A("IO2", 15, 128, 16), -15.0, ALU.is_equal)
+    tt(cf("U16"), cf("U16"), cf("If"), ALU.subtract)
+    for b in range(2):
+        ts(cf("E%d" % b), A("IO3"), 300.0 * b, ALU.is_equal, 0.5, ALU.mult)
+        ts(cf("O%d" % b), A("IO3"), 300.0 * b + 1, ALU.is_equal, 0.5, ALU.mult)
+        ts(cb("GX%d" % b, p1=8), A("IO4", 0, 128, 1, 0, 8), 300.0 * b, ALU.is_equal)
+    tt(cb("GX", p1=8), cb("GX0", p1=8), cb("GX1", p1=8), ALU.add)
+    ts(A("MS", 2, 1026, 16, 64, 128), A("IO", 0, 64, 1, 64, 128), 64.0, ALU.is_equal, 0.5, ALU.mult)
+    ts(A("MS", 5, 1029, 16, 0, 64), A("IO", 0, 64, 1, 0, 64), 0.0, ALU.is_equal, 0.5, ALU.mult)
+    for n, s in (("Ib", 1.0), ("n4I", -4096.0), ("nIb", -1.0), ("I2k", 2048.0), ("n8I", -8192.0)):
+        act(cb(n), cf("If"), s)
+    act(cf("nIf"), cf("If"), -1.0); act(cf("n2If"), cf("If"), -2.0)
+    ts(A("CH", 0, 128), cf("If"), 2.0 ** -10 - 1.0, ALU.mult)
+    ts(A("CH", 128, 256), cf("If"), 2.0 ** -11 - 0.5, ALU.mult)
+
+    ts(A("SI", 256, 512), A("EI", 256, 512), 1, ALU.bitwise_and)
+    ts(A("pX", 0, 256), A("SI", 256, 512), 8191.0, ALU.mult)
+    tt(A("P0"), A("pX", 0, 256), A("EI", 256, 512), ALU.add)
+    cp(A("FF", 0, 256, 1, 0, 8), A("FI", 0, 256, 1, 0, 8))
+    mm(A("pA", 0, 256), [(cb("GX", p1=8), A("FF", 0, 256, 1, 0, 8))])
+    act(A("FB"), A("pA", 0, 256))
+    mm(A("pZ", 0, 256), [(cf("U16"), A("P0"))])
+    tt(A("pZ", 256, 512), A("pZ", 0, 256), A("FB"), ALU.mult)
+    tt(A("RR"), A("pZ", 256, 512), A("P0"), ALU.add)
+    for h in range(2):
+        for k, m in enumerate("EO"):
+            mm(A("pA", 192 * h + 64 * k, 192 * h + 64 * k + 64),
+               [(cf("%s%d" % (m, b)), A("RR", 128 * h + b, 128 * h + 128, 2)) for b in range(2)])
+        mm(A("pA", 192 * h + 128, 192 * h + 192),
+           [(cb("GX%d" % b, p1=8), A("FF", 128 * h + b, 128 * h + 128, 2, 0, 8)) for b in range(2)])
+        cp(A3("IN0", h, 0, 3), A("pA", 192 * h, 192 * h + 192))
+    ts(A("SI", 0, 256), A("EI", 0, 256), 1, ALU.bitwise_and)
+    ts(A("pX", 256, 512), A("SI", 0, 256), 8191.0, ALU.mult)
+    tt(A("pV1", 0, 256), A("pX", 256, 512), A("EI", 0, 256), ALU.add)
+    cp(A("KP", 256, 512), A("pV1", 0, 256))
+    tt(A("KP", 512, 768), A("pV1", 0, 256), A("KP", 256, 512), ALU.subtract)
+    ts(A("KP", 0, 256), A("SI", 0, 256), 2.0, ALU.mult, -1.0, ALU.add)
+    for k, bank in enumerate(["pE0", "pE1", "pV0", "pV1"]):
+        for cc in (2 * k, 2 * k + 1):
+            mm(A(bank, 256 * (cc % 2), 256 * (cc % 2) + 256),
+               [(A("MS", 2 - pc + 128 * cc, 130 - pc + 128 * cc), A("KP", 256 * pc, 256 * pc + 256)) for pc in range(3)])
+        cp(A("TK0", 512 * k, 512 * k + 512), A(bank), ENG["kb"][k])
+    flip(A("TF0", 4096, 6144), A("TF0", 0, 2048))
+    flip(A("TF0", 6144, 7168), A("TF0", 0, 1024), "S")
+    flip(A("TF0", 7168, 8192), A("TF0", 1024, 2048), "S")
+    ms(cb("N2k", 0, 64), -2048.0); ms(cb("C3", 0, 64), 393216.0)
+
+    def Wm(k, c0=0, c1=144, st=1):
+        return A("W", 144 * k + c0, 144 * k + c1, st)
+
+    def wrows(k, rows):
+        (r0, w0) = rows[0]
+        sel(Wm(k), A("ZB"), [[-16, 9], [200, 16]], -r0 - 3000, w0)
+        for r, w in rows[1:]:
+            sel(Wm(k, 15, 128, 16), Wm(k, 15, 128, 16), [[-16, 8]], -r, w)
+    wrows(0, [(0, -4096.0), (1, 0.5), (2, 0.5), (4, 0.5), (5, 0.5)])
+    wrows(1, [(0, 8192.0), (1, -1.0), (2, -1.0), (4, 1.0), (5, 1.0)])
+    dg = [[-1, 128]]
+    sel(cf("DnIf"), A("ZF"), dg, 1, 1.0)
+    sel(cf("DnIf", 0, 128, 8), A("ZF", 0, 16), [[-8, 16]], -7, 1.0)
+    sel(cf("DnIf"), cf("DnIf"), dg, 0, -1.0)
+    sel(cf("IUpf"), A("ZF"), dg, -1, -1.0)
+    sel(cf("IUpf", 7, 128, 8), A("ZF", 0, 16), [[-8, 16]], 0, -1.0)
+    sel(cf("IUpf"), cf("IUpf"), dg, 0, 1.0)
+    sel(cf("Upf"), A("ZF"), dg, -1, 1.0)
+    sel(cf("Upf", 7, 128, 8), A("ZF", 0, 16), [[-8, 16]], 0, 1.0)
+    wrows(2, [(0, 1.0)])
+    sel(Wm(2, 15, 128, 16), A("ONE", 0, 8), [[-16, 8]], 0, 0.0, ALU.is_ge)
+    sel(Wm(2, 15, 128, 16), Wm(2, 15, 128, 16), [[16, 8]], 15, 0.0, ALU.is_ge, -1)
+    for n, src in (("B8I", "ONE"), ("nB4", "M4")):
+        sel(cb(n), A(src, 0, 128), [[-8, 16], [0, 8]], 0, 0.0, ALU.is_ge)
+        sel(cb(n), cb(n), [[8, 16], [0, 8]], 7, 0.0, ALU.is_ge, -1)
+    sel(cb("B8I"), cb("B8I"), dg, 0, 9.0)
+    iota(cb("C16M"), [[16, 128]], 2048, 0)
+    iota(cb("C16", 0, 64), [[16, 64]], 0, 0)
+    op("G", [lambda: g.iota(T.COI[:, 0:1], [[0, 1]], 0, 1)], [A("COI", 0, 1)], [], 140.0)
+    act(cb("DnIb"), cf("DnIf")); act(cb("DnI8"), cf("DnIf"), -8192.0); act(cb("IUp8"), cf("IUpf"), -8192.0); act(cb("Up8"), cf("Upf"), -8192.0)
+    ms(cb("C20", 0, 64), 20.0); ms(cb("EI8"), 0.125); ms(col(2), 9.0); ms(cb("CC", p1=32), C23 / 32)
+    ts(A("COI", 4, 5), A("COI", 0, 1), 15, ALU.bitwise_and)
+    cp(col(1), A("COI", 4, 5))
+    ts(cb("QT", 0, 64), A("ONE", 0, 64), col(1), ALU.mult)
+    cp(A("KF"), A("EI", 0, 256))
+    dma(A("TK0", 2048, 4096), X(T.faces[:]), "dc0", 512)
+    dma(A("TF1", 4096, 6144), A("TF0", 4096, 6144), "dn1", 512)
+    dma(A("TK1", 0, 2048), A("TK0", 0, 2048), "dk1", 512)
+    dma(A("TF1", 0, 2048), X(T.faces[:]), "df1", 512)
+
+    def background(t):
+        if t == 0:
+            dma(A("TK1", 4096, 6144), X(T.faces[:]), "dc1", 512)
+        if t == 1:
+            dma(A("TK0", 4096, 6144), X(T.faces[:]), "dc2", 512)
+            dma(X(T.yx[:, 0:2048]), A("TF0", 0, 2048), "dyx", 512)
+            dma(X(T.y0[:, 0:2048]), A("KF", 0, 256, 1, 0, 64), "dy", 64)
+            dma(X(T.y1[:, 0:2048]), A("KF", 0, 256, 1, 64, 128), "dy", 64)
+    p8 = [[-16, 8], [-1, 8]]
+    pz = [[-16, 8], [-1, 8], [300, 2]]
+    for b in range(2):
+        sel(cf("a%d" % b), A("ZF"), pz, -8 * b, 2.0)
+        sel(cf("b%d" % b), A("ZF"), pz, -8 * b - 300, 2.0)
+        sel(cf("c%d" % b), A("ZF"), pz, -8 * b, -2.0)
+        sel(cf("c%d" % b, 1, 128, 2), cf("c%d" % b, 1, 128, 2), p8, -8 * b, 2.0)
+        sel(cf("d%d" % b), A("ZF"), pz, -8 * b + 1, 2.0)
+        sel(cf("d%d" % b, 0, 128, 16), A("ZF", 0, 8), [[-16, 8]], -8 * b - 7, 2.0)
+        sel(cf("d%d" % b, 1, 128, 2), cf("d%d" % b, 1, 128, 2), p8, -8 * b, -2.0)
+        sel(cf("FT", 8 * b, 8 * b + 8), A("ZF", 0, 8), [[-16, 8]], -8 * b, 1.0)
+    for k, rows in ((3, [(3, 0, -8192.0), (4, 0, 2.0), (5, 0, 2.0), (0, 1, -8192.0), (1, 1, 2.0), (2, 1, 2.0)]),
+                    (4, [(3, 0, 1.0), (0, 1, 1.0)])):
+        sel(Wm(k), A("ZB"), [[0, 144]], 1000, 0.0)
+        for r, kid, w in rows:
+            a = Wm(k, 7 + 64 * kid, 64 + 64 * kid, 8)
+            sel(a, a, [[-16, 8]], -r, w)
+
+    def L(n, h, k=0, per=1):
+        return A(n, 64 * (per * h + k), 64 * (per * h + k) + 64)
+
+    def Zb(k, h):
+        return L("Z", h, k, 6)
+
+    def big(n, h, base=0):
+        return A(n, base + 1024 * h, base + 1024 * h + 1024)
+
+    def halves(fn, out, base, win, lst, h, eng):
+        c = base + 1024 * h
+        if eng[2 * h] == eng[2 * h + 1]:
+            fn(A(out, c, c + 1024), IX(win, L(lst, h)), eng[2 * h])
+        else:
+            for k in range(2):
+                fn(A(out, c + 512 * k, c + 512 * k + 512), IX(win, A(lst, 64 * h + 32 * k, 64 * h + 32 * k + 32)), eng[2 * h + k])
+
+    def pE(h, c0, c1):
+        return A("pE%d" % h, c0, c1)
+
+    def visit(t):
+        last = t == RO - 1
+        tf, tfn, tk, tkn, inb = "TF%d" % (t % 2), "TF%d" % ((t + 1) % 2), "TK%d" % (t % 2), "TK%d" % ((t + 1) % 2), "IN%d" % t
+        kv = 0 if t == 0 else 2048
+        Ib = cb("Ib")
+        for h in range(2):
+            K = A3("PH", h, 0)
+            if t > 0:
+                op("X", [], [A3(inb, h, 0, 3)], [], 0.0, "rs%d%d" % (t - 1, h), neng)
+            act(big("FW", h), IX(A(tf, 0, 8192), A3(inb, h, 1)))
+            cp(A3("PH", h, 0, 3), A3(inb, h, 0, 3))
+            ts(L("sK", h), A3(inb, h, 0), 4096.0, ALU.is_ge, 0.5, ALU.subtract)
+            if t == 0:
+                ts(L("TT", h), A3(inb, h, 0), 392192.5, ALU.add)
+                mm(L("pA", h, 6), [(cf("If"), K), (cb("nIb"), L("TT", h)), (Ib, cb("C3", 0, 64))])
+                cp(L("p16", h), L("pA", h, 6))
+            else:
+                mm(L("pA", h), [(cf("If"), K), (cb("n4I"), L("sK", h)), (Ib, cb("N2k", 0, 64))])
+                cp(L("p16", h), L("pA", h))
+            halves(cp, "G", 0, A(tk, 0, kv + 2048), "p16", h, ENG["g"][t])
+            gq = [A("G", 1024 * h + q, 1024 * h + 1024, 16) for q in range(16)]
+            mm(A("pV%d" % h, 0, 64), [(Wm(1, 15 - q, 143 - q), gq[q]) for q in range(16)])
+            tt(L("sd", h), A("pV%d" % h, 0, 64), L("sK", h), ALU.mult)
+            mm(L("pX", h, 4), [(Wm(0, 15 - q, 143 - q), gq[q]) for q in range(16)], stop=False, lock=True)
+            mm(L("pX", h, 4), [(cf("If"), L("sd", h))], start=False, lock=True)
+            cp(L("u16", h), L("pX", h, 4))
+        for h in range(2):
+            ts(Zb(0, h), A3(inb, h, 1), 4096.0, ALU.is_ge, 0.5, ALU.subtract)
+            cp(Zb(1, h), A3("PH", h, 1), "S")
+            tt(Zb(2, h), A3("PH", h, 1), Zb(1, h), ALU.subtract)
+            ts(Zb(3, h), L("u16", h), 4096.0, ALU.is_ge, 0.5, ALU.subtract)
+            cp(Zb(4, h), L("pX", h, 4), ENG["k0h"])
+            tt(Zb(5, h), L("pX", h, 4), Zb(4, h), ALU.subtract)
+            pk = (None, [("pK", 0, 1)])
+            op("P", [lambda cl=cl, h=h: g.tensor.transpose(T.pK[0:48, :, 16 * cl:16 * cl + 16], T.Z[:, 384 * h + cl:384 * h + 384:8], Ib[0])
+                     for cl in range(8)], [pk], [A("Z", 384 * h, 384 * h + 384), Ib], 8 * (10 + 128 * NOM["pe"]))
+            ks = (T["KS%d" % h][0:48, :, :], [("KS%d" % h, 0, 1)], 1024, 2, False)
+            cp(ks, (T.pK[0:48, :, :], pk[1], 1024, 2, False), ENG["kev"][h])
+            c = kv + 2048 + 1024 * h
+            for gg in range(8):
+                dma((T[tk][16 * gg:16 * gg + 6, c:c + 1024], [(tk, c, c + 1024, gg)]), (T["KS%d" % h][0:48, gg, :], ks[1]),
+                    "kc%d%d" % (t, h), 35)
+        background(t)
+        if not last:
+            for h in range(2):
+                mm(pE(h, 256, 320), [(cb("DnIb" if k else "DnI8"), Zb(k, h)) for k in range(3)])
+                mm(pE(h, 320, 384), [(cf("IUpf"), A3("PH", h, 0)), (cb("IUp8"), L("sK", h))])
+                for k in range(2):
+                    tt(L("Q", h, 2 * k), pE(h, 256 + 64 * k, 320 + 64 * k), A3("PH", h, 2), ALU.mult)
+        for h in range(2):
+            K = A3("PH", h, 0)
+            nH = [(cb("nIb"), Zb(1, h)), (cb("nIb"), Zb(2, h))]
+            mm(pE(h, 0, 64), [(Ib, Zb(4, h)), (Ib, Zb(5, h)), (cf("n2If"), L("sd", h)), (cf("nIf"), K)])
+            mm(pE(h, 64, 128), nH + [(Ib, L("CB", 2 * MB.index("C16M") + h)), (Ib, cb("QT", 0, 64))])
+            if last:
+                mm(pE(h, 128, 192), [(cb("n8I"), L("sK", h))])
+                mm(pE(h, 192, 256), [(cb("n8I"), Zb(0, h))])
+            else:
+                mm(pE(h, 128, 192), [(Ib if k else cb("n8I"), Zb(k, h)) for k in range(3)] + [(cf("nIf"), K), (cf("If"), L("Q", h))])
+                mm(pE(h, 192, 256), [(cb("Up8"), L("sK", h)), (cf("Upf"), K)] + nH + [(cf("If"), L("Q", h, 2))])
+        for h in range(2):
+            tt(big("D", h), IX(A(tf, 0, 8192), L("u16", h)), big("FW", h), ALU.subtract)
+            ts(big("NR", h), big("D", h), C28, ALU.add, C28, ALU.is_equal)
+            mm(L("pA", h, 4), [(Wm(2, 15 - q, 143 - q), A("NR", 1024 * h + q, 1024 * h + 1024, 16)) for q in range(16)])
+            for k in range(2):
+                c = 1024 * h + 512 * k
+                mm(A("pV%d" % k), [(A("CH", 0, 128), A("FW", c, c + 512)), (A("CH", 128, 256), A("D", c, c + 512)),
+                                   (cb("CC", p1=32), A("ONE", 0, 512, 1, 0, 32))])
+                act(A(tf, 8192 + c, 8704 + c), A("pV%d" % k), 1.0, 255.0 - C23)
+            ts(L("SP", h), L("pA", h, 4), col(2), ALU.is_ge)
+            for k in range(4):
+                mm(L("pZ", h, k, 4), [(cb("B8I"), L("SP", h))] if k < 2 else [(cb("nB4"), L("SP", h)), (Ib, cb("C20", 0, 64))])
+            mk = A("MK", 256 * h, 256 * h + 256)
+            ts(mk, A("pZ", 256 * h, 256 * h + 256), 11.0, ALU.is_ge)
+            mm(L("pA", h, 2), [(Ib, cb("C16", 0, 64)), (cb("I2k"), L("MK", h, 0, 4))])
+            ts(L("m16", h), L("pA", h, 2), col(1), ALU.add)
+            r = A("R", 192 * h, 192 * h + 128)
+            tt(pE(h, 256, 512), pE(h, 0, 256), mk, ALU.mult)
+            tt(A("R1", 128 * h, 128 * h + 128), pE(h, 256, 384), A3("PH", h, 0, 2), ALU.add)
+            tt(r, pE(h, 384, 512), A("R1", 128 * h, 128 * h + 128), ALU.add)
+            tt(L("R", h, 2, 3), A3("PH", h, 2), L("MK", h, 2, 4), ALU.not_equal)
+            if not last:
+                o = A("OUT%d" % t, 192 * h, 192 * h + 192)
+                cp(o, A("R", 192 * h, 192 * h + 192))
+                op("G", [lambda o=o, h=h: g.remote_dma(T["IN%d" % (t + 1)][:, h, :], o[0], T.sem["rs%d%d" % (t, h)],
+                                                       T.sem["ls%d%d" % (t, h)], pid, rid, rmask)],
+                   [], [o], 1000.0, "ls%d%d" % (t, h), neng, NOM["rlat"])
+            o = big(tfn, h, 2048)
+            halves(flip, tfn, 2048, A(tf, 6144 + 1024 * h, 9216 + 1024 * h), "m16", h, ENG["m"][t])
+            halves(cp, tkn, 2048, A(tk, kv + 1024 * h, kv + 3072 + 1024 * h), "m16", h, ENG["k"][t])
+            if not last:
+                flip(big(tfn, h, 6144), o)
+                continue
+            dma(X(T.yx[:, 2048 + 1024 * h:3072 + 1024 * h]), o, "ox%d" % h, 256)
+            ts(pE(h, 0, 128), r, 4096.0, ALU.is_ge, -4095.5, ALU.mult)
+            tt(A("EH", 128 * h, 128 * h + 128), pE(h, 0, 128), r, ALU.add)
+            for k in range(2):
+                tt(L("FE", h, k, 2), L("EH", h, k, 2), A3("PH", h, 2), ALU.mult)
+            for b in range(2):
+                mm(A("pE%d" % h, 128 + b, 256, 2), [(cf("a%d" % b), L("EH", h, 0, 2)), (cf("b%d" % b), L("EH", h, 1, 2)),
+                                                    (cf("c%d" % b), L("FE", h, 0, 2)), (cf("d%d" % b), L("FE", h, 1, 2))])
+            for b in range(2):
+                mm(A("pE%d" % h, 256 + b, 384, 2, 0, 8), [(cf("FT", 8 * b, 8 * b + 8), L("R", h, 2, 3))])
+            cp(A("YB", 128 * h, 128 * h + 128), pE(h, 128, 256))
+            dma(X(T.yb[:, 128 * h:128 * h + 128]), A("YB", 128 * h, 128 * h + 128), "ob%d" % h, 64)
+            cp(A("YF", 128 * h, 128 * h + 128, 1, 0, 8), A("pE%d" % h, 256, 384, 1, 0, 8))
+            c = 2048 + 1024 * h
+            py = A("pX", 128 * h, 128 * h + 128)
+            mm(py, [(Wm(k, 7 - bl, 135 - bl), A(tkn, c + 128 * bl, c + 128 * bl + 128)) for bl in range(8) for k in (3, 4)], lock=True)
+            act(A("YS", 128 * h, 128 * h + 128), py, 1.0, -4095.5)
+            dma(X(T.y0[:, c:c + 1024]), A("YS", 128 * h, 128 * h + 128, 1, 0, 64), "oy%d" % h, 32)
+            dma(X(T.y1[:, c:c + 1024]), A("YS", 128 * h, 128 * h + 128, 1, 64, 128), "oy%d" % h, 32, "S")
+        if last:
+            dma(X(T.yf[:]), A("YF", 0, 256, 1, 0, 8), "of", 8)
+        else:
+            mm(A("pA", 384, 448), [(cb("EI8"), L("MK", h, 2, 4)) for h in range(2)])
+            act(A("JK"), A("pA", 384, 448), acc=col(3))
+            cp(A("COI", 8, 9), col(3))
+            ts(A("COI", 12, 13), A("COI", 8, 9), 1, ALU.bitwise_and)
+            ts(col(2), A("COI", 12, 13), 9.0, ALU.add)
+
+    for t in range(RO):
+        visit(t)
+    emit(g, T, order(ops))
+
+
+def meets(a, b):
+    return a[1] < b[2] and b[1] < a[2] and (len(a) < 4 or len(b) < 4 or a[3] == b[3])
+
+
+def order(ops):
+    pred = [set() for _ in ops]
+    hist = {}
+    for i, o in enumerate(ops):
+        for kind in ("r", "w"):
+            for r in o[kind]:
+                for (r2, kind2, j) in hist.get(r[0], []):
+                    if meets(r, r2) and "w" in (kind, kind2) and not (o["sem"] and o["sem"] == ops[j]["sem"]):
+                        pred[i].add(j)
+        for kind in ("r", "w"):
+            for r in o[kind]:
+                hist.setdefault(r[0], []).append((r, kind, i))
+    seen = set()
+    assert sorted(ORDER) == list(range(len(ops)))
+    for i in ORDER:
+        assert pred[i] <= seen
+        seen.add(i)
+    return [ops[i] for i in ORDER]
+
+
+def emit(g, T, ops):
+    queue = {"V": g.vector, "S": g.scalar, "P": g.tensor, "G": g, "Y": g.sync}
+    own = {"V": "sV", "S": "sS", "P": "sP", "G": "sG"}
+    total = {}
+    for o in ops:
+        if o["sem"] is not None:
+            total[o["sem"]] = total.get(o["sem"], 0) + o["n"]
+    count = {s: 0 for s in own.values()}
+    known = {e: {} for e in queue}
+    hist = {}
+    for i, o in enumerate(ops):
+        e = o["e"]
+        need = {}
+        for kind in ("r", "w"):
+            for r in o[kind]:
+                psum = SCRATCH[r[0]][0] == "psum"
+                for (r2, kind2, o2) in hist.get(r[0], []):
+                    if o2["e"] == "P" and e == "P":
+                        continue
+                    if o2["sem"] is not None and o2["sem"] == o["sem"]:
+                        continue
+                    if (psum and o2["e"] != e) or (meets(r, r2) and "w" in (kind, kind2)):
+                        s, v = o2["tok"]
+                        if v > need.get(s, (0, None))[0]:
+                            need[s] = (v, o2)
+        if e != "X":
+            for s, (v, o2) in sorted(need.items(), key=lambda x: -x[1][1]["i"]):
+                if known[e].get(s, 0) < v:
+                    queue[e].wait_ge(T.sem[s], v)
+                    known[e][s] = v
+                    for s2, v2 in o2["kn"].items():
+                        known[e][s2] = max(known[e].get(s2, 0), v2)
+            o["kn"] = dict(known[e])
+            for fn in o["fns"]:
+                ins = fn()
+                if o["sem"] is None:
+                    count[own[e]] += 1
+                    ins.then_inc(T.sem[own[e]], 1)
+            if o["sem"] is None:
+                o["tok"] = (own[e], count[own[e]])
+            else:
+                if o["sem"] in DSEM:
+                    ins.then_inc(T.sem[o["sem"]], 16)
+                    if total[o["sem"]] > 16:
+                        o["kn"] = {}
+                o["tok"] = (o["sem"], total[o["sem"]])
+        else:
+            o["kn"] = {}
+            o["tok"] = (o["sem"], o["n"])
+        o["i"] = i
+        for kind in ("r", "w"):
+            for r in o[kind]:
+                hist.setdefault(r[0], []).append((r, kind, o))
+    for s, v in list(count.items()) + list(total.items()):
+        if known["Y"].get(s, 0) < v:
+            g.sync.wait_ge(T.sem[s], v)

@@ -2,6 +2,7 @@ from concourse.mybir import AluOpType as ALU, ActivationFunctionType as ACT
 
 F, B, I, U, H16 = "float32", "bfloat16", "int32", "uint16", "float16"
 RO = 4
+NT = (4, 8)
 MF = ["If", "nIf", "n2If", "Upf", "IUpf", "DnIf", "U16", "E0", "E1", "O0", "O1",
       "a0", "a1", "b0", "b1", "c0", "c1", "d0", "d1", "FT"]
 MB = ["Ib", "nIb", "n4I", "I2k", "n8I", "DnIb", "IUp8", "Up8", "B8I", "nB4", "EI8", "CC", "GX", "GX0", "GX1",
@@ -13,10 +14,10 @@ SCRATCH = {
     "IN0": ("sbuf", [128, 2, 192], U), "IN1": ("sbuf", [128, 2, 192], U), "IN2": ("sbuf", [128, 2, 192], U), "IN3": ("sbuf", [128, 2, 192], U),
     "OUT0": ("sbuf", [128, 384], U), "OUT1": ("sbuf", [128, 384], U), "OUT2": ("sbuf", [128, 384], U),
     "PH": ("sbuf", [128, 2, 192], F), "R": ("sbuf", [128, 384], F), "R1": ("sbuf", [128, 256], F), "Q": ("sbuf", [128, 256], F),
-    "sK": ("sbuf", [128, 128], B), "Z": ("sbuf", [128, 768], B), "SP": ("sbuf", [128, 128], B), "MK": ("sbuf", [128, 512], B),
+    "Z": ("sbuf", [128, 896], B), "SP": ("sbuf", [128, 128], B), "MK": ("sbuf", [128, 512], B),
     "p16": ("sbuf", [128, 128], U), "u16": ("sbuf", [128, 128], U), "m16": ("sbuf", [128, 128], U),
     "sd": ("sbuf", [128, 128], F), "TT": ("sbuf", [128, 128], B),
-    "KS0": ("sbuf", [128, 8, 128], B), "KS1": ("sbuf", [128, 8, 128], B),
+    "KS0": ("sbuf", [128, 8, 64], B), "KS1": ("sbuf", [128, 8, 128], B),
     "EI": ("sbuf", [128, 512], I), "SI": ("sbuf", [128, 512], I), "FI": ("sbuf", [128, 256], I),
     "P0": ("sbuf", [128, 256], F), "S0": ("sbuf", [128, 256], F), "KP": ("sbuf", [128, 768], B), "FF": ("sbuf", [128, 256], B),
     "FB": ("sbuf", [128, 256], F), "RR": ("sbuf", [128, 256], F), "KF": ("sbuf", [128, 256], F),
@@ -38,8 +39,8 @@ SEMAPHORES = ["sV", "sS", "sP", "sG"] + DSEM + ["ls%d%d" % (t, h) for t in range
 C23 = 12582912.0
 C28 = 402653184.0
 NOM = {"cy": 1.04, "pe": 0.52, "ga": 1.56, "fix": 60.0, "wake": 60.0, "dlat": 1900.0, "rlat": 4000.0, "kb": 4.5}
-ENG = {"g": ["VSSS"] * 4, "m": ["SSSV"] * 4, "k": ["SSSS"] * 4, "kev": "VV", "k0h": "S", "kb": "SVSV"}
-SEQ = "00090a07010b08020q0m03060l040o2f0g0p0h2g0r0k2i0f350u2j140s2k0w0i15161i2h05301g1j1c2x2z2l2y1k0x2m0y1n2v311l0v2w0t113q1m223g201s3a3f1v3i1x21123e1u133j1o0n3r0z3l1w170j3t363b0c24251y181p192a1z1a1q2b1b2c321r2d1d2637442e1e1t271f28291h3c2n454i3k474k41484u4j5a46495r434a4b5v424l3u3d0d3v4c3y4m2o104n2p4t4e4v2q4d5x382r5t0e4f5q4g612u664x2s4o5p4h2t4q3z3w3x6769403s4w3m4y5s686a994p3n34595b3h4r6d4z4s3o5d6u6b3p656c60506f6e6g6h6v566z5752515c545e6i585y7055536o6j5z6k6w6l6r6m6n5f6p716q5u5g6375626s235k735w745n3372645o765j5m6x5l795h5i7c9a7a777b6y787d7j6t7e7f7g7k7h7i7o7q7r8d7s7l9e8e7t8f7v7u9d9m7p9g7w9f7m7n7y7x8183848t7z8u85808h9i8g869o8i879t9n8j9l82888k9u8r8a8s8m8p898n8v8b8q9w8l8c8o8xah9v9x9ya09kaia39zak8w8y39a4ala19ca29qa59h9ba6a88za7a9af9paaabajac90ad9sao95ar9j93aeas91aqap969rat9792am98aw94axazauayanavb0b6agb1b2b3b4b5bbbdbec0bfc1cxbgbhbibcczbjc2blbkbobrbqbmcgcwbnbscyc4c3chd7btc5budcd6c6d5d4b7bvbpddb8deb9babwc7bxciccdjc8bycedhbzcbcke0cacdc9cfdfdid0dgdmdldke1e5cjd2dncle6e2dodrdpdud1dqdadsdxdtcmdve7dwd3eacnebdbe8e9cvd9ecdyctd8cseicoe3cqefcucpegcrehedepejeee4ekdzelemeneoeuexewghfjeygiezf0f1eqf4fkerevesetflf2f7f9fafzfbf3f5fcggfnglgmfdf6fmfogngffpg0fef8gofgfqgpfffsg1fwfrfhgufugqfifvg3hofyftfxgsgrgvgtgxgwgyg4hrgzg2hpg5hsh2h0gjh1h3h7hth4h5g6hqh9g8gchagdgkgehvhuhcgahwhzg9hbhxhygbhki0h6g7i3i4i5hfibi1hdici2hlh8i6i7hgiehei8ihi9iihmidiahjifhhighiimijhniliqikinioip"
+ENG = {"g": ["VSSS"] * 4, "m": ["SSSV"] * 4, "k": ["SSVS"] * 4, "av": ["SSSS"] * 4, "ng": "VSSV", "kev": "VV", "k0h": "V", "kb": "SVSV"}
+SEQ = "00090b0a080102060c0q072j0r03040o0j0d0f2k0l0u2l0p0s0y1n360g311i0x0v0h1j0w0i0t1o050k1k140n1l1g150m1m162b111t12261w13222c1c27253c17282g1s18232d1v192h212i1a1b2e1x331q1d2f2y421e29413f431z2a1u2w1f2r441y1h2m1p4f204q451r2n2o464h47485k2p3e4i2q2s4j544930372v382z4g4k394r2x4b3a3v5m4a3n553o105o4c0e5j2t4d3d5n5s5z324n2u3g4l4s4e3q5u3k4t4m604o4u3l3w0z61354p3z4v563h62664z6n3s5140696350683x67643i4y3y533r5r57655p523j5q6a6q6b3m4x5l3p6o4w6c6r583t5i6d3u6h246k5t345w6e6p6f6g5v6i6u6j596l6w6v6x6y5y6m5e5b5x5d6z5g6s5f725c5h735a70756t7d8y7476717778797e7c7f7g7b7a8z7h7j7k867l877m927n7o939b7i957p943b907r7q917u7w7x7s7y8k889d7z7t808l9c899i8a96979a7v819j83828b9k988h998f849p858e9s9l8ma68d8c9r9m9t9q9n8g8j9u9f8i9o8n9v8o9w9xa3a09h9ya79g9za8a18pa2aba4ad8ta58uaf8qagah8xae9e8rai8wa98valac8saoamajaaanawapakaqarasaxatauayazb0b2b3bpavb4cib5bqb7b6cqchb1cjb8ckbab9bdbfbgbbc3bhbrcrbibcbjbscmcxcpbtcsbebkbuc4bvbmblcobycyc1bnd0boc2c5dlc0czd1bxbwd2bzd4dmd7d3d6d8d5cwd9c6dacldbdcdndidddfc7dedgcndhdsc8ducudjdwdtcvcccbdvctdxcfcadoe0cdcee1c9e3cgdqdpe2e4dke5dydrebdze6e7e8e9ecefehedeif4eaeeejfzfyekelemegf5epeseneueveweofieqexfxfjf6g3eyerg1f7g2g4fwf8etf1f9g5fbezfeg6f0fffcf2gbfhf3gdgcfkg9h6fgfagegag7fdflgfg8hbggh7ghhcfmgjgigkh8fngoh9glfuhdfrgqfvgmfpgrhfhefshhgthgfqg0hifthafogshjh1hlgnhohmgwhkguhnh2huhqi0i1gxhpgvgphvhwhxhshrhyhthzh0h3i2i5i4h4gyi3i6iagzi7h5i8i9"
 ORDER = [int(SEQ[k:k + 2], 36) for k in range(0, len(SEQ), 2)]
 
 
@@ -108,7 +109,7 @@ def rank_program(g, core, T, topo):
 
     def act(o, i, scale=1.0, bias=0.0, acc=None):
         if acc is not None:
-            op("S", [lambda: g.scalar.activation(o[0], i[0], ACT.Identity, accum_out=acc[0])], [o, acc], [i], vc(o, i, 1, False))
+            op("S", [lambda: g.scalar.activation(o[0], i[0], ACT.Identity, bias=bias, accum_out=acc[0])], [o, acc], [i], vc(o, i, 1, False))
         elif bias == 0.0:
             op("S", [lambda: g.scalar.activation(o[0], i[0], ACT.Copy, scale=scale)], [o], [i], vc(o, i, 1, False))
         else:
@@ -144,28 +145,28 @@ def rank_program(g, core, T, topo):
     def sel(o, i, pat, base, fill, cmp=ALU.not_equal, cm=1):
         op("G", [lambda: g.affine_select(o[0], i[0], pat, cmp, fill, base, cm)], [o], [i], 170 + 2 * NOM["cy"] * o[2])
 
-    dma(A("EI", 256, 512), X(T.belts[:]), "db", 128)
-    dma(A("FI", 0, 256, 1, 0, 8), X(T.flip[:]), "df", 8, "S")
     dma(A("EI", 0, 256, 1, 0, 64), X(T.kid0[:]), "dk", 64, "S")
     dma(A("EI", 0, 256, 1, 64, 128), X(T.kid1[:]), "dk", 64)
+    dma(A("EI", 256, 512), X(T.belts[:]), "db", 128)
+    dma(A("FI", 0, 256, 1, 0, 8), X(T.flip[:]), "df", 8, "S")
     dma(A("TF0", 0, 2048), X(T.faces[:]), "dp", 512)
     dma(A("TF0", 2048, 4096), X(T.faces[:]), "dv", 512)
     iota(A("IO2"), [[-1, 128]], 0, 1)
-    iota(A("IO3"), [[-16, 8], [300, 2], [-2, 8]], 0, 1)
+    ms(A("KP", 0, 256, 1, 0, 64), 0.0)
     iota(A("IO4"), [[-1, 8], [300, 2], [0, 8]], 0, 1)
     iota(A("IO"), [[-1, 8], [-8, 8]], 0, 1)
     ms(A("MS"), 0.0); ms(A("ZF"), 0.0); ms(A("ZB"), 0.0); ms(A("ONE"), 1.0); ms(A("M4"), -4.0)
     ts(cf("If"), A("IO2"), 0.0, ALU.is_equal)
-    ts(cf("U16"), A("IO2"), 1.0, ALU.is_equal)
-    ts(cf("U16", 15, 128, 16), A("IO2", 15, 128, 16), -15.0, ALU.is_equal)
-    tt(cf("U16"), cf("U16"), cf("If"), ALU.subtract)
+    sel(cf("U16"), A("ZF"), [[-1, 128]], -1, 1.0)
+    sel(cf("U16", 15, 128, 16), A("ZF", 0, 8), [[-16, 8]], 0, 1.0)
+    sel(cf("U16"), cf("U16"), [[-1, 128]], 0, -1.0)
     for b in range(2):
-        ts(cf("E%d" % b), A("IO3"), 300.0 * b, ALU.is_equal, 0.5, ALU.mult)
-        ts(cf("O%d" % b), A("IO3"), 300.0 * b + 1, ALU.is_equal, 0.5, ALU.mult)
+        sel(cf("E%d" % b), A("ZF"), [[-16, 8], [300, 2], [-2, 8]], -300 * b, 0.5)
+        sel(cf("O%d" % b), A("ZF"), [[-16, 8], [300, 2], [-2, 8]], -300 * b - 1, 0.5)
         ts(cb("GX%d" % b, p1=8), A("IO4", 0, 128, 1, 0, 8), 300.0 * b, ALU.is_equal)
     tt(cb("GX", p1=8), cb("GX0", p1=8), cb("GX1", p1=8), ALU.add)
     ts(A("MS", 2, 1026, 16, 64, 128), A("IO", 0, 64, 1, 64, 128), 64.0, ALU.is_equal, 0.5, ALU.mult)
-    ts(A("MS", 5, 1029, 16, 0, 64), A("IO", 0, 64, 1, 0, 64), 0.0, ALU.is_equal, 0.5, ALU.mult)
+    ts(A("MS", 4, 1028, 16, 0, 64), A("IO", 0, 64, 1, 0, 64), 0.0, ALU.is_equal, 0.5, ALU.mult)
     for n, s in (("Ib", 1.0), ("n4I", -4096.0), ("nIb", -1.0), ("I2k", 2048.0), ("n8I", -8192.0)):
         act(cb(n), cf("If"), s)
     act(cf("nIf"), cf("If"), -1.0); act(cf("n2If"), cf("If"), -2.0)
@@ -193,16 +194,17 @@ def rank_program(g, core, T, topo):
     tt(A("pV1", 0, 256), A("pX", 256, 512), A("EI", 0, 256), ALU.add)
     cp(A("KP", 256, 512), A("pV1", 0, 256))
     tt(A("KP", 512, 768), A("pV1", 0, 256), A("KP", 256, 512), ALU.subtract)
-    ts(A("KP", 0, 256), A("SI", 0, 256), 2.0, ALU.mult, -1.0, ALU.add)
+    ms(cb("C3", 0, 64), 393216.0)
+    ts(A("KP", 0, 256, 1, 64, 128), A("SI", 0, 256, 1, 64, 128), 2.0, ALU.mult, -1.0, ALU.add)
     for k, bank in enumerate(["pE0", "pE1", "pV0", "pV1"]):
         for cc in (2 * k, 2 * k + 1):
             mm(A(bank, 256 * (cc % 2), 256 * (cc % 2) + 256),
                [(A("MS", 2 - pc + 128 * cc, 130 - pc + 128 * cc), A("KP", 256 * pc, 256 * pc + 256)) for pc in range(3)])
         cp(A("TK0", 512 * k, 512 * k + 512), A(bank), ENG["kb"][k])
-    flip(A("TF0", 4096, 6144), A("TF0", 0, 2048))
-    flip(A("TF0", 6144, 7168), A("TF0", 0, 1024), "S")
-    flip(A("TF0", 7168, 8192), A("TF0", 1024, 2048), "S")
-    ms(cb("N2k", 0, 64), -2048.0); ms(cb("C3", 0, 64), 393216.0)
+    flip(A("TF0", 4096, 5120), A("TF0", 0, 1024), ENG["ng"][0])
+    flip(A("TF0", 6144, 7168), A("TF0", 0, 1024), ENG["ng"][1])
+    flip(A("TF0", 7168, 8192), A("TF0", 1024, 2048), ENG["ng"][2])
+    ms(cb("N2k", 0, 64), -2048.0); flip(A("TF0", 5120, 6144), A("TF0", 1024, 2048), ENG["ng"][3])
 
     def Wm(k, c0=0, c1=144, st=1):
         return A("W", 144 * k + c0, 144 * k + c1, st)
@@ -212,8 +214,8 @@ def rank_program(g, core, T, topo):
         sel(Wm(k), A("ZB"), [[-16, 9], [200, 16]], -r0 - 3000, w0)
         for r, w in rows[1:]:
             sel(Wm(k, 15, 128, 16), Wm(k, 15, 128, 16), [[-16, 8]], -r, w)
-    wrows(0, [(0, -4096.0), (1, 0.5), (2, 0.5), (4, 0.5), (5, 0.5)])
-    wrows(1, [(0, 8192.0), (1, -1.0), (2, -1.0), (4, 1.0), (5, 1.0)])
+    wrows(0, [(0, -4096.0), (1, 0.5), (2, 0.5), (3, 0.5), (4, 0.5)])
+    wrows(1, [(0, 8192.0), (1, -1.0), (2, -1.0), (3, 1.0), (4, 1.0)])
     dg = [[-1, 128]]
     sel(cf("DnIf"), A("ZF"), dg, 1, 1.0)
     sel(cf("DnIf", 0, 128, 8), A("ZF", 0, 16), [[-8, 16]], -7, 1.0)
@@ -234,7 +236,7 @@ def rank_program(g, core, T, topo):
     iota(cb("C16", 0, 64), [[16, 64]], 0, 0)
     op("G", [lambda: g.iota(T.COI[:, 0:1], [[0, 1]], 0, 1)], [A("COI", 0, 1)], [], 140.0)
     act(cb("DnIb"), cf("DnIf")); act(cb("DnI8"), cf("DnIf"), -8192.0); act(cb("IUp8"), cf("IUpf"), -8192.0); act(cb("Up8"), cf("Upf"), -8192.0)
-    ms(cb("C20", 0, 64), 20.0); ms(cb("EI8"), 0.125); ms(col(2), 9.0); ms(cb("CC", p1=32), C23 / 32)
+    ms(cb("C20", 0, 64), 20.0); ms(cb("EI8"), 0.125); ms(col(2), 10.0); ms(col(3), 1.0); ms(cb("CC", p1=32), C23 / 32)
     ts(A("COI", 4, 5), A("COI", 0, 1), 15, ALU.bitwise_and)
     cp(col(1), A("COI", 4, 5))
     ts(cb("QT", 0, 64), A("ONE", 0, 64), col(1), ALU.mult)
@@ -263,18 +265,19 @@ def rank_program(g, core, T, topo):
         sel(cf("d%d" % b, 0, 128, 16), A("ZF", 0, 8), [[-16, 8]], -8 * b - 7, 2.0)
         sel(cf("d%d" % b, 1, 128, 2), cf("d%d" % b, 1, 128, 2), p8, -8 * b, -2.0)
         sel(cf("FT", 8 * b, 8 * b + 8), A("ZF", 0, 8), [[-16, 8]], -8 * b, 1.0)
-    for k, rows in ((3, [(3, 0, -8192.0), (4, 0, 2.0), (5, 0, 2.0), (0, 1, -8192.0), (1, 1, 2.0), (2, 1, 2.0)]),
-                    (4, [(3, 0, 1.0), (0, 1, 1.0)])):
+    for k, rows in ((3, [(3, 0, 2.0), (4, 0, 2.0), (1, 1, 2.0), (2, 1, 2.0)]),):
         sel(Wm(k), A("ZB"), [[0, 144]], 1000, 0.0)
         for r, kid, w in rows:
             a = Wm(k, 7 + 64 * kid, 64 + 64 * kid, 8)
             sel(a, a, [[-16, 8]], -r, w)
 
     def L(n, h, k=0, per=1):
+        if n == "sK":
+            n, per = "Z", 7
         return A(n, 64 * (per * h + k), 64 * (per * h + k) + 64)
 
     def Zb(k, h):
-        return L("Z", h, k, 6)
+        return L("Z", h, k + 1, 7)
 
     def big(n, h, base=0):
         return A(n, base + 1024 * h, base + 1024 * h + 1024)
@@ -285,7 +288,7 @@ def rank_program(g, core, T, topo):
             fn(A(out, c, c + 1024), IX(win, L(lst, h)), eng[2 * h])
         else:
             for k in range(2):
-                fn(A(out, c + 512 * k, c + 512 * k + 512), IX(win, A(lst, 64 * h + 32 * k, 64 * h + 32 * k + 32)), eng[2 * h + k])
+                fn(A(out, c + 512 * k, c + 512 * k + 512), IX(win, A(lst, 64 * h + 32 * k, 64 * h + 32 * k + 32)), eng[2 * h + k].upper())
 
     def pE(h, c0, c1):
         return A("pE%d" % h, c0, c1)
@@ -301,7 +304,7 @@ def rank_program(g, core, T, topo):
                 op("X", [], [A3(inb, h, 0, 3)], [], 0.0, "rs%d%d" % (t - 1, h), neng)
             act(big("FW", h), IX(A(tf, 0, 8192), A3(inb, h, 1)))
             cp(A3("PH", h, 0, 3), A3(inb, h, 0, 3))
-            ts(L("sK", h), A3(inb, h, 0), 4096.0, ALU.is_ge, 0.5, ALU.subtract)
+            ts(A("Z", 448 * h, 448 * h + 128), A3(inb, h, 0, 2), 4096.0, ALU.is_ge, 0.5, ALU.subtract)
             if t == 0:
                 ts(L("TT", h), A3(inb, h, 0), 392192.5, ALU.add)
                 mm(L("pA", h, 6), [(cf("If"), K), (cb("nIb"), L("TT", h)), (Ib, cb("C3", 0, 64))])
@@ -317,21 +320,20 @@ def rank_program(g, core, T, topo):
             mm(L("pX", h, 4), [(cf("If"), L("sd", h))], start=False, lock=True)
             cp(L("u16", h), L("pX", h, 4))
         for h in range(2):
-            ts(Zb(0, h), A3(inb, h, 1), 4096.0, ALU.is_ge, 0.5, ALU.subtract)
             cp(Zb(1, h), A3("PH", h, 1), "S")
             tt(Zb(2, h), A3("PH", h, 1), Zb(1, h), ALU.subtract)
-            ts(Zb(3, h), L("u16", h), 4096.0, ALU.is_ge, 0.5, ALU.subtract)
-            cp(Zb(4, h), L("pX", h, 4), ENG["k0h"])
-            tt(Zb(5, h), L("pX", h, 4), Zb(4, h), ALU.subtract)
+            cp(Zb(3, h), L("pX", h, 4), ENG["k0h"])
+            tt(Zb(4, h), L("pX", h, 4), Zb(3, h), ALU.subtract)
             pk = (None, [("pK", 0, 1)])
-            op("P", [lambda cl=cl, h=h: g.tensor.transpose(T.pK[0:48, :, 16 * cl:16 * cl + 16], T.Z[:, 384 * h + cl:384 * h + 384:8], Ib[0])
-                     for cl in range(8)], [pk], [A("Z", 384 * h, 384 * h + 384), Ib], 8 * (10 + 128 * NOM["pe"]))
-            ks = (T["KS%d" % h][0:48, :, :], [("KS%d" % h, 0, 1)], 1024, 2, False)
-            cp(ks, (T.pK[0:48, :, :], pk[1], 1024, 2, False), ENG["kev"][h])
+            op("P", [lambda cl=cl, h=h: g.tensor.transpose(T.pK[0:320 // NT[h], :, 16 * cl:16 * cl + 16],
+                                                           T.Z[:, 448 * h + 64 + cl:448 * h + 384:NT[h]], Ib[0])
+                     for cl in range(NT[h])], [pk], [A("Z", 448 * h + 64, 448 * h + 384), Ib], NT[h] * (10 + 128 * NOM["pe"]))
+            ks = (T["KS%d" % h][0:320 // NT[h], :, :], [("KS%d" % h, 0, 1)], 128 * NT[h], 2, False)
+            cp(ks, (T.pK[0:320 // NT[h], :, 0:16 * NT[h]], pk[1], 128 * NT[h], 2, False), ENG["kev"][h])
             c = kv + 2048 + 1024 * h
             for gg in range(8):
-                dma((T[tk][16 * gg:16 * gg + 6, c:c + 1024], [(tk, c, c + 1024, gg)]), (T["KS%d" % h][0:48, gg, :], ks[1]),
-                    "kc%d%d" % (t, h), 35)
+                dma((T[tk][16 * gg:16 * gg + 5, c:c + 1024], [(tk, c, c + 1024, gg)]), (T["KS%d" % h][0:320 // NT[h], gg, :], ks[1]),
+                    "kc%d%d" % (t, h), 320 // NT[h])
         background(t)
         if not last:
             for h in range(2):
@@ -342,7 +344,7 @@ def rank_program(g, core, T, topo):
         for h in range(2):
             K = A3("PH", h, 0)
             nH = [(cb("nIb"), Zb(1, h)), (cb("nIb"), Zb(2, h))]
-            mm(pE(h, 0, 64), [(Ib, Zb(4, h)), (Ib, Zb(5, h)), (cf("n2If"), L("sd", h)), (cf("nIf"), K)])
+            mm(pE(h, 0, 64), [(Ib, Zb(3, h)), (Ib, Zb(4, h)), (cf("n2If"), L("sd", h)), (cf("nIf"), K)])
             mm(pE(h, 64, 128), nH + [(Ib, L("CB", 2 * MB.index("C16M") + h)), (Ib, cb("QT", 0, 64))])
             if last:
                 mm(pE(h, 128, 192), [(cb("n8I"), L("sK", h))])
@@ -356,10 +358,14 @@ def rank_program(g, core, T, topo):
             mm(L("pA", h, 4), [(Wm(2, 15 - q, 143 - q), A("NR", 1024 * h + q, 1024 * h + 1024, 16)) for q in range(16)])
             for k in range(2):
                 c = 1024 * h + 512 * k
-                mm(A("pV%d" % k), [(A("CH", 0, 128), A("FW", c, c + 512)), (A("CH", 128, 256), A("D", c, c + 512)),
-                                   (cb("CC", p1=32), A("ONE", 0, 512, 1, 0, 32))])
-                act(A(tf, 8192 + c, 8704 + c), A("pV%d" % k), 1.0, 255.0 - C23)
-            ts(L("SP", h), L("pA", h, 4), col(2), ALU.is_ge)
+                half = [(A("CH", 0, 128), A("FW", c, c + 512)), (A("CH", 128, 256), A("D", c, c + 512))]
+                if ENG["av"][t][2 * h + k] == "S":
+                    mm(A("pV%d" % k), half + [(cb("CC", p1=32), A("ONE", 0, 512, 1, 0, 32))])
+                    act(A(tf, 8192 + c, 8704 + c), A("pV%d" % k), 1.0, 255.0 - C23)
+                else:
+                    mm(A("pV%d" % k), half)
+                    ts(A(tf, 8192 + c, 8704 + c), A("pV%d" % k), C23, ALU.add, C23 - 255.0, ALU.subtract)
+            ts(L("SP", h), L("pA", h, 4), col(3), ALU.add, col(2), ALU.is_ge)
             for k in range(4):
                 mm(L("pZ", h, k, 4), [(cb("B8I"), L("SP", h))] if k < 2 else [(cb("nB4"), L("SP", h)), (Ib, cb("C20", 0, 64))])
             mk = A("MK", 256 * h, 256 * h + 256)
@@ -398,18 +404,18 @@ def rank_program(g, core, T, topo):
             cp(A("YF", 128 * h, 128 * h + 128, 1, 0, 8), A("pE%d" % h, 256, 384, 1, 0, 8))
             c = 2048 + 1024 * h
             py = A("pX", 128 * h, 128 * h + 128)
-            mm(py, [(Wm(k, 7 - bl, 135 - bl), A(tkn, c + 128 * bl, c + 128 * bl + 128)) for bl in range(8) for k in (3, 4)], lock=True)
-            act(A("YS", 128 * h, 128 * h + 128), py, 1.0, -4095.5)
+            mm(py, [(Wm(3, 7 - bl, 135 - bl), A(tkn, c + 128 * bl, c + 128 * bl + 128)) for bl in range(8)], lock=True)
+            ts(A("S0", 128 * h, 128 * h + 128), py, 8192.0, ALU.is_ge, -8191.0, ALU.mult)
+            tt(A("YS", 128 * h, 128 * h + 128), py, A("S0", 128 * h, 128 * h + 128), ALU.add)
             dma(X(T.y0[:, c:c + 1024]), A("YS", 128 * h, 128 * h + 128, 1, 0, 64), "oy%d" % h, 32)
             dma(X(T.y1[:, c:c + 1024]), A("YS", 128 * h, 128 * h + 128, 1, 64, 128), "oy%d" % h, 32, "S")
         if last:
             dma(X(T.yf[:]), A("YF", 0, 256, 1, 0, 8), "of", 8)
         else:
             mm(A("pA", 384, 448), [(cb("EI8"), L("MK", h, 2, 4)) for h in range(2)])
-            act(A("JK"), A("pA", 384, 448), acc=col(3))
-            cp(A("COI", 8, 9), col(3))
-            ts(A("COI", 12, 13), A("COI", 8, 9), 1, ALU.bitwise_and)
-            ts(col(2), A("COI", 12, 13), 9.0, ALU.add)
+            act(A("JK"), A("pA", 384, 448), bias=1.0 / 64, acc=col(3))
+            act(col(4), col(3), 0.49995, C23)
+            act(col(2), col(4), 2.0, 10.0 - 2 * C23)
 
     for t in range(RO):
         visit(t)

@@ -2,46 +2,68 @@ from concourse.mybir import AluOpType as ALU, ActivationFunctionType as ACT
 
 F, B, I, U, H16 = "float32", "bfloat16", "int32", "uint16", "float16"
 RO = 4
-NT = (4, 8)
-MF = ["If", "nIf", "n2If", "Upf", "IUpf", "DnIf", "U16", "E0", "E1", "O0", "O1",
-      "a0", "a1", "b0", "b1", "c0", "c1", "d0", "d1", "FT"]
-MB = ["Ib", "nIb", "n4I", "I2k", "n8I", "DnIb", "IUp8", "Up8", "B8I", "nB4", "EI8", "CC", "GX", "GX0", "GX1",
-      "C16M", "C16", "QT", "N2k", "C20", "C3", "DnI8"]
+PK = "pZ"
+NT = 4
+MF = ["If", "U16", "E0", "E1", "O0", "O1", "a0", "a1", "b0", "b1", "c0", "c1", "d0", "d1", "FT"]
+MB = ["Ib", "nIb", "I2", "nhI", "Kp", "Kn", "Dn", "IDn", "UpI", "B8I", "nB4", "EI8", "CC",
+      "GX0", "GX1", "GXp", "GXn", "C16", "C20", "C3"]
 SCRATCH = {
-    "TF0": ("sbuf", [128, 10240], B), "TF1": ("sbuf", [128, 10240], B),
-    "TK0": ("sbuf", [128, 6144], B), "TK1": ("sbuf", [128, 6144], B),
+    "TF0": ("sbuf", [128, 10240], B), "TF1": ("sbuf", [128, 10240], B), "TK": ("sbuf", [128, 10240], B),
     "G": ("sbuf", [128, 2048], B), "FW": ("sbuf", [128, 2048], B), "D": ("sbuf", [128, 2048], B), "NR": ("sbuf", [128, 2048], B),
-    "IN0": ("sbuf", [128, 2, 192], U), "IN1": ("sbuf", [128, 2, 192], U), "IN2": ("sbuf", [128, 2, 192], U), "IN3": ("sbuf", [128, 2, 192], U),
-    "OUT0": ("sbuf", [128, 384], U), "OUT1": ("sbuf", [128, 384], U), "OUT2": ("sbuf", [128, 384], U),
-    "PH": ("sbuf", [128, 2, 192], F), "R": ("sbuf", [128, 384], F), "R1": ("sbuf", [128, 256], F), "Q": ("sbuf", [128, 256], F),
-    "Z": ("sbuf", [128, 896], B), "SP": ("sbuf", [128, 128], B), "MK": ("sbuf", [128, 512], B),
-    "p16": ("sbuf", [128, 128], U), "u16": ("sbuf", [128, 128], U), "m16": ("sbuf", [128, 128], U),
-    "sd": ("sbuf", [128, 128], F), "TT": ("sbuf", [128, 128], B),
-    "KS0": ("sbuf", [128, 8, 64], B), "KS1": ("sbuf", [128, 8, 128], B),
+    "IN0": ("sbuf", [128, 384], F), "IN1": ("sbuf", [128, 384], F), "IN2": ("sbuf", [128, 384], F), "IN3": ("sbuf", [128, 384], F),
+    "R0": ("sbuf", [128, 384], F), "R1": ("sbuf", [128, 384], F), "R2": ("sbuf", [128, 384], F), "R3": ("sbuf", [128, 384], F),
+    "TR": ("sbuf", [128, 384], B), "UF": ("sbuf", [128, 128], F), "X16": ("sbuf", [128, 256], U), "TN": ("sbuf", [128, 384], B), "PC": ("sbuf", [128, 256], H16),
+    "Z": ("sbuf", [128, 2, 256], B), "SP": ("sbuf", [128, 128], B), "MK": ("sbuf", [128, 256], B),
+    "p16": ("sbuf", [128, 128], U), "u16": ("sbuf", [128, 128], U), "m16": ("sbuf", [128, 128], U), "TT": ("sbuf", [128, 128], B),
+    "KS0": ("sbuf", [128, 8, 16 * NT], B), "KS1": ("sbuf", [128, 8, 16 * NT], B),
     "EI": ("sbuf", [128, 512], I), "SI": ("sbuf", [128, 512], I), "FI": ("sbuf", [128, 256], I),
-    "P0": ("sbuf", [128, 256], F), "S0": ("sbuf", [128, 256], F), "KP": ("sbuf", [128, 768], B), "FF": ("sbuf", [128, 256], B),
-    "FB": ("sbuf", [128, 256], F), "RR": ("sbuf", [128, 256], F), "KF": ("sbuf", [128, 256], F),
-    "IO": ("sbuf", [128, 64], F), "IO2": ("sbuf", [128, 128], F), "IO3": ("sbuf", [128, 128], F), "IO4": ("sbuf", [128, 128], F),
-    "MS": ("sbuf", [128, 1040], B), "CF": ("sbuf", [128, 128 * len(MF)], F), "CB": ("sbuf", [128, 128 * len(MB)], B),
-    "CH": ("sbuf", [128, 256], H16),
-    "W": ("sbuf", [128, 5 * 144], B), "ZF": ("sbuf", [128, 128], F), "ZB": ("sbuf", [128, 144], B),
-    "ONE": ("sbuf", [128, 512], B), "M4": ("sbuf", [128, 128], B),
-    "COL": ("sbuf", [128, 32], F), "COI": ("sbuf", [128, 16], I), "JK": ("sbuf", [128, 64], F),
+    "P0": ("sbuf", [128, 256], F), "KP": ("sbuf", [128, 512], B), "FF": ("sbuf", [128, 512], B),
+    "RR": ("sbuf", [128, 256], F), "KF": ("sbuf", [128, 256], F), "IO2": ("sbuf", [128, 128], F),
+    "CF": ("sbuf", [128, 128 * len(MF)], F), "CB": ("sbuf", [128, 128 * len(MB)], B), "CH": ("sbuf", [128, 256], H16),
+    "CM": ("sbuf", [128, 128], H16), "CT": ("sbuf", [128, 256], B), "W": ("sbuf", [128, 4 * 144], B),
+    "ZF": ("sbuf", [128, 128], F), "ZB": ("sbuf", [128, 144], B), "ONE": ("sbuf", [128, 512], B),
+    "COL": ("sbuf", [128, 40], F), "COI": ("sbuf", [128, 16], I), "JK": ("sbuf", [128, 64], F),
     "EH": ("sbuf", [128, 256], F), "FE": ("sbuf", [128, 256], F), "YB": ("sbuf", [128, 256], F), "YF": ("sbuf", [128, 256], F),
-    "YS": ("sbuf", [128, 256], F),
-    "pA": ("psum", [128, 512], F), "pX": ("psum", [128, 512], F), "pE0": ("psum", [128, 512], F), "pE1": ("psum", [128, 512], F),
-    "pZ": ("psum", [128, 512], F), "pV0": ("psum", [128, 512], F), "pV1": ("psum", [128, 512], F), "pK": ("psum", [128, 8, 128], B),
+    "YT": ("sbuf", [128, 256], F), "YK": ("sbuf", [128, 256], F), "YS": ("sbuf", [128, 8, 64], F),
+    "pA": ("psum", [128, 512], F), "pZ": ("psum", [128, 512], F), "pL0": ("psum", [128, 512], F), "pL1": ("psum", [128, 512], F),
+    "pV0": ("psum", [128, 512], F), "pV1": ("psum", [128, 512], F), "pK": ("psum", [128, 8, 128], B), "pY": ("psum", [128, 8, 64], F),
 }
-DSEM = ["dk", "db", "df", "dp", "dv", "dc0", "dc1", "dc2", "df1", "dn1", "dk1", "dyx", "dy",
-        "ox0", "ox1", "ob0", "ob1", "oy0", "oy1", "of"] + ["kc%d%d" % (t, h) for t in range(4) for h in range(2)]
+DSEM = ["dk", "db", "df", "dp", "dv", "kd", "dc0", "dc1", "dc2", "df1", "dn1", "dyx", "dy",
+        "ox0", "ox1", "ob0", "ob1", "oy0", "oy1", "of"] + ["kc%d%d" % (t, h) for t in range(3) for h in range(2)]
 SEMAPHORES = ["sV", "sS", "sP", "sG"] + DSEM + ["ls%d%d" % (t, h) for t in range(3) for h in range(2)] \
     + ["rs%d%d" % (t, h) for t in range(3) for h in range(2)]
 C23 = 12582912.0
 C28 = 402653184.0
-NOM = {"cy": 1.04, "pe": 0.52, "ga": 1.56, "fix": 60.0, "wake": 60.0, "dlat": 1900.0, "rlat": 4000.0, "kb": 4.5}
-ENG = {"g": ["VSSS"] * 4, "m": ["SSSV"] * 4, "k": ["SSVS"] * 4, "av": ["SSSS"] * 4, "ng": "VSSV", "kev": "VV", "k0h": "V", "kb": "SVSV"}
-SEQ = "00090b0a080102060c0q072j0r03040o0j0d0f2k0l0u2l0p0s0y1n360g311i0x0v0h1j0w0i0t1o050k1k140n1l1g150m1m162b111t12261w13222c1c27253c17282g1s18232d1v192h212i1a1b2e1x331q1d2f2y421e29413f431z2a1u2w1f2r441y1h2m1p4f204q451r2n2o464h47485k2p3e4i2q2s4j544930372v382z4g4k394r2x4b3a3v5m4a3n553o105o4c0e5j2t4d3d5n5s5z324n2u3g4l4s4e3q5u3k4t4m604o4u3l3w0z61354p3z4v563h62664z6n3s5140696350683x67643i4y3y533r5r57655p523j5q6a6q6b3m4x5l3p6o4w6c6r583t5i6d3u6h246k5t345w6e6p6f6g5v6i6u6j596l6w6v6x6y5y6m5e5b5x5d6z5g6s5f725c5h735a70756t7d8y7476717778797e7c7f7g7b7a8z7h7j7k867l877m927n7o939b7i957p943b907r7q917u7w7x7s7y8k889d7z7t808l9c899i8a96979a7v819j83828b9k988h998f849p858e9s9l8ma68d8c9r9m9t9q9n8g8j9u9f8i9o8n9v8o9w9xa3a09h9ya79g9za8a18pa2aba4ad8ta58uaf8qagah8xae9e8rai8wa98valac8saoamajaaanawapakaqarasaxatauayazb0b2b3bpavb4cib5bqb7b6cqchb1cjb8ckbab9bdbfbgbbc3bhbrcrbibcbjbscmcxcpbtcsbebkbuc4bvbmblcobycyc1bnd0boc2c5dlc0czd1bxbwd2bzd4dmd7d3d6d8d5cwd9c6dacldbdcdndidddfc7dedgcndhdsc8ducudjdwdtcvcccbdvctdxcfcadoe0cdcee1c9e3cgdqdpe2e4dke5dydrebdze6e7e8e9ecefehedeif4eaeeejfzfyekelemegf5epeseneueveweofieqexfxfjf6g3eyerg1f7g2g4fwf8etf1f9g5fbezfeg6f0fffcf2gbfhf3gdgcfkg9h6fgfagegag7fdflgfg8hbggh7ghhcfmgjgigkh8fngoh9glfuhdfrgqfvgmfpgrhfhefshhgthgfqg0hifthafogshjh1hlgnhohmgwhkguhnh2huhqi0i1gxhpgvgphvhwhxhshrhyhthzh0h3i2i5i4h4gyi3i6iagzi7h5i8i9"
-ORDER = [int(SEQ[k:k + 2], 36) for k in range(0, len(SEQ), 2)]
+BIG = 1.5 * 2.0 ** 40
+
+FIRST = """load zero tka cols ga sa tkb ba rot ka rr kb kc kdma ff eo0 in0 eo1 in1 fa0 x0 pc0 tt0 kp0 kx0 fa1 fw gb x1 pc1 tt1 kp1 kx1
+ K01V K12S up0 u0 H02S K23V K34V op0 gc oh0S up1 u1 va ol0 op1 gd H24S oh1S ol1 vb bg
+ U01 U12 a0 nr0 cnt0 prc0 pra0 U23 sp0 pz0 mk0 av0 ev0S av1 ev1S a1 U34 pk0 m0 S02S kw0 hi0V lo0 nr1 cnt1 prc1 prb0 tr0 ks0 kd0
+ lw0 r0 sp1 pz1 mk1 av2 ev2S av3 ev3S pra1 prb1 flip0 pk1 m1 S23S kw1 hi1V lo1 S34V tr1 ks1 kd1 flip1 lw1 r1 par x0+"""
+MIDDLE = """H02S x1 H23V K01V K12S pc0 H34S K23V up0 u0 K34S pc1 up1 u1
+ U01 U12 a0 nr0 cnt0 prc0 pra0 U23 sp0 pz0 mk0 av0 ev0S av1 ev1S a1 U34 pk0 m0 S02S kw0 hi0V lo0 nr1 cnt1 prc1 prb0 tr0 ks0 kd0
+ lw0 r0 sp1 pz1 mk1 av2 ev2S av3 ev3S pra1 prb1 flip0 pk1 m1 S23S kw1 hi1V lo1 S34V tr1 ks1 kd1 flip1 lw1 r1 par x0+"""
+LAST = """H02S x1 H23V K01V K12S pc0 H34S K23V up0 u0 K34S pc1 up1 u1
+ U01 U12 a0 nr0 cnt0 prc0 pra0 U23 sp0 pz0 mk0 av0 ev0S av1 ev1S a1 U34 pk0 m0 S02S kw0 yt0 nr1 cnt1 prc1 prb0 ytr0 ys0 yk0
+ lw0 r0 sp1 pz1 mk1 av2 ev2S av3 ev3S pra1 prb1 yx0 eh0 ybp0 yb0 pk1 m1 S23S kw1 yt1 S34V lw1 r1 yx1 ytr1 ys1 yk1 eh1 ybp1 yb1"""
+ORDER = """load zero tka sa ba cols ga tkb ka rot kb rr ff eo0 kc gb in0 eo1 fa1 in1 kdma fw pc0 tt0 tt1 x0 pc1 fa0 kp0 x1 gc kp1 kx0 K12S kx1 op1 K24S vb op0 va pra1 oh1V K01V pra0 up0 oh0V a1 bg ol0 u0 a0 H02S up1 U01 prc0 U12 nr0 ol1 gd prq0 H24S prb0 av0 cnt0 u1 U34 sp0 U23 av1 pz0 prb1 mk0 nr1 kw0 lw0 ev1S av3 cnt1 r0 out0+ prq1 hi0V sp1 prc1 pk0 lo0 tr0 pz1 ev0S mk1 ks0 ev3S av2 kw1 m0 lw1 ev2S S02S hi1V kt0 par lo1 pk1 kd0 m1 r1 tr1 ks1 S24S kd1 x0+ pc0+ kt1 flip1 flip0
+H12S pra0 x1 out2 thr- H01V K12S K01V prb0 pc1 K24S prq0 up0 pra1 prq1 u0 a0 U01 H24S out1 up1 a1 U12 nr0 u1 U23 U34 av0 cnt0 prc0 sp0 av1 nr1 pz0 prb1 mk0 kw0 lw0 cnt1 r0 sp1 pk0 hi0V pz1 lo0 m0 tr0 prc1 ev1S ev0S mk1 kw1 ks0 pk1 lw1 av2 S02S hi1V lo1 ev2S m1 tr1 flip0 ks1 x0+ av3 ev3S kt0 pc0+ kd0 pra0+ prb0+ kd1 kt1 r1 S24S flip1
+K01V K12S up0 x1 pc1 a0 H01V pra1 prq0 H12S u0 U01 par- U12 prb1 nr0 K24S av0 up1 H24S thr- u1 U23 cnt0 sp0 a1 ev0S pz0 av2 U34 mk0 prc0 nr1 kw0 ev2S lw0 cnt1 r0 pk0 sp1 av1 hi0V pz1 ev1S lo0 tr0 mk1 prc1 prq1 m0 ks0 kd0 S02S kt0 kw1 pk1 m1 lw1 r1 av3 hi1V lo1 tr1 ks1 kd1 flip0 x0+ ev3S S24S pc0+ kt1 flip1 pra0+ prq0+
+H12S H01V K12S x1 K24S K01V prb0 pc1 up0 u0 par- pra1 H24S prc0 a0 U01 U12 thr- up1 av0 nr0 u1 U23 av1 cnt0 prq1 ev0S prc1 sp0 pz0 mk0 av2 pk0 U34 ev1S m0 nr1 kw0 lw0 av3 cnt1 S02S yt0 sp1 ev2S r0 ytr0 pz1 prb1 a1 mk1 pk1 ev3S eh0 ys0 kw1 lw1 m1 yx0 S24S yt1 r1 ybp0 ytr1 eh1 ybp1 ys1 yq0 yk0 yx1 yq1S yk1 yb0 yb1""".split("\n")
+ORDER = """load zero sa tka cols ba ga ka rot kb tkb gc ff gb rr eo1 fa1 eo0 in1 kc fa0 pc1 in0 vb fw kdma pc0 tt0 tt1 kp0 kp1 x0 kx0 K12S K01V kx1 x1 pra1 pra0 H02S up0 va u0 U12 U01 op0 op1 a0 K24S gd nr0 uf0S up1 a1 u1 oh0V bg cnt0 oh1V H24S ol0 prb1 av0 U23 ev0S sp0 pz0 U34 mk0 nr1 prb0 ol1 lw0 uf1S pk0 cnt1 r0 prc0 m0 sp1 kw0 pz1 av1 hi0V lo0 mk1 tr0 prc1 ev1S kw1 ks0 lw1 av3 ev3S kd0 hi1V S02S lo1 r1 pk1 kt0 m1 tr1 ks1 x1+ kt1 par flip0 x0+ av2 out2+ ev2S pc0+ S24S flip1 kd1
+K01V pra0 pc1 prb0 H01V K12S up0 H12S pra1 uf0S a0 u0 prc0 prb1 K24S thr- H24S U01 U12 up1 nr0 out0 u1 av0 cnt0 sp0 U23 a1 ev0S pz0 av1 av2 out1 U34 mk0 uf1S nr1 lw0 kw0 pk0 cnt1 r0 hi0V sp1 lo0 m0 pz1 mk1 ev1S tr0 lw1 S02S prc1 par ev2S kw1 ks0 kt0 pk1 av3 r1 hi1V kd0 m1 x0+ lo1 flip0 tr1 ks1 thr pc0+ pra0+ ev3S x1+ kt1 S24S pc1+ flip1 kd1
+H01V H12S prb0 K01V K12S up0 u0 a0 U01 U12 K24S nr0 uf0S pra1 prc0 up1 a1 u1 av0 H24S cnt0 av1 U34 sp0 uf1S pz0 prb1 U23 mk0 nr1 lw0 ev0S av2 kw0 r0 cnt1 hi0V pk0 lo0 ev1S sp1 m0 tr0 ks0 pz1 mk1 kd0 ev2S prc1 lw1 par S02S kt0 kw1 pk1 thr r1 hi1V lo1 x0+ av3 ev3S pc0+ m1 S24S tr1 ks1 flip0 flip1 pra0+ kt1
+H12S kd1- H01V K12S prb0 x1 K24S K01V up0 pc1 pra1 u0 U12 a0 H24S prb1 up1 av1 U01 uf1S nr0 u1 U23 a1 cnt0 sp0 U34 uf0S prc0 pz0 av0 mk0 nr1 ev1S pk0 kw0 av3 cnt1 yt0 m0 ytr0 ev3S sp1 pz1 lw0 ev0S mk1 ys0 prc1 S02S kw1 r0 av2 yx0 yt1 ytr1 pk1 ev2S eh0 ys1 lw1 m1 r1 yq0 ybp0 yk1 yq1S eh1 S24S yk0 yb0 ybp1 yx1 yb1""".split("\n")
+FIRST = "load zero ga tka cols ba tkb ff ka kb kc rot rr eo0 sa va gb in0 eo1 kdma pc0 tt0 fa0 fw kp0 op0 in1 kx0 K12S K01V up0 x0 tt1 fa1 pc1 kp1 u0 kx1 gc op1 H02S vb bg pra0 a0 x1 gd oh0V U12 K24S up1 U01 nr0 oh1V ol1 u1 ol0 cnt0 sp0 H24S pz0 prb0 mk0 lw0 av0 U34 r0 uf0S uf1S U23 nr1 pk0 m0 prc0 av1 kw0 hi0V cnt1 ev1S lo0 tr0 sp1 pz1 mk1 prc1 ks0 kw1 ev0S pk1 par hi1V m1 kd0 aw2 kt0 lo1 tr1 ks1 kd1 pra1 prb1 kt1 S02S thr a1 lw1 flip0 ev2V S23S r1 x0+ aw3 ev3V S34S flip1 pc0+ pra0+ prb0+"
+MIDDLE = "K01V out0 x1 K12S H02S up0 u0 U12 out1 U01 a0 nr0 av1 K24S up1 pc1 u1 cnt0 sp0 pra1 H24S U23 uf0S pz0 mk0 av0 ev1S ev0S U34 uf1S lw0 r0 prb1 nr1 prc0 kw0 hi0V lo0 pk0 cnt1 sp1 tr0 m0 pz1 ks0 kt0 kd0 mk1 prc1 kw1 aw2 hi1V lo1 S02S pk1 m1 tr1 ks1 kd1 aw3 kt1 x0+ ev2V flip0 par thr a1 lw1 r1 S23S ev3V S34S pc0+ pra0+ prb0+ flip1 out2"
+LAST = "K12S K01V up0 H02S u0 x1 uf0S a0 prc0 U12 av1 U01 nr0 K24S up1 cnt0 pc1 H24S u1 sp0 pra1 pz0 mk0 av0 uf1S kw0 ev0S a1 U34 ev1S yt0 ytr0 ys0 U23 pk0 m0 lw0 S02S av2 ev2S nr1 cnt1 r0 av3 eh0 sp1 pz1 mk1 prc1 pk1 m1 kw1 ev3S yt1 S34V prb1 S23S lw1 yk0 yq0 r1 yx0 ytr1 ys1 yx1 eh1 yq1S ybp0 yk1 ybp1 yb0 yb1"
+FIRST = "zero load tka cols ba ka kb kc ga rot tkb kdma gb rr ff sa eo1 va gc eo0 fa1 in1 fa0 op0 in0 tt0 gd tn0V pc0 kp0 x0 tn1V fw kx0 K12S H02S op1 pc1 tt1 kp1 oh0V ol0 K01V kx1 x1 vb up0 u0 U01 U12 nr0 pra0 a0 oh1V K24S uf0S pra1 ol1 H24S af0 ad0 ac0 up1 bg u1 cnt0 sp0 prc0 pz0 mk0 ev0S prb0 lw0 r0 af1 ad1 ac1 pk0 U23 ev1S ar0+ kw0 hi0S prb1 af2 af3 U34 lo0 tr0 ad3 nr1 cnt1 sp1 ks0 kt0 uf1S prc1 pz1 m0 kd0 a1 mk1 lw1 r1 ac3 pk1 ev3S kw1 hi1V m1 ad2 ac2 ev2S par lo1 tr1 ks1 S23V S34S flip1 S02S flip0 kd1 kt1 tn0S+ thr x0+ pc0+ pra0+ prb0+"
+MIDDLE = "H12S H01V ar1 af0 K01V af1 K12S up0 x1 u0 tn1S a0 pc1 pra1 U01 K24S U12 up1 u1 ad0 nr0 H24S U34 uf1S ac0 ad1 ac1 uf0S cnt0 ev0S prb1 sp0 ev1S pz0 U23 prc0 mk0 lw0 pk0 nr1 kw0 r0 ar0+ cnt1 sp1 a1 hi0S pz1 lo0 mk1 tr0 ks0 kd0 af2 lw1 pk1 kt0 r1 par prc1 kw1 m0 hi1V lo1 tr1 af3 ad3 out2 m1 ks1 kd1 ad2 S02S flip0 ac3 ev3S kt1 out0 ac2 ev2S S23V S34S flip1 out1 tn0S+ pc0+ pra0+ x0+ prb0+ thr"
+LAST = "H12S ar1 K12S H01V K01V x1 tn1S pc1 up0 pra1 K24S u0 U01 a0 av0 up1 U12 nr0 cnt0 H24S u1 uf1S uf0S sp0 ev0S a1 U23 pz0 mk0 U34 av1 ev1S prc0 kw0 yt0 av2 ev2S lw0 nr1 ytr0 pk0 ys0 cnt1 r0 m0 prc1 sp1 pz1 yk0 yq0 S02S av3 mk1 kw1 pk1 eh0 prb1 yx0 lw1 yt1 ev3S ytr1 ys1 ybp0 yq1S yk1 m1 r1 eh1 ybp1 S23S S34V yb0 yx1 yb1"
+FIRST = "zero ga cols tka load ba rot ka kb kc gb fa0 fa1 tkb rr va ff eo1 sa kdma in1 x1 eo0 in0 tn0V op1 tt0 fw pc0 tn1V kp0 op0 pc1 kx0 x0 K01V oh1V tt1 oh0V K12S up0 ol1 ol0 kp1 gc vb H02S pra0 gd pra1 af1 kx1 K24S H24S a0 u0 U01 af0 U12 nr0 ad0 ad1 ac1 up1 u1 cnt0 ac0 sp0 prb0 uf0S prc0 U23 uf1S ev1S pz0 bg U34 a1 mk0 lw0 pk0 kw0 nr1 r0 m0 cnt1 af3 ad3 ac3 prb1 ar0+ sp1 pz1 hi0S lo0 mk1 ev0S S02S af2 tr0 ad2 ac2 ev2S ks0 kt0 lw1 r1 prc1 kw1 ev3S par hi1V thr lo1 pk1 kd0 m1 S34S S23V tr1 ks1 kd1 x0+ flip1 flip0 tn0S+ pc0+ pra0+ prb0+ kt1"
+MIDDLE = "ar1 x1 H12S af1 K12S tn1S H01V af0 K01V up0 pc1 u0 U01 K24S a0 H24S pra1 U12 nr0 up1 u1 ad1 U34 ad0 cnt0 uf0S ac0 sp0 U23 ac1 pz0 mk0 prc0 prb1 lw0 ev1S nr1 kw0 cnt1 a1 uf1S pk0 r0 ev0S sp1 pz1 hi0S lo0 out0 mk1 tr0 ks0 prc1 af2 m0 kw1 hi1V lo1 kd0 lw1 r1 S02S kt0 pk1 m1 af3 ad3 ac3 ev3S tr1 ad2 ac2 ev2S ks1 kt1 flip0 S23V S34S flip1 ar0+ x0+ par tn0S+ thr pc0+ out2 kd1 pra0+ prb0+ out1"
+LAST = "K12S ar1 x1 K01V up0 H01V K24S H12S u0 U01 a0 up1 U12 nr0 u1 av0 H24S av1 tn1S uf1S uf0S U34 ev1S cnt0 sp0 U23 pz0 mk0 nr1 prc0 kw0 pk0 cnt1 pc1 pra1 prb1 yt0 ytr0 sp1 pz1 mk1 ev0S lw0 a1 lw1 m0 ys0 r0 S02S yx0 eh0 pk1 m1 prc1 kw1 av3 av2 yq0 ev3S yk0 yt1 r1 eh1 ytr1 ybp0 ybp1 ev2S S23S S34V yx1 ys1 yk1 yq1S yb0 yb1"
+ORDER = [FIRST, MIDDLE, MIDDLE, LAST]
 
 
 def rank_program(g, core, T, topo):
@@ -53,22 +75,18 @@ def rank_program(g, core, T, topo):
     rmask = topo.mask(core, nxt)
     neng = len(topo.engines(core, nxt))
     ops = []
-    wid = {F: 4, I: 4, B: 2, U: 2, H16: 2}
+    tag = [""]
 
     def A(n, c0=None, c1=None, st=1, p0=0, p1=128):
         if c0 is None:
             c0, c1 = 0, SCRATCH[n][1][-1]
-        ap = T[n][p0:p1, c0:c1] if st == 1 else T[n][p0:p1, c0:c1:st]
-        return (ap, [(n, c0, c1)], (c1 - c0 + st - 1) // st, wid[SCRATCH[n][2]], False)
+        return (T[n][p0:p1, c0:c1] if st == 1 else T[n][p0:p1, c0:c1:st], [(n, c0, c1)])
 
-    def A3(n, h, k, w=1):
-        a, b = 64 * k, 64 * (k + w)
-        if h is None:
-            return (T[n][:, :, a:b], [(n, a, b), (n, 192 + a, 192 + b)], 128 * w, wid[SCRATCH[n][2]], False)
-        return (T[n][:, h, a:b], [(n, 192 * h + a, 192 * h + b)], 64 * w, wid[SCRATCH[n][2]], False)
+    def Zc(h, c0, c1):
+        return (T.Z[:, h, c0:c1], [("Z", 256 * h + c0, 256 * h + c1)])
 
     def IX(win, off):
-        return (win[0].indirect(off[0]), win[1] + off[1], 16 * off[2], win[3], True)
+        return (win[0].indirect(off[0]), win[1] + off[1])
 
     def cf(n, c0=0, c1=128, st=1, p1=128):
         k = 128 * MF.index(n); return A("CF", k + c0, k + c1, st, 0, p1)
@@ -76,12 +94,12 @@ def rank_program(g, core, T, topo):
     def cb(n, c0=0, c1=128, st=1, p0=0, p1=128):
         k = 128 * MB.index(n); return A("CB", k + c0, k + c1, st, p0, p1)
 
-    def col(k):
-        return A("COL", 4 * k, 4 * k + 1)
+    def col(k, p0=0, p1=128):
+        return A("COL", 4 * k, 4 * k + 1, 1, p0, p1)
 
-    def op(e, fns, outs, ins, cost, sem=None, n=1, lat=0.0):
+    def op(e, fns, outs, ins, sem=None, n=1):
         ops.append({"e": e, "fns": fns, "w": [r for a in outs for r in a[1]], "r": [r for a in ins for r in a[1]],
-                    "sem": sem, "n": n, "c": cost, "lat": lat})
+                    "sem": sem, "n": n, "tag": tag[0]})
 
     def sa(x):
         return x[0] if isinstance(x, tuple) else x
@@ -89,37 +107,31 @@ def rank_program(g, core, T, topo):
     def aps(*xs):
         return [x for x in xs if isinstance(x, tuple)]
 
-    def vc(o, i, two=1, fast=True):
-        if i[4]:
-            return NOM["fix"] + NOM["cy"] * NOM["ga"] * i[2]
-        return NOM["fix"] + NOM["cy"] * max(64, i[2] * two * (0.5 if fast and o[3] == 2 and i[3] == 2 else 1))
-
     def ts(o, i, s1, o0, s2=None, o1=None):
         if o1 is None:
-            op("V", [lambda: g.vector.tensor_scalar(o[0], i[0], sa(s1), None, o0)], [o], aps(i, s1), vc(o, i))
+            op("V", [lambda: g.vector.tensor_scalar(o[0], i[0], sa(s1), None, o0)], [o], aps(i, s1))
         else:
-            op("V", [lambda: g.vector.tensor_scalar(o[0], i[0], sa(s1), sa(s2), o0, o1)], [o], aps(i, s1, s2), vc(o, i))
+            op("V", [lambda: g.vector.tensor_scalar(o[0], i[0], sa(s1), sa(s2), o0, o1)], [o], aps(i, s1, s2))
 
     def tt(o, a, b, o0):
-        two = 2 if SCRATCH[a[1][0][0]][0] == SCRATCH[b[1][0][0]][0] else 1
-        op("V", [lambda: g.vector.tensor_tensor(o[0], a[0], b[0], o0)], [o], [a, b], vc(o, a, two, b[3] == 2))
+        op("V", [lambda: g.vector.tensor_tensor(o[0], a[0], b[0], o0)], [o], [a, b])
 
     def ms(o, c):
-        op("V", [lambda: g.vector.memset(o[0], c)], [o], [], vc(o, o))
+        op("V", [lambda: g.vector.memset(o[0], c)], [o], [])
 
     def act(o, i, scale=1.0, bias=0.0, acc=None):
         if acc is not None:
-            op("S", [lambda: g.scalar.activation(o[0], i[0], ACT.Identity, bias=bias, accum_out=acc[0])], [o, acc], [i], vc(o, i, 1, False))
+            op("S", [lambda: g.scalar.activation(o[0], i[0], ACT.Identity, bias=bias, accum_out=acc[0])], [o, acc], [i])
         elif bias == 0.0:
-            op("S", [lambda: g.scalar.activation(o[0], i[0], ACT.Copy, scale=scale)], [o], [i], vc(o, i, 1, False))
+            op("S", [lambda: g.scalar.activation(o[0], i[0], ACT.Copy, scale=scale)], [o], [i])
         else:
-            op("S", [lambda: g.scalar.activation(o[0], i[0], ACT.Identity, bias=bias, scale=scale)], [o], [i], vc(o, i, 1, False))
+            op("S", [lambda: g.scalar.activation(o[0], i[0], ACT.Identity, bias=sa(bias), scale=scale)], [o], aps(i, bias))
 
     def cp(o, i, e="V"):
         if e == "S":
             act(o, i)
         else:
-            op("V", [lambda: g.vector.tensor_copy(o[0], i[0])], [o], [i], vc(o, i))
+            op("V", [lambda: g.vector.tensor_copy(o[0], i[0])], [o], [i])
 
     def flip(o, i, e="V"):
         if e == "S":
@@ -127,323 +139,393 @@ def rank_program(g, core, T, topo):
         else:
             ts(o, i, -1.0, ALU.mult, 255.0, ALU.add)
 
-    def mm(o, terms, start=True, stop=True, lock=False):
+    def mm(o, terms, start=True, stop=True, whole=False):
         op("P", [lambda l=l, r=r, k=k: g.tensor.matmul(o[0], l[0], r[0], start and k == 0, stop and k == len(terms) - 1)
-                 for k, (l, r) in enumerate(terms)],
-           [o] + ([A("pX", 511, 512)] if lock else []), [a for lr in terms for a in lr], sum(10 + NOM["pe"] * max(min(64, l[2]), r[2]) * (4 if l[3] == 4 else 1) for l, r in terms))
+                 for k, (l, r) in enumerate(terms)], [o] + ([(None, [(o[1][0][0], 0, 512)])] if whole else []), [a for lr in terms for a in lr])
 
-    def dma(o, i, sem, kb, q="Y"):
-        op(q, [lambda: (g.sync if q == "Y" else g.scalar).dma_start(o[0], i[0])], [o], [i], 100.0, sem, 16, NOM["dlat"])
-        ops[-1]["kb"] = kb
+    def acc(o, terms, stop=False):
+        mm(o, terms, False, stop, stop)
+
+    def wipe(o, mask, stop=False):
+        acc(o, [(cb("Kp"), mask), (cb("Kn"), mask)], stop)
+
+    def pC(k, w=1):
+        return (T.pY[:, k:k + w, :], [("pY", 0, 64)])
+
+    def dma(o, i, sem, q="Y"):
+        op(q, [lambda: (g.sync if q == "Y" else g.scalar).dma_start(o[0], i[0])], [o], [i], sem, 16)
 
     def X(ap):
         return (ap, [])
 
     def iota(o, pat, base, cm):
-        op("G", [lambda: g.iota(o[0], pat, base, cm, allow_small_or_imprecise_dtypes=True)], [o], [], 130 + 2 * NOM["cy"] * o[2])
+        op("G", [lambda: g.iota(o[0], pat, base, cm, allow_small_or_imprecise_dtypes=True)], [o], [])
 
     def sel(o, i, pat, base, fill, cmp=ALU.not_equal, cm=1):
-        op("G", [lambda: g.affine_select(o[0], i[0], pat, cmp, fill, base, cm)], [o], [i], 170 + 2 * NOM["cy"] * o[2])
-
-    dma(A("EI", 0, 256, 1, 0, 64), X(T.kid0[:]), "dk", 64, "S")
-    dma(A("EI", 0, 256, 1, 64, 128), X(T.kid1[:]), "dk", 64)
-    dma(A("EI", 256, 512), X(T.belts[:]), "db", 128)
-    dma(A("FI", 0, 256, 1, 0, 8), X(T.flip[:]), "df", 8, "S")
-    dma(A("TF0", 0, 2048), X(T.faces[:]), "dp", 512)
-    dma(A("TF0", 2048, 4096), X(T.faces[:]), "dv", 512)
-    iota(A("IO2"), [[-1, 128]], 0, 1)
-    ms(A("KP", 0, 256, 1, 0, 64), 0.0)
-    iota(A("IO4"), [[-1, 8], [300, 2], [0, 8]], 0, 1)
-    iota(A("IO"), [[-1, 8], [-8, 8]], 0, 1)
-    ms(A("MS"), 0.0); ms(A("ZF"), 0.0); ms(A("ZB"), 0.0); ms(A("ONE"), 1.0); ms(A("M4"), -4.0)
-    ts(cf("If"), A("IO2"), 0.0, ALU.is_equal)
-    sel(cf("U16"), A("ZF"), [[-1, 128]], -1, 1.0)
-    sel(cf("U16", 15, 128, 16), A("ZF", 0, 8), [[-16, 8]], 0, 1.0)
-    sel(cf("U16"), cf("U16"), [[-1, 128]], 0, -1.0)
-    for b in range(2):
-        sel(cf("E%d" % b), A("ZF"), [[-16, 8], [300, 2], [-2, 8]], -300 * b, 0.5)
-        sel(cf("O%d" % b), A("ZF"), [[-16, 8], [300, 2], [-2, 8]], -300 * b - 1, 0.5)
-        ts(cb("GX%d" % b, p1=8), A("IO4", 0, 128, 1, 0, 8), 300.0 * b, ALU.is_equal)
-    tt(cb("GX", p1=8), cb("GX0", p1=8), cb("GX1", p1=8), ALU.add)
-    ts(A("MS", 2, 1026, 16, 64, 128), A("IO", 0, 64, 1, 64, 128), 64.0, ALU.is_equal, 0.5, ALU.mult)
-    ts(A("MS", 4, 1028, 16, 0, 64), A("IO", 0, 64, 1, 0, 64), 0.0, ALU.is_equal, 0.5, ALU.mult)
-    for n, s in (("Ib", 1.0), ("n4I", -4096.0), ("nIb", -1.0), ("I2k", 2048.0), ("n8I", -8192.0)):
-        act(cb(n), cf("If"), s)
-    act(cf("nIf"), cf("If"), -1.0); act(cf("n2If"), cf("If"), -2.0)
-    ts(A("CH", 0, 128), cf("If"), 2.0 ** -10 - 1.0, ALU.mult)
-    ts(A("CH", 128, 256), cf("If"), 2.0 ** -11 - 0.5, ALU.mult)
-
-    ts(A("SI", 256, 512), A("EI", 256, 512), 1, ALU.bitwise_and)
-    ts(A("pX", 0, 256), A("SI", 256, 512), 8191.0, ALU.mult)
-    tt(A("P0"), A("pX", 0, 256), A("EI", 256, 512), ALU.add)
-    cp(A("FF", 0, 256, 1, 0, 8), A("FI", 0, 256, 1, 0, 8))
-    mm(A("pA", 0, 256), [(cb("GX", p1=8), A("FF", 0, 256, 1, 0, 8))])
-    act(A("FB"), A("pA", 0, 256))
-    mm(A("pZ", 0, 256), [(cf("U16"), A("P0"))])
-    tt(A("pZ", 256, 512), A("pZ", 0, 256), A("FB"), ALU.mult)
-    tt(A("RR"), A("pZ", 256, 512), A("P0"), ALU.add)
-    for h in range(2):
-        for k, m in enumerate("EO"):
-            mm(A("pA", 192 * h + 64 * k, 192 * h + 64 * k + 64),
-               [(cf("%s%d" % (m, b)), A("RR", 128 * h + b, 128 * h + 128, 2)) for b in range(2)])
-        mm(A("pA", 192 * h + 128, 192 * h + 192),
-           [(cb("GX%d" % b, p1=8), A("FF", 128 * h + b, 128 * h + 128, 2, 0, 8)) for b in range(2)])
-        cp(A3("IN0", h, 0, 3), A("pA", 192 * h, 192 * h + 192))
-    ts(A("SI", 0, 256), A("EI", 0, 256), 1, ALU.bitwise_and)
-    ts(A("pX", 256, 512), A("SI", 0, 256), 8191.0, ALU.mult)
-    tt(A("pV1", 0, 256), A("pX", 256, 512), A("EI", 0, 256), ALU.add)
-    cp(A("KP", 256, 512), A("pV1", 0, 256))
-    tt(A("KP", 512, 768), A("pV1", 0, 256), A("KP", 256, 512), ALU.subtract)
-    ms(cb("C3", 0, 64), 393216.0)
-    ts(A("KP", 0, 256, 1, 64, 128), A("SI", 0, 256, 1, 64, 128), 2.0, ALU.mult, -1.0, ALU.add)
-    for k, bank in enumerate(["pE0", "pE1", "pV0", "pV1"]):
-        for cc in (2 * k, 2 * k + 1):
-            mm(A(bank, 256 * (cc % 2), 256 * (cc % 2) + 256),
-               [(A("MS", 2 - pc + 128 * cc, 130 - pc + 128 * cc), A("KP", 256 * pc, 256 * pc + 256)) for pc in range(3)])
-        cp(A("TK0", 512 * k, 512 * k + 512), A(bank), ENG["kb"][k])
-    flip(A("TF0", 4096, 5120), A("TF0", 0, 1024), ENG["ng"][0])
-    flip(A("TF0", 6144, 7168), A("TF0", 0, 1024), ENG["ng"][1])
-    flip(A("TF0", 7168, 8192), A("TF0", 1024, 2048), ENG["ng"][2])
-    ms(cb("N2k", 0, 64), -2048.0); flip(A("TF0", 5120, 6144), A("TF0", 1024, 2048), ENG["ng"][3])
+        op("G", [lambda: g.affine_select(o[0], i[0], pat, cmp, fill, base, cm)], [o], [i])
 
     def Wm(k, c0=0, c1=144, st=1):
         return A("W", 144 * k + c0, 144 * k + c1, st)
 
-    def wrows(k, rows):
-        (r0, w0) = rows[0]
-        sel(Wm(k), A("ZB"), [[-16, 9], [200, 16]], -r0 - 3000, w0)
-        for r, w in rows[1:]:
+    def wrows(k, rows, w):
+        sel(Wm(k), A("ZB"), [[-16, 9], [200, 16]], -rows[0] - 3000, w)
+        for r in rows[1:]:
             sel(Wm(k, 15, 128, 16), Wm(k, 15, 128, 16), [[-16, 8]], -r, w)
-    wrows(0, [(0, -4096.0), (1, 0.5), (2, 0.5), (3, 0.5), (4, 0.5)])
-    wrows(1, [(0, 8192.0), (1, -1.0), (2, -1.0), (3, 1.0), (4, 1.0)])
+
+    def rows2list(o, k, n, c, start, stop, whole=False):
+        mm(o, [(Wm(k, 15 - q, 143 - q), A(n, c + q, c + 1024, 16)) for q in range(16)], start, stop, whole)
+
+    def L(n, h, k=0, per=1, w=1):
+        return A(n, 64 * (per * h + k), 64 * (per * h + k + w))
+
+    def pL(h, k, w=1):
+        return A("pL%d" % h, 64 * k, 64 * (k + w))
+
     dg = [[-1, 128]]
-    sel(cf("DnIf"), A("ZF"), dg, 1, 1.0)
-    sel(cf("DnIf", 0, 128, 8), A("ZF", 0, 16), [[-8, 16]], -7, 1.0)
-    sel(cf("DnIf"), cf("DnIf"), dg, 0, -1.0)
-    sel(cf("IUpf"), A("ZF"), dg, -1, -1.0)
-    sel(cf("IUpf", 7, 128, 8), A("ZF", 0, 16), [[-8, 16]], 0, -1.0)
-    sel(cf("IUpf"), cf("IUpf"), dg, 0, 1.0)
-    sel(cf("Upf"), A("ZF"), dg, -1, 1.0)
-    sel(cf("Upf", 7, 128, 8), A("ZF", 0, 16), [[-8, 16]], 0, 1.0)
-    wrows(2, [(0, 1.0)])
-    sel(Wm(2, 15, 128, 16), A("ONE", 0, 8), [[-16, 8]], 0, 0.0, ALU.is_ge)
-    sel(Wm(2, 15, 128, 16), Wm(2, 15, 128, 16), [[16, 8]], 15, 0.0, ALU.is_ge, -1)
-    for n, src in (("B8I", "ONE"), ("nB4", "M4")):
-        sel(cb(n), A(src, 0, 128), [[-8, 16], [0, 8]], 0, 0.0, ALU.is_ge)
-        sel(cb(n), cb(n), [[8, 16], [0, 8]], 7, 0.0, ALU.is_ge, -1)
-    sel(cb("B8I"), cb("B8I"), dg, 0, 9.0)
-    iota(cb("C16M"), [[16, 128]], 2048, 0)
-    iota(cb("C16", 0, 64), [[16, 64]], 0, 0)
-    op("G", [lambda: g.iota(T.COI[:, 0:1], [[0, 1]], 0, 1)], [A("COI", 0, 1)], [], 140.0)
-    act(cb("DnIb"), cf("DnIf")); act(cb("DnI8"), cf("DnIf"), -8192.0); act(cb("IUp8"), cf("IUpf"), -8192.0); act(cb("Up8"), cf("Upf"), -8192.0)
-    ms(cb("C20", 0, 64), 20.0); ms(cb("EI8"), 0.125); ms(col(2), 10.0); ms(col(3), 1.0); ms(cb("CC", p1=32), C23 / 32)
-    ts(A("COI", 4, 5), A("COI", 0, 1), 15, ALU.bitwise_and)
-    cp(col(1), A("COI", 4, 5))
-    ts(cb("QT", 0, 64), A("ONE", 0, 64), col(1), ALU.mult)
-    cp(A("KF"), A("EI", 0, 256))
-    dma(A("TK0", 2048, 4096), X(T.faces[:]), "dc0", 512)
-    dma(A("TF1", 4096, 6144), A("TF0", 4096, 6144), "dn1", 512)
-    dma(A("TK1", 0, 2048), A("TK0", 0, 2048), "dk1", 512)
-    dma(A("TF1", 0, 2048), X(T.faces[:]), "df1", 512)
+    zb, z8, nf = A("ZB", 0, 128), A("ZB", 0, 128, 1, 0, 8), A("FF", 256, 512, 1, 0, 8)
 
-    def background(t):
-        if t == 0:
-            dma(A("TK1", 4096, 6144), X(T.faces[:]), "dc1", 512)
-        if t == 1:
-            dma(A("TK0", 4096, 6144), X(T.faces[:]), "dc2", 512)
-            dma(X(T.yx[:, 0:2048]), A("TF0", 0, 2048), "dyx", 512)
-            dma(X(T.y0[:, 0:2048]), A("KF", 0, 256, 1, 0, 64), "dy", 64)
-            dma(X(T.y1[:, 0:2048]), A("KF", 0, 256, 1, 64, 128), "dy", 64)
-    p8 = [[-16, 8], [-1, 8]]
-    pz = [[-16, 8], [-1, 8], [300, 2]]
-    for b in range(2):
-        sel(cf("a%d" % b), A("ZF"), pz, -8 * b, 2.0)
-        sel(cf("b%d" % b), A("ZF"), pz, -8 * b - 300, 2.0)
-        sel(cf("c%d" % b), A("ZF"), pz, -8 * b, -2.0)
-        sel(cf("c%d" % b, 1, 128, 2), cf("c%d" % b, 1, 128, 2), p8, -8 * b, 2.0)
-        sel(cf("d%d" % b), A("ZF"), pz, -8 * b + 1, 2.0)
-        sel(cf("d%d" % b, 0, 128, 16), A("ZF", 0, 8), [[-16, 8]], -8 * b - 7, 2.0)
-        sel(cf("d%d" % b, 1, 128, 2), cf("d%d" % b, 1, 128, 2), p8, -8 * b, -2.0)
-        sel(cf("FT", 8 * b, 8 * b + 8), A("ZF", 0, 8), [[-16, 8]], -8 * b, 1.0)
-    for k, rows in ((3, [(3, 0, 2.0), (4, 0, 2.0), (1, 1, 2.0), (2, 1, 2.0)]),):
-        sel(Wm(k), A("ZB"), [[0, 144]], 1000, 0.0)
-        for r, kid, w in rows:
-            a = Wm(k, 7 + 64 * kid, 64 + 64 * kid, 8)
-            sel(a, a, [[-16, 8]], -r, w)
-
-    def L(n, h, k=0, per=1):
-        if n == "sK":
-            n, per = "Z", 7
-        return A(n, 64 * (per * h + k), 64 * (per * h + k) + 64)
-
-    def Zb(k, h):
-        return L("Z", h, k + 1, 7)
-
-    def big(n, h, base=0):
-        return A(n, base + 1024 * h, base + 1024 * h + 1024)
-
-    def halves(fn, out, base, win, lst, h, eng):
-        c = base + 1024 * h
-        if eng[2 * h] == eng[2 * h + 1]:
-            fn(A(out, c, c + 1024), IX(win, L(lst, h)), eng[2 * h])
-        else:
+    def setup(kind, h, e):
+        if kind == "load":
+            dma(A("EI", 256, 512), X(T.belts[:]), "db")
+            dma(A("FI", 0, 256, 1, 0, 8), X(T.flip[:]), "df", "S")
+            dma(A("EI", 0, 256, 1, 0, 64), X(T.kid0[:]), "dk", "S")
+            dma(A("EI", 0, 256, 1, 64, 128), X(T.kid1[:]), "dk")
+            dma(A("TF0", 0, 2048), X(T.faces[:]), "dp")
+        elif kind == "zero":
+            ms(A("ZF"), 0.0); ms(A("ZB"), 0.0)
+            iota(A("IO2"), dg, 0, 1)
+            ts(cf("If"), A("IO2"), 0.0, ALU.is_equal)
+        elif kind == "tka":
+            ms(A("TK", 0, 2048), 0.0)
+        elif kind == "tkb":
+            act(A("TK", 2048, 4096), A("TK", 0, 2048))
+        elif kind == "cols":
+            ms(col(5, 0, 64), 8191.0); ms(col(5, 64, 128), -8193.0); ms(col(6, 0, 64), -4096.0); ms(col(6, 64, 128), 4096.0)
+        elif kind == "ga":
+            sel(cf("U16"), A("ZF"), dg, -1, 1.0)
+            sel(cf("U16", 15, 128, 16), A("ZF", 0, 8), [[-16, 8]], 0, 1.0)
+            sel(cf("U16"), cf("U16"), dg, 0, -1.0)
+            sel(cb("GXp", p1=8), z8, [[-1, 8], [0, 16]], 0, BIG)
+            sel(cb("GXn", p1=8), z8, [[-1, 8], [0, 16]], 0, -BIG)
+            for m, o in (("E", 0), ("O", 1)):
+                for b in range(2):
+                    sel(cf("%s%d" % (m, b)), A("ZF"), [[-16, 8], [300, 2], [-2, 8]], -300 * b - o, 0.5)
+            for b in range(2):
+                sel(cb("GX%d" % b, p1=8), z8, [[-1, 8], [300, 2], [0, 8]], -300 * b, 4096.0)
+        elif kind == "sa":
+            for n, s in (("Ib", 1.0), ("nIb", -1.0), ("nhI", -0.5), ("I2", 2.0), ("Kp", BIG / 4096), ("Kn", -BIG / 4096)):
+                act(cb(n), cf("If"), s)
+            for o, c in ((cb("C3"), 397312.0), (cb("C20"), 20.0), (cb("EI8"), 0.125 / 4096), (cb("CC"), C23 / 32),
+                         (A("CT", 128, 256), 4096.0), (A("CT", 64, 128), 4096.0), (A("CT", 0, 64), 8192.0)):
+                act(o, A("ZB", 0, o[1][0][2] - o[1][0][1]), 1.0, c)
+        elif kind == "ba":
+            ts(A("SI", 256, 512), A("EI", 256, 512), 1, ALU.bitwise_and)
+            ts(A("pV1", 0, 256), A("SI", 256, 512), 8191.0, ALU.mult, -4096.0, ALU.add)
+            tt(A("P0"), A("pV1", 0, 256), A("EI", 256, 512), ALU.add)
+            ts(nf, A("FI", 0, 256, 1, 0, 8), 0.0, ALU.is_equal)
+        elif kind == "rot":
+            mm(A("pZ", 0, 256), [(cf("U16"), A("P0")), (cb("GXp", p1=8), nf), (cb("GXn", p1=8), nf)])
+        elif kind == "rr":
+            tt(A("RR"), A("pZ", 0, 256), A("P0"), ALU.add)
+        elif kind == "ka":
+            ts(A("SI", 0, 256), A("EI", 0, 256), 1, ALU.bitwise_and)
+            ts(A("pV0", 0, 256), A("SI", 0, 256), col(5), ALU.mult, col(6), ALU.add)
+        elif kind == "kb":
+            tt(A("pV0", 256, 512), A("pV0", 0, 256), A("EI", 0, 256), ALU.add)
+            cp(A("KP", 0, 256), A("pV0", 256, 512))
+        elif kind == "kc":
+            tt(A("KP", 256, 512), A("pV0", 256, 512), A("KP", 0, 256), ALU.subtract)
+        elif kind == "kdma":
+            for r in range(4):
+                for turn in range(2):
+                    c = 2048 - 2048 * turn
+                    dma((T.TK[r + turn:128:16, c:c + 2048], [("TK", c, c + 2048)]),
+                        A("KP", 256 * (r // 2), 256 * (r // 2) + 256, 1, 64 * (r % 2), 64 * (r % 2) + 64), "kd")
+            dma(A("TF0", 2048, 4096), X(T.faces[:]), "dv")
+        elif kind == "ff":
+            act(A("FF", 0, 256, 1, 0, 8), nf, -1.0, 1.0)
+        elif kind == "eo":
+            bank = "pL%d" % h
+            for k, m in enumerate("EO"):
+                mm(A(bank, 64 * k, 64 * k + 64), [(cf("%s%d" % (m, b)), A("RR", 128 * h + b, 128 * h + 128, 2)) for b in range(2)])
+            mm(A(bank, 128, 192), [(cb("GX%d" % b, p1=8), A("FF", 128 * h + b, 128 * h + 128, 2, 0, 8)) for b in range(2)])
+        elif kind == "in":
+            cp(A("IN0", 192 * h, 192 * h + 192), pL(h, 0, 3), "S")
+        elif kind == "fa":
+            flip(A("TF0", 4096 + 1024 * h, 5120 + 1024 * h), A("TF0", 1024 * h, 1024 * h + 1024))
+        elif kind == "fw":
+            flip(A("TF0", 6144, 8192), A("TF0", 0, 2048), "S")
+        elif kind == "gb":
+            wrows(0, [1, 3], 1.0)
+            wrows(3, [0, 2], 1.0)
+            wrows(1, [0, 2, 4], 0.5)
+        elif kind == "gc":
+            iota(Wm(2), [[0, 144]], 0, 0)
+            iota(Wm(2, 15, 128, 16), [[0, 8]], 1, 0)
+            sel(Wm(2, 15, 128, 16), Wm(2, 15, 128, 16), [[-16, 8]], 0, 0.0, ALU.is_ge)
+            sel(Wm(2, 15, 128, 16), Wm(2, 15, 128, 16), [[16, 8]], 15, 0.0, ALU.is_ge, -1)
+            op("G", [lambda: g.iota(T.COI[:, 0:1], [[0, 1]], 0, 1)], [A("COI", 0, 1)], [])
+            iota(cb("C16"), [[16, 128]], 0, 0)
+            for n, c in (("nB4", -4), ("B8I", 1)):
+                iota(cb(n), [[0, 128]], c, 0)
+                sel(cb(n), cb(n), [[-8, 16], [0, 8]], 0, 0.0, ALU.is_ge)
+                sel(cb(n), cb(n), [[8, 16], [0, 8]], 7, 0.0, ALU.is_ge, -1)
+            sel(cb("B8I"), cb("B8I"), dg, 0, 9.0)
+        elif kind == "gd":
+            for n, o, w, c in (("IDn", 1, -1.0, 0), ("Dn", 1, 1.0, 0), ("UpI", -1, 1.0, 7)):
+                sel(cb(n), zb, dg, o, w)
+                sel(cb(n, c, 128, 8), A("ZB", 0, 16), [[-8, 16]], c - 7, w)
+                if n != "Dn":
+                    sel(cb(n), cb(n), dg, 0, -w)
+        elif kind == "va":
+            ts(A("CH", 0, 128), cf("If"), 2.0 ** -10 - 1.0, ALU.mult)
+            ts(A("CH", 128, 256), cf("If"), 2.0 ** -11 - 0.5, ALU.mult)
+            ms(A("ONE", 0, 512, 1, 0, 32), 1.0); ms(col(2), 10.0); ms(col(3), 1.0)
+        elif kind == "vb":
+            ts(A("COI", 4, 5), A("COI", 0, 1), 15, ALU.bitwise_and)
+            ts(col(1), A("COI", 4, 5), 2048.0, ALU.add)
+            ts(A("CM"), cb("C16"), col(1), ALU.add, -2048.0, ALU.add)
+        elif kind == "bg":
+            dma(A("TK", 4096, 6144), A("TK", 2048, 4096), "dc0")
+            dma(A("TK", 8192, 10240), A("TK", 0, 2048), "dc1")
+            dma(A("TK", 6144, 8192), A("TK", 0, 2048), "dc2")
+            dma(A("TF1", 4096, 6144), A("TF0", 4096, 6144), "dn1")
+            dma(A("TF1", 0, 2048), X(T.faces[:]), "df1")
+        elif kind == "tt":
+            ts(L("TT", h), L("IN0", h, 0, 3), 394240.5, ALU.add)
+        elif kind == "kp":
+            mm(L("pZ", h, 4), [(cb("Ib"), L("PC", h, 0, 2)), (cb("nhI"), L("TN", h, 0, 3)), (cb("nIb"), L("TT", h)), (cb("Ib"), cb("C3", 0, 64))])
+        elif kind == "kx":
+            cp(L("p16", h), L("pZ", h, 4))
+        elif kind == "op":
             for k in range(2):
-                fn(A(out, c + 512 * k, c + 512 * k + 512), IX(win, A(lst, 64 * h + 32 * k, 64 * h + 32 * k + 32)), eng[2 * h + k].upper())
+                rows2list(A("pV%d" % h, 64 * k, 64 * k + 64), 3 - 3 * k, "TK", 2048 + 1024 * h, True, True)
+        elif kind == "oh":
+            cp(Zc(h, 0, 128), A("pV%d" % h, 0, 128), e)
+        elif kind == "ol":
+            tt(Zc(h, 128, 256), A("pV%d" % h, 0, 128), Zc(h, 0, 128), ALU.subtract)
+        else:
+            raise ValueError(kind)
 
-    def pE(h, c0, c1):
-        return A("pE%d" % h, c0, c1)
+    def outputs_of_the_drawn(k):
+        if k == 0:
+            cp(A("KF"), A("EI", 0, 256))
+            ms(col(7, 0, 32), 4096.0); ms(col(7, 32, 64), 4097.0)
+            return
+        if k == 1:
+            dma(X(T.yx[:, 0:2048]), A("TF0", 0, 2048), "dyx")
+            dma(X(T.y0[:, 0:2048]), A("KF", 0, 256, 1, 0, 64), "dy")
+            dma(X(T.y1[:, 0:2048]), A("KF", 0, 256, 1, 64, 128), "dy")
+            return
+        p8 = [[-16, 8], [-1, 8]]
+        pz = [[-16, 8], [-1, 8], [300, 2]]
+        w = 2.0 / 4096
+        for b in range(2):
+            sel(cf("a%d" % b), A("ZF"), pz, -8 * b, 2.0)
+            sel(cf("b%d" % b), A("ZF"), pz, -8 * b - 300, 2.0)
+            sel(cf("c%d" % b), A("ZF"), pz, -8 * b, -w)
+            sel(cf("c%d" % b, 1, 128, 2), cf("c%d" % b, 1, 128, 2), p8, -8 * b, w)
+            sel(cf("d%d" % b), A("ZF"), pz, -8 * b + 1, w)
+            sel(cf("d%d" % b, 0, 128, 16), A("ZF", 0, 8), [[-16, 8]], -8 * b - 7, w)
+            sel(cf("d%d" % b, 1, 128, 2), cf("d%d" % b, 1, 128, 2), p8, -8 * b, -w)
+            sel(cf("FT", 8 * b, 8 * b + 8), A("ZF", 0, 8), [[-16, 8]], -8 * b, w / 2)
 
-    def visit(t):
+    def kid_rows(t, h, turn, q):
+        c = 4096 + 4096 * turn + 1024 * h
+        for gg in range(8):
+            p = 16 * gg + turn
+            dma((T.TK[p:p + 4, c:c + 1024], [("TK", c, c + 1024, gg)]), (T["KS%d" % h][0:256 // NT, gg, :], [("KS%d" % h, 0, 1)]),
+                "kc%d%d" % (t, h), q)
+
+    def step(name, t):
+        if name[-1] in "+-":
+            name, t = name[:-1], t + (1 if name[-1] == "+" else -1)
+        if name[:2] == "ar":
+            k = int(name[2])
+            return op("X", [], [L("IN%d" % t, k, 0, 3, 3)], [], "rs%d%d" % (t - 1, k), neng) if t else None
         last = t == RO - 1
-        tf, tfn, tk, tkn, inb = "TF%d" % (t % 2), "TF%d" % ((t + 1) % 2), "TK%d" % (t % 2), "TK%d" % ((t + 1) % 2), "IN%d" % t
-        kv = 0 if t == 0 else 2048
-        Ib = cb("Ib")
-        for h in range(2):
-            K = A3("PH", h, 0)
-            if t > 0:
-                op("X", [], [A3(inb, h, 0, 3)], [], 0.0, "rs%d%d" % (t - 1, h), neng)
-            act(big("FW", h), IX(A(tf, 0, 8192), A3(inb, h, 1)))
-            cp(A3("PH", h, 0, 3), A3(inb, h, 0, 3))
-            ts(A("Z", 448 * h, 448 * h + 128), A3(inb, h, 0, 2), 4096.0, ALU.is_ge, 0.5, ALU.subtract)
-            if t == 0:
-                ts(L("TT", h), A3(inb, h, 0), 392192.5, ALU.add)
-                mm(L("pA", h, 6), [(cf("If"), K), (cb("nIb"), L("TT", h)), (Ib, cb("C3", 0, 64))])
-                cp(L("p16", h), L("pA", h, 6))
-            else:
-                mm(L("pA", h), [(cf("If"), K), (cb("n4I"), L("sK", h)), (Ib, cb("N2k", 0, 64))])
-                cp(L("p16", h), L("pA", h))
-            halves(cp, "G", 0, A(tk, 0, kv + 2048), "p16", h, ENG["g"][t])
-            gq = [A("G", 1024 * h + q, 1024 * h + 1024, 16) for q in range(16)]
-            mm(A("pV%d" % h, 0, 64), [(Wm(1, 15 - q, 143 - q), gq[q]) for q in range(16)])
-            tt(L("sd", h), A("pV%d" % h, 0, 64), L("sK", h), ALU.mult)
-            mm(L("pX", h, 4), [(Wm(0, 15 - q, 143 - q), gq[q]) for q in range(16)], stop=False, lock=True)
-            mm(L("pX", h, 4), [(cf("If"), L("sd", h))], start=False, lock=True)
-            cp(L("u16", h), L("pX", h, 4))
-        for h in range(2):
-            cp(Zb(1, h), A3("PH", h, 1), "S")
-            tt(Zb(2, h), A3("PH", h, 1), Zb(1, h), ALU.subtract)
-            cp(Zb(3, h), L("pX", h, 4), ENG["k0h"])
-            tt(Zb(4, h), L("pX", h, 4), Zb(3, h), ALU.subtract)
-            pk = (None, [("pK", 0, 1)])
-            op("P", [lambda cl=cl, h=h: g.tensor.transpose(T.pK[0:320 // NT[h], :, 16 * cl:16 * cl + 16],
-                                                           T.Z[:, 448 * h + 64 + cl:448 * h + 384:NT[h]], Ib[0])
-                     for cl in range(NT[h])], [pk], [A("Z", 448 * h + 64, 448 * h + 384), Ib], NT[h] * (10 + 128 * NOM["pe"]))
-            ks = (T["KS%d" % h][0:320 // NT[h], :, :], [("KS%d" % h, 0, 1)], 128 * NT[h], 2, False)
-            cp(ks, (T.pK[0:320 // NT[h], :, 0:16 * NT[h]], pk[1], 128 * NT[h], 2, False), ENG["kev"][h])
-            c = kv + 2048 + 1024 * h
-            for gg in range(8):
-                dma((T[tk][16 * gg:16 * gg + 5, c:c + 1024], [(tk, c, c + 1024, gg)]), (T["KS%d" % h][0:320 // NT[h], gg, :], ks[1]),
-                    "kc%d%d" % (t, h), 320 // NT[h])
-        background(t)
-        if not last:
-            for h in range(2):
-                mm(pE(h, 256, 320), [(cb("DnIb" if k else "DnI8"), Zb(k, h)) for k in range(3)])
-                mm(pE(h, 320, 384), [(cf("IUpf"), A3("PH", h, 0)), (cb("IUp8"), L("sK", h))])
-                for k in range(2):
-                    tt(L("Q", h, 2 * k), pE(h, 256 + 64 * k, 320 + 64 * k), A3("PH", h, 2), ALU.mult)
-        for h in range(2):
-            K = A3("PH", h, 0)
-            nH = [(cb("nIb"), Zb(1, h)), (cb("nIb"), Zb(2, h))]
-            mm(pE(h, 0, 64), [(Ib, Zb(3, h)), (Ib, Zb(4, h)), (cf("n2If"), L("sd", h)), (cf("nIf"), K)])
-            mm(pE(h, 64, 128), nH + [(Ib, L("CB", 2 * MB.index("C16M") + h)), (Ib, cb("QT", 0, 64))])
-            if last:
-                mm(pE(h, 128, 192), [(cb("n8I"), L("sK", h))])
-                mm(pE(h, 192, 256), [(cb("n8I"), Zb(0, h))])
-            else:
-                mm(pE(h, 128, 192), [(Ib if k else cb("n8I"), Zb(k, h)) for k in range(3)] + [(cf("nIf"), K), (cf("If"), L("Q", h))])
-                mm(pE(h, 192, 256), [(cb("Up8"), L("sK", h)), (cf("Upf"), K)] + nH + [(cf("If"), L("Q", h, 2))])
-        for h in range(2):
-            tt(big("D", h), IX(A(tf, 0, 8192), L("u16", h)), big("FW", h), ALU.subtract)
-            ts(big("NR", h), big("D", h), C28, ALU.add, C28, ALU.is_equal)
-            mm(L("pA", h, 4), [(Wm(2, 15 - q, 143 - q), A("NR", 1024 * h + q, 1024 * h + 1024, 16)) for q in range(16)])
-            for k in range(2):
-                c = 1024 * h + 512 * k
-                half = [(A("CH", 0, 128), A("FW", c, c + 512)), (A("CH", 128, 256), A("D", c, c + 512))]
-                if ENG["av"][t][2 * h + k] == "S":
-                    mm(A("pV%d" % k), half + [(cb("CC", p1=32), A("ONE", 0, 512, 1, 0, 32))])
-                    act(A(tf, 8192 + c, 8704 + c), A("pV%d" % k), 1.0, 255.0 - C23)
+        tf, tfn, inb, rb = "TF%d" % (t % 2), "TF%d" % ((t + 1) % 2), "IN%d" % t, "R%d" % t
+        if name[0] in "KHUS":
+            a, b, e = int(name[1]), int(name[2]), name[3:]
+            h, o = a // 2, 32 * (a % 2)
+            n = 32 * (b - a)
+            if name[0] == "K":
+                if t == 0:
+                    cp(A("G", 512 * a, 512 * b), IX(A("TK", 0, 4096), A("p16", 32 * a, 32 * b)), e)
                 else:
-                    mm(A("pV%d" % k), half)
-                    ts(A(tf, 8192 + c, 8704 + c), A("pV%d" % k), C23, ALU.add, C23 - 255.0, ALU.subtract)
-            ts(L("SP", h), L("pA", h, 4), col(3), ALU.add, col(2), ALU.is_ge)
-            for k in range(4):
-                mm(L("pZ", h, k, 4), [(cb("B8I"), L("SP", h))] if k < 2 else [(cb("nB4"), L("SP", h)), (Ib, cb("C20", 0, 64))])
-            mk = A("MK", 256 * h, 256 * h + 256)
-            ts(mk, A("pZ", 256 * h, 256 * h + 256), 11.0, ALU.is_ge)
-            mm(L("pA", h, 2), [(Ib, cb("C16", 0, 64)), (cb("I2k"), L("MK", h, 0, 4))])
-            ts(L("m16", h), L("pA", h, 2), col(1), ALU.add)
-            r = A("R", 192 * h, 192 * h + 128)
-            tt(pE(h, 256, 512), pE(h, 0, 256), mk, ALU.mult)
-            tt(A("R1", 128 * h, 128 * h + 128), pE(h, 256, 384), A3("PH", h, 0, 2), ALU.add)
-            tt(r, pE(h, 384, 512), A("R1", 128 * h, 128 * h + 128), ALU.add)
-            tt(L("R", h, 2, 3), A3("PH", h, 2), L("MK", h, 2, 4), ALU.not_equal)
-            if not last:
-                o = A("OUT%d" % t, 192 * h, 192 * h + 192)
-                cp(o, A("R", 192 * h, 192 * h + 192))
-                op("G", [lambda o=o, h=h: g.remote_dma(T["IN%d" % (t + 1)][:, h, :], o[0], T.sem["rs%d%d" % (t, h)],
-                                                       T.sem["ls%d%d" % (t, h)], pid, rid, rmask)],
-                   [], [o], 1000.0, "ls%d%d" % (t, h), neng, NOM["rlat"])
-            o = big(tfn, h, 2048)
-            halves(flip, tfn, 2048, A(tf, 6144 + 1024 * h, 9216 + 1024 * h), "m16", h, ENG["m"][t])
-            halves(cp, tkn, 2048, A(tk, kv + 1024 * h, kv + 3072 + 1024 * h), "m16", h, ENG["k"][t])
-            if not last:
-                flip(big(tfn, h, 6144), o)
-                continue
-            dma(X(T.yx[:, 2048 + 1024 * h:3072 + 1024 * h]), o, "ox%d" % h, 256)
-            ts(pE(h, 0, 128), r, 4096.0, ALU.is_ge, -4095.5, ALU.mult)
-            tt(A("EH", 128 * h, 128 * h + 128), pE(h, 0, 128), r, ALU.add)
+                    cp(A("G", 512 * a, 512 * b), IX(A("TK", 2048, 10240), A("X16", 128 * h + o, 128 * h + o + n)), e)
+            elif name[0] == "H":
+                cp(A("FW", 512 * a, 512 * b), IX(A(tf, 0, 8192), A("X16", 128 * h + 64 + o, 128 * h + 64 + o + n)), e)
+            elif name[0] == "U":
+                tt(A("D", 512 * a, 512 * b), IX(A(tf, 0, 8192), A("u16", 32 * a, 32 * b)), A("FW", 512 * a, 512 * b), ALU.subtract)
+            else:
+                flip(A(tfn, 2048 + 512 * a, 2048 + 512 * b), IX(A(tf, 6144 + 1024 * h, 9216 + 1024 * h), A("m16", 32 * a, 32 * b)), e)
+            return
+        e = name[-1] if name[-1] in "VS" else ""
+        kind = name.rstrip("VS")
+        h = int(kind[-1]) if kind[-1].isdigit() else 0
+        kind = kind.rstrip("0123")
+        Ib, nIb = cb("Ib"), cb("nIb")
+        if kind == "out":
+            return outputs_of_the_drawn(h) if t == 1 else None
+        if kind in ("av", "aw", "af", "ad", "ac", "ev"):
+            c, bank = 512 * h, A("pV%d" % (h % 2))
+            o = A(tf, 8192 + c, 8704 + c)
+            terms = [(A("CH", 0, 128), A("FW", c, c + 512)), (A("CH", 128, 256), A("D", c, c + 512)), (cb("CC", p1=32), A("ONE", 0, 512, 1, 0, 32))]
+            if kind in ("av", "aw"):
+                mm(bank, terms[:3 if kind == "av" else 2])
+            elif kind != "ev":
+                k = "fdc".index(kind[1])
+                mm(bank, terms[k:k + 1], k == 0, k == 2 or e == "V")
+            elif e == "S":
+                act(o, bank, 1.0, 255.0 - C23)
+            else:
+                ts(o, bank, C23, ALU.add, C23 - 255.0, ALU.subtract)
+            return
+        pK, pH, tK, tH, tF = L("PC", h, 0, 2), L("PC", h, 1, 2), L("TN", h, 0, 3), L("TN", h, 1, 3), L("TN", h, 2, 3)
+        less = [(nIb, L("PC", h, 0, 2, 2)), (Ib, L("TN", h, 0, 3, 2))]
+        ngo, opn = L("MK", h, 0, 2), L("MK", h, 1, 2)
+        pk, np_ = (None, [("pK", 0, 1)]), 256 // NT
+        ks = (T["KS%d" % h][0:np_, :, :], [("KS%d" % h, 0, 1)])
+        py, ys = (None, [("pY", 0, 1)]), (T.YS[0:64, :, 32 * h:32 * h + 32], [("YS", h, h + 1)])
+        if kind == "x":
+            ts(L("X16", h, 0, 2, 2), L(inb, h, 0, 3, 2), 2048.0, ALU.add)
+        elif kind == "tn":
+            if e == "S":
+                act(L("TR", h, 0, 3, 3), L(inb, h, 0, 3, 3), 1.0, 786432.5)
+                act(L("TN", h, 0, 3, 3), L("TR", h, 0, 3, 3), -1.0, 786432.0)
+            else:
+                ts(L("TN", h, 0, 3, 3), L(inb, h, 0, 3, 3), 2048.0, ALU.is_ge, -4096.0, ALU.mult)
+        elif kind == "pc":
+            tt(L("PC", h, 0, 2, 2), L(inb, h, 0, 3, 2), L("TN", h, 0, 3, 2), ALU.add)
+        elif kind == "up":
+            rows2list(L("pZ", h, 4), 0, "G", 1024 * h, True, True)
+        elif kind == "u":
+            ts(L("u16", h), L("pZ", h, 4), 0.5, ALU.mult, 2048.0, ALU.add)
+        elif kind == "uf":
+            cp(L("UF", h), L("pZ", h, 4), e)
+        elif kind == "a":
+            rows2list(pL(h, 0), 1, "G", 1024 * h, False, False)
+        elif kind == "prc":
+            mm(pC(0, 2), [(nIb, Zc(h, 0, 128)), (nIb, Zc(h, 128, 256))], True, False)
+            acc(pC(1), [(cb("I2"), pH), (cb("I2"), tH), (Ib, A("CT", 0, 64))])
+            acc(pC(0), [(cf("If"), L("UF", h))])
+        elif kind == "pra":
+            mm(pL(h, 0, 2), less, True, False, True)
+            acc(pL(h, 1), [(Ib, L("CM", h))])
+        elif kind == "prb":
+            if last:
+                acc(pL(h, 4, 3), [(cb("I2"), L("TN", h, 0, 3, 3))])
+            else:
+                acc(pL(h, 4), [(cb("IDn"), pH), (cb("IDn"), tH)])
+                acc(pL(h, 5), [(cb("UpI"), pK), (cb("UpI"), tK)])
+                wipe(pL(h, 4), tF); wipe(pL(h, 5), tF)
+                acc(pL(h, 4, 2), less)
+                acc(pL(h, 4), [(cb("Dn"), pH), (cb("Dn"), tH)])
+                acc(pL(h, 5), [(Ib, pK), (Ib, tK)])
+                acc(pL(h, 6), [(cb("I2"), tF)])
+            acc(pL(h, 4, 3), [(Ib, A("CT", 64, 256))])
+        elif kind == "nr":
+            ts(A("NR", 1024 * h, 1024 * h + 1024), A("D", 1024 * h, 1024 * h + 1024), C28, ALU.add, C28, ALU.is_equal)
+        elif kind == "cnt":
+            rows2list(L("pA", h), 2, "NR", 1024 * h, True, True)
+        elif kind == "sp":
+            ts(L("SP", h), L("pA", h), col(3), ALU.add, col(2), ALU.is_ge)
+        elif kind == "pz":
+            mm(L("pZ", h, 0, 2), [(cb("B8I"), L("SP", h))])
+            mm(L("pZ", h, 1, 2), [(cb("nB4"), L("SP", h)), (Ib, cb("C20", 0, 64))])
+        elif kind == "mk":
+            ts(L("MK", h, 0, 2, 2), L("pZ", h, 0, 2, 2), 11.0, ALU.is_lt, 4096.0, ALU.mult)
+        elif kind == "pk":
+            mm(L(PK, h, 6 if PK == "pZ" else 2), [(Ib, cb("C16", 0, 64)), (cb("nhI"), ngo)])
+        elif kind == "m":
+            ts(L("m16", h), L(PK, h, 6 if PK == "pZ" else 2), col(1), ALU.add)
+        elif kind == "kw":
+            wipe(pC(0), ngo); wipe(pC(1), ngo)
+            acc(pC(0, 2), [(Ib, Zc(h, 0, 128)), (Ib, Zc(h, 128, 256))], True)
+        elif kind == "hi":
+            cp(Zc(h, 0, 128), pC(0, 2), e)
+        elif kind == "lo":
+            tt(Zc(h, 128, 256), pC(0, 2), Zc(h, 0, 128), ALU.subtract)
+        elif kind == "tr":
+            op("P", [lambda cl=cl: g.tensor.transpose(T.pK[0:np_, :, 16 * cl:16 * cl + 16], T.Z[:, h, cl:256:NT], Ib[0])
+                     for cl in range(NT)], [pk], [Zc(h, 0, 256), Ib])
+        elif kind == "ks":
+            cp(ks, (T.pK[0:np_, :, 0:16 * NT], pk[1]), e or "V")
+        elif kind == "kd":
+            kid_rows(t, h, 0, "Y")
+        elif kind == "kt":
+            kid_rows(t, h, 1, e or "Y")
+        elif kind == "lw":
             for k in range(2):
-                tt(L("FE", h, k, 2), L("EH", h, k, 2), A3("PH", h, 2), ALU.mult)
-            for b in range(2):
-                mm(A("pE%d" % h, 128 + b, 256, 2), [(cf("a%d" % b), L("EH", h, 0, 2)), (cf("b%d" % b), L("EH", h, 1, 2)),
-                                                    (cf("c%d" % b), L("FE", h, 0, 2)), (cf("d%d" % b), L("FE", h, 1, 2))])
-            for b in range(2):
-                mm(A("pE%d" % h, 256 + b, 384, 2, 0, 8), [(cf("FT", 8 * b, 8 * b + 8), L("R", h, 2, 3))])
-            cp(A("YB", 128 * h, 128 * h + 128), pE(h, 128, 256))
-            dma(X(T.yb[:, 128 * h:128 * h + 128]), A("YB", 128 * h, 128 * h + 128), "ob%d" % h, 64)
-            cp(A("YF", 128 * h, 128 * h + 128, 1, 0, 8), A("pE%d" % h, 256, 384, 1, 0, 8))
-            c = 2048 + 1024 * h
-            py = A("pX", 128 * h, 128 * h + 128)
-            mm(py, [(Wm(3, 7 - bl, 135 - bl), A(tkn, c + 128 * bl, c + 128 * bl + 128)) for bl in range(8)], lock=True)
-            ts(A("S0", 128 * h, 128 * h + 128), py, 8192.0, ALU.is_ge, -8191.0, ALU.mult)
-            tt(A("YS", 128 * h, 128 * h + 128), py, A("S0", 128 * h, 128 * h + 128), ALU.add)
-            dma(X(T.y0[:, c:c + 1024]), A("YS", 128 * h, 128 * h + 128, 1, 0, 64), "oy%d" % h, 32)
-            dma(X(T.y1[:, c:c + 1024]), A("YS", 128 * h, 128 * h + 128, 1, 64, 128), "oy%d" % h, 32, "S")
-        if last:
-            dma(X(T.yf[:]), A("YF", 0, 256, 1, 0, 8), "of", 8)
-        else:
-            mm(A("pA", 384, 448), [(cb("EI8"), L("MK", h, 2, 4)) for h in range(2)])
+                wipe(pL(h, k), ngo)
+            for k in range(3):
+                wipe(pL(h, 4 + k), opn, k == 2)
+        elif kind == "r":
+            r = L(rb, h, 0, 3, 3)
+            tt(r, pL(h, 4, 3), L(inb, h, 0, 3, 3), ALU.add)
+            tt(L(rb, h, 0, 3, 2), pL(h, 0, 2), L(rb, h, 0, 3, 2), ALU.add)
+            if not last:
+                op("G", [lambda: g.remote_dma(T["IN%d" % (t + 1)][:, 192 * h:192 * h + 192], r[0], T.sem["rs%d%d" % (t, h)],
+                                              T.sem["ls%d%d" % (t, h)], pid, rid, rmask)], [], [r], "ls%d%d" % (t, h), neng)
+        elif kind == "flip":
+            flip(A(tfn, 6144 + 1024 * h, 7168 + 1024 * h), A(tfn, 2048 + 1024 * h, 3072 + 1024 * h))
+        elif kind == "par":
+            mm(A("pA", 384, 448), [(cb("EI8"), L("MK", hh, 1, 2)) for hh in range(2)])
+        elif kind == "thr":
             act(A("JK"), A("pA", 384, 448), bias=1.0 / 64, acc=col(3))
             act(col(4), col(3), 0.49995, C23)
             act(col(2), col(4), 2.0, 10.0 - 2 * C23)
+        elif kind == "yx":
+            dma(X(T.yx[:, 2048 + 1024 * h:3072 + 1024 * h]), A(tfn, 2048 + 1024 * h, 3072 + 1024 * h), "ox%d" % h)
+        elif kind == "yt":
+            ts(L("YT", h, 0, 2), pC(0), 4096.0, ALU.is_ge, -8191.0, ALU.mult)
+            ts(L("YT", h, 1, 2), pC(1), 4096.0, ALU.is_ge, -8193.0, ALU.mult)
+            tt(L("YK", h, 0, 2, 2), pC(0, 2), L("YT", h, 0, 2, 2), ALU.add)
+        elif kind == "ytr":
+            op("P", [lambda cl=cl: g.tensor.transpose(T.pY[0:64, :, 32 * h + 16 * cl:32 * h + 16 * cl + 16],
+                                                      T.YK[:, 128 * h + cl:128 * h + 128:2], cf("If")[0])
+                     for cl in range(2)], [py], [L("YK", h, 0, 2, 2), cf("If")])
+        elif kind == "ys":
+            act(ys, (T.pY[0:64, :, 32 * h:32 * h + 32], py[1]), 1.0, col(7, 0, 64))
+        elif kind == "yk":
+            for gg in range(8):
+                dma(X(T.y0[gg, 2048 + 1024 * h:3072 + 1024 * h]), (T.YS[0:32, gg, 32 * h:32 * h + 32], ys[1]), "oy%d" % h)
+        elif kind == "yq":
+            for gg in range(8):
+                dma(X(T.y1[gg, 2048 + 1024 * h:3072 + 1024 * h]), (T.YS[32:64, gg, 32 * h:32 * h + 32], ys[1]), "oy%d" % h, e or "Y")
+        elif kind == "eh":
+            r = L(rb, h, 0, 3, 2)
+            ts(pL(h, 0, 2), r, 2048.0, ALU.is_ge, -4095.5, ALU.mult)
+            tt(L("EH", h, 0, 2, 2), pL(h, 0, 2), r, ALU.add)
+            for k in range(2):
+                tt(L("FE", h, k, 2), L("EH", h, k, 2), L(inb, h, 2, 3), ALU.mult)
+        elif kind == "ybp":
+            bank = "pL%d" % h
+            for b in range(2):
+                mm(A(bank, 256 + b, 384, 2), [(cf("a%d" % b), L("EH", h, 0, 2)), (cf("b%d" % b), L("EH", h, 1, 2)),
+                                              (cf("c%d" % b), L("FE", h, 0, 2)), (cf("d%d" % b), L("FE", h, 1, 2))])
+            for b in range(2):
+                mm(A(bank, 384 + b, 512, 2, 0, 8), [(cf("FT", 8 * b, 8 * b + 8), L(rb, h, 2, 3))])
+        elif kind == "yb":
+            bank = "pL%d" % h
+            ts(A("YB", 128 * h, 128 * h + 128), A(bank, 256, 384), 4096.0, ALU.add)
+            dma(X(T.yb[:, 128 * h:128 * h + 128]), A("YB", 128 * h, 128 * h + 128), "ob%d" % h)
+            cp(A("YF", 128 * h, 128 * h + 128, 1, 0, 8), A(bank, 384, 512, 1, 0, 8))
+            if h == 1:
+                dma(X(T.yf[:]), A("YF", 0, 256, 1, 0, 8), "of")
+        else:
+            setup(kind, h, e)
 
     for t in range(RO):
-        visit(t)
-    emit(g, T, order(ops))
+        for name in ORDER[t].split():
+            tag[0] = (name, t)
+            step(name, t)
+    emit(g, T, [o for o in ops if o["fns"] or o["e"] == "X"])
 
 
 def meets(a, b):
     return a[1] < b[2] and b[1] < a[2] and (len(a) < 4 or len(b) < 4 or a[3] == b[3])
-
-
-def order(ops):
-    pred = [set() for _ in ops]
-    hist = {}
-    for i, o in enumerate(ops):
-        for kind in ("r", "w"):
-            for r in o[kind]:
-                for (r2, kind2, j) in hist.get(r[0], []):
-                    if meets(r, r2) and "w" in (kind, kind2) and not (o["sem"] and o["sem"] == ops[j]["sem"]):
-                        pred[i].add(j)
-        for kind in ("r", "w"):
-            for r in o[kind]:
-                hist.setdefault(r[0], []).append((r, kind, i))
-    seen = set()
-    assert sorted(ORDER) == list(range(len(ops)))
-    for i in ORDER:
-        assert pred[i] <= seen
-        seen.add(i)
-    return [ops[i] for i in ORDER]
 
 
 def emit(g, T, ops):

@@ -2,67 +2,53 @@ from concourse.mybir import AluOpType as ALU, ActivationFunctionType as ACT
 
 F, B, I, U, H16 = "float32", "bfloat16", "int32", "uint16", "float16"
 RO = 4
-PK = "pZ"
 NT = 4
 MF = ["If", "U16", "E0", "E1", "O0", "O1", "a0", "a1", "b0", "b1", "c0", "c1", "d0", "d1", "FT"]
 MB = ["Ib", "nIb", "I2", "nhI", "Kp", "Kn", "Dn", "IDn", "UpI", "B8I", "nB4", "EI8", "CC",
       "GX0", "GX1", "GXp", "GXn", "C16", "C20", "C3"]
 SCRATCH = {
-    "TF0": ("sbuf", [128, 10240], B), "TF1": ("sbuf", [128, 10240], B), "TK": ("sbuf", [128, 10240], B),
+    "TF0": ("sbuf", [128, 10240], B), "TF1": ("sbuf", [128, 10240], B), "TK": ("sbuf", [128, 8192], B),
     "G": ("sbuf", [128, 2048], B), "FW": ("sbuf", [128, 2048], B), "D": ("sbuf", [128, 2048], B), "NR": ("sbuf", [128, 2048], B),
-    "IN0": ("sbuf", [128, 384], F), "IN1": ("sbuf", [128, 384], F), "IN2": ("sbuf", [128, 384], F), "IN3": ("sbuf", [128, 384], F),
-    "R0": ("sbuf", [128, 384], F), "R1": ("sbuf", [128, 384], F), "R2": ("sbuf", [128, 384], F), "R3": ("sbuf", [128, 384], F),
-    "TR": ("sbuf", [128, 384], B), "UF": ("sbuf", [128, 128], F), "X16": ("sbuf", [128, 256], U), "TN": ("sbuf", [128, 384], B), "PC": ("sbuf", [128, 256], H16),
-    "Z": ("sbuf", [128, 2, 256], B), "SP": ("sbuf", [128, 128], B), "MK": ("sbuf", [128, 256], B),
+    "IN0": ("sbuf", [128, 2, 3, 64], F), "IN1": ("sbuf", [128, 2, 3, 64], F), "IN2": ("sbuf", [128, 2, 3, 64], F), "IN3": ("sbuf", [128, 2, 3, 64], F),
+    "R0": ("sbuf", [128, 2, 3, 64], F), "R1": ("sbuf", [128, 2, 3, 64], F), "R2": ("sbuf", [128, 2, 3, 64], F), "R3": ("sbuf", [128, 2, 3, 64], F),
+    "TR": ("sbuf", [128, 2, 3, 64], B), "TN": ("sbuf", [128, 2, 3, 64], B), "PC": ("sbuf", [128, 2, 2, 64], H16),
+    "X16": ("sbuf", [128, 2, 2, 64], U), "MK": ("sbuf", [128, 2, 2, 64], B), "UF": ("sbuf", [128, 128], F),
+    "Z": ("sbuf", [128, 2, 256], B), "SP": ("sbuf", [128, 128], B),
     "p16": ("sbuf", [128, 128], U), "u16": ("sbuf", [128, 128], U), "m16": ("sbuf", [128, 128], U), "TT": ("sbuf", [128, 128], B),
     "KS0": ("sbuf", [128, 8, 16 * NT], B), "KS1": ("sbuf", [128, 8, 16 * NT], B),
     "EI": ("sbuf", [128, 512], I), "SI": ("sbuf", [128, 512], I), "FI": ("sbuf", [128, 256], I),
     "P0": ("sbuf", [128, 256], F), "KP": ("sbuf", [128, 512], B), "FF": ("sbuf", [128, 512], B),
     "RR": ("sbuf", [128, 256], F), "KF": ("sbuf", [128, 256], F), "IO2": ("sbuf", [128, 128], F),
     "CF": ("sbuf", [128, 128 * len(MF)], F), "CB": ("sbuf", [128, 128 * len(MB)], B), "CH": ("sbuf", [128, 256], H16),
-    "CM": ("sbuf", [128, 128], H16), "CT": ("sbuf", [128, 256], B), "W": ("sbuf", [128, 4 * 144], B),
+    "CM": ("sbuf", [128, 128], H16), "CT": ("sbuf", [128, 512], B), "W": ("sbuf", [128, 4 * 144], B),
     "ZF": ("sbuf", [128, 128], F), "ZB": ("sbuf", [128, 144], B), "ONE": ("sbuf", [128, 512], B),
     "COL": ("sbuf", [128, 40], F), "COI": ("sbuf", [128, 16], I), "JK": ("sbuf", [128, 64], F),
     "EH": ("sbuf", [128, 256], F), "FE": ("sbuf", [128, 256], F), "YB": ("sbuf", [128, 256], F), "YF": ("sbuf", [128, 256], F),
     "YT": ("sbuf", [128, 256], F), "YK": ("sbuf", [128, 256], F), "YS": ("sbuf", [128, 8, 64], F),
-    "pA": ("psum", [128, 512], F), "pZ": ("psum", [128, 512], F), "pL0": ("psum", [128, 512], F), "pL1": ("psum", [128, 512], F),
+    "pA": ("psum", [128, 512], F), "pZ": ("psum", [128, 512], F), "pL0": ("psum", [128, 2, 4, 64], F), "pL1": ("psum", [128, 2, 4, 64], F),
     "pV0": ("psum", [128, 512], F), "pV1": ("psum", [128, 512], F), "pK": ("psum", [128, 8, 128], B), "pY": ("psum", [128, 8, 64], F),
 }
-DSEM = ["dk", "db", "df", "dp", "dv", "kd", "dc0", "dc1", "dc2", "df1", "dn1", "dyx", "dy",
-        "ox0", "ox1", "ob0", "ob1", "oy0", "oy1", "of"] + ["kc%d%d" % (t, h) for t in range(3) for h in range(2)]
-SEMAPHORES = ["sV", "sS", "sP", "sG"] + DSEM + ["ls%d%d" % (t, h) for t in range(3) for h in range(2)] \
-    + ["rs%d%d" % (t, h) for t in range(3) for h in range(2)]
+DSEM = ["dk", "db", "df", "dp", "dv", "kd", "dc0", "dc1", "df1", "dn1", "dyx", "dy", "ox0", "ox1", "ob0", "ob1", "oy0", "oy1", "of"] \
+    + ["%s%d%d" % (k, t, h) for k in ("kc", "ku") for t in range(3) for h in range(2)]
+SEMAPHORES = ["sV", "sS", "sP", "sG"] + DSEM + ["%s%d%d" % (k, t, h) for k in ("ls", "rs") for t in range(3) for h in range(2)]
 C23 = 12582912.0
 C28 = 402653184.0
 BIG = 1.5 * 2.0 ** 40
 
-FIRST = """load zero tka cols ga sa tkb ba rot ka rr kb kc kdma ff eo0 in0 eo1 in1 fa0 x0 pc0 tt0 kp0 kx0 fa1 fw gb x1 pc1 tt1 kp1 kx1
- K01V K12S up0 u0 H02S K23V K34V op0 gc oh0S up1 u1 va ol0 op1 gd H24S oh1S ol1 vb bg
- U01 U12 a0 nr0 cnt0 prc0 pra0 U23 sp0 pz0 mk0 av0 ev0S av1 ev1S a1 U34 pk0 m0 S02S kw0 hi0V lo0 nr1 cnt1 prc1 prb0 tr0 ks0 kd0
- lw0 r0 sp1 pz1 mk1 av2 ev2S av3 ev3S pra1 prb1 flip0 pk1 m1 S23S kw1 hi1V lo1 S34V tr1 ks1 kd1 flip1 lw1 r1 par x0+"""
-MIDDLE = """H02S x1 H23V K01V K12S pc0 H34S K23V up0 u0 K34S pc1 up1 u1
- U01 U12 a0 nr0 cnt0 prc0 pra0 U23 sp0 pz0 mk0 av0 ev0S av1 ev1S a1 U34 pk0 m0 S02S kw0 hi0V lo0 nr1 cnt1 prc1 prb0 tr0 ks0 kd0
- lw0 r0 sp1 pz1 mk1 av2 ev2S av3 ev3S pra1 prb1 flip0 pk1 m1 S23S kw1 hi1V lo1 S34V tr1 ks1 kd1 flip1 lw1 r1 par x0+"""
-LAST = """H02S x1 H23V K01V K12S pc0 H34S K23V up0 u0 K34S pc1 up1 u1
- U01 U12 a0 nr0 cnt0 prc0 pra0 U23 sp0 pz0 mk0 av0 ev0S av1 ev1S a1 U34 pk0 m0 S02S kw0 yt0 nr1 cnt1 prc1 prb0 ytr0 ys0 yk0
- lw0 r0 sp1 pz1 mk1 av2 ev2S av3 ev3S pra1 prb1 yx0 eh0 ybp0 yb0 pk1 m1 S23S kw1 yt1 S34V lw1 r1 yx1 ytr1 ys1 yk1 eh1 ybp1 yb1"""
-ORDER = """load zero tka sa ba cols ga tkb ka rot kb rr ff eo0 kc gb in0 eo1 fa1 in1 kdma fw pc0 tt0 tt1 x0 pc1 fa0 kp0 x1 gc kp1 kx0 K12S kx1 op1 K24S vb op0 va pra1 oh1V K01V pra0 up0 oh0V a1 bg ol0 u0 a0 H02S up1 U01 prc0 U12 nr0 ol1 gd prq0 H24S prb0 av0 cnt0 u1 U34 sp0 U23 av1 pz0 prb1 mk0 nr1 kw0 lw0 ev1S av3 cnt1 r0 out0+ prq1 hi0V sp1 prc1 pk0 lo0 tr0 pz1 ev0S mk1 ks0 ev3S av2 kw1 m0 lw1 ev2S S02S hi1V kt0 par lo1 pk1 kd0 m1 r1 tr1 ks1 S24S kd1 x0+ pc0+ kt1 flip1 flip0
-H12S pra0 x1 out2 thr- H01V K12S K01V prb0 pc1 K24S prq0 up0 pra1 prq1 u0 a0 U01 H24S out1 up1 a1 U12 nr0 u1 U23 U34 av0 cnt0 prc0 sp0 av1 nr1 pz0 prb1 mk0 kw0 lw0 cnt1 r0 sp1 pk0 hi0V pz1 lo0 m0 tr0 prc1 ev1S ev0S mk1 kw1 ks0 pk1 lw1 av2 S02S hi1V lo1 ev2S m1 tr1 flip0 ks1 x0+ av3 ev3S kt0 pc0+ kd0 pra0+ prb0+ kd1 kt1 r1 S24S flip1
-K01V K12S up0 x1 pc1 a0 H01V pra1 prq0 H12S u0 U01 par- U12 prb1 nr0 K24S av0 up1 H24S thr- u1 U23 cnt0 sp0 a1 ev0S pz0 av2 U34 mk0 prc0 nr1 kw0 ev2S lw0 cnt1 r0 pk0 sp1 av1 hi0V pz1 ev1S lo0 tr0 mk1 prc1 prq1 m0 ks0 kd0 S02S kt0 kw1 pk1 m1 lw1 r1 av3 hi1V lo1 tr1 ks1 kd1 flip0 x0+ ev3S S24S pc0+ kt1 flip1 pra0+ prq0+
-H12S H01V K12S x1 K24S K01V prb0 pc1 up0 u0 par- pra1 H24S prc0 a0 U01 U12 thr- up1 av0 nr0 u1 U23 av1 cnt0 prq1 ev0S prc1 sp0 pz0 mk0 av2 pk0 U34 ev1S m0 nr1 kw0 lw0 av3 cnt1 S02S yt0 sp1 ev2S r0 ytr0 pz1 prb1 a1 mk1 pk1 ev3S eh0 ys0 kw1 lw1 m1 yx0 S24S yt1 r1 ybp0 ytr1 eh1 ybp1 ys1 yq0 yk0 yx1 yq1S yk1 yb0 yb1""".split("\n")
-ORDER = """load zero sa tka cols ba ga ka rot kb tkb gc ff gb rr eo1 fa1 eo0 in1 kc fa0 pc1 in0 vb fw kdma pc0 tt0 tt1 kp0 kp1 x0 kx0 K12S K01V kx1 x1 pra1 pra0 H02S up0 va u0 U12 U01 op0 op1 a0 K24S gd nr0 uf0S up1 a1 u1 oh0V bg cnt0 oh1V H24S ol0 prb1 av0 U23 ev0S sp0 pz0 U34 mk0 nr1 prb0 ol1 lw0 uf1S pk0 cnt1 r0 prc0 m0 sp1 kw0 pz1 av1 hi0V lo0 mk1 tr0 prc1 ev1S kw1 ks0 lw1 av3 ev3S kd0 hi1V S02S lo1 r1 pk1 kt0 m1 tr1 ks1 x1+ kt1 par flip0 x0+ av2 out2+ ev2S pc0+ S24S flip1 kd1
-K01V pra0 pc1 prb0 H01V K12S up0 H12S pra1 uf0S a0 u0 prc0 prb1 K24S thr- H24S U01 U12 up1 nr0 out0 u1 av0 cnt0 sp0 U23 a1 ev0S pz0 av1 av2 out1 U34 mk0 uf1S nr1 lw0 kw0 pk0 cnt1 r0 hi0V sp1 lo0 m0 pz1 mk1 ev1S tr0 lw1 S02S prc1 par ev2S kw1 ks0 kt0 pk1 av3 r1 hi1V kd0 m1 x0+ lo1 flip0 tr1 ks1 thr pc0+ pra0+ ev3S x1+ kt1 S24S pc1+ flip1 kd1
-H01V H12S prb0 K01V K12S up0 u0 a0 U01 U12 K24S nr0 uf0S pra1 prc0 up1 a1 u1 av0 H24S cnt0 av1 U34 sp0 uf1S pz0 prb1 U23 mk0 nr1 lw0 ev0S av2 kw0 r0 cnt1 hi0V pk0 lo0 ev1S sp1 m0 tr0 ks0 pz1 mk1 kd0 ev2S prc1 lw1 par S02S kt0 kw1 pk1 thr r1 hi1V lo1 x0+ av3 ev3S pc0+ m1 S24S tr1 ks1 flip0 flip1 pra0+ kt1
-H12S kd1- H01V K12S prb0 x1 K24S K01V up0 pc1 pra1 u0 U12 a0 H24S prb1 up1 av1 U01 uf1S nr0 u1 U23 a1 cnt0 sp0 U34 uf0S prc0 pz0 av0 mk0 nr1 ev1S pk0 kw0 av3 cnt1 yt0 m0 ytr0 ev3S sp1 pz1 lw0 ev0S mk1 ys0 prc1 S02S kw1 r0 av2 yx0 yt1 ytr1 pk1 ev2S eh0 ys1 lw1 m1 r1 yq0 ybp0 yk1 yq1S eh1 S24S yk0 yb0 ybp1 yx1 yb1""".split("\n")
-FIRST = "load zero ga tka cols ba tkb ff ka kb kc rot rr eo0 sa va gb in0 eo1 kdma pc0 tt0 fa0 fw kp0 op0 in1 kx0 K12S K01V up0 x0 tt1 fa1 pc1 kp1 u0 kx1 gc op1 H02S vb bg pra0 a0 x1 gd oh0V U12 K24S up1 U01 nr0 oh1V ol1 u1 ol0 cnt0 sp0 H24S pz0 prb0 mk0 lw0 av0 U34 r0 uf0S uf1S U23 nr1 pk0 m0 prc0 av1 kw0 hi0V cnt1 ev1S lo0 tr0 sp1 pz1 mk1 prc1 ks0 kw1 ev0S pk1 par hi1V m1 kd0 aw2 kt0 lo1 tr1 ks1 kd1 pra1 prb1 kt1 S02S thr a1 lw1 flip0 ev2V S23S r1 x0+ aw3 ev3V S34S flip1 pc0+ pra0+ prb0+"
-MIDDLE = "K01V out0 x1 K12S H02S up0 u0 U12 out1 U01 a0 nr0 av1 K24S up1 pc1 u1 cnt0 sp0 pra1 H24S U23 uf0S pz0 mk0 av0 ev1S ev0S U34 uf1S lw0 r0 prb1 nr1 prc0 kw0 hi0V lo0 pk0 cnt1 sp1 tr0 m0 pz1 ks0 kt0 kd0 mk1 prc1 kw1 aw2 hi1V lo1 S02S pk1 m1 tr1 ks1 kd1 aw3 kt1 x0+ ev2V flip0 par thr a1 lw1 r1 S23S ev3V S34S pc0+ pra0+ prb0+ flip1 out2"
-LAST = "K12S K01V up0 H02S u0 x1 uf0S a0 prc0 U12 av1 U01 nr0 K24S up1 cnt0 pc1 H24S u1 sp0 pra1 pz0 mk0 av0 uf1S kw0 ev0S a1 U34 ev1S yt0 ytr0 ys0 U23 pk0 m0 lw0 S02S av2 ev2S nr1 cnt1 r0 av3 eh0 sp1 pz1 mk1 prc1 pk1 m1 kw1 ev3S yt1 S34V prb1 S23S lw1 yk0 yq0 r1 yx0 ytr1 ys1 yx1 eh1 yq1S ybp0 yk1 ybp1 yb0 yb1"
-FIRST = "zero load tka cols ba ka kb kc ga rot tkb kdma gb rr ff sa eo1 va gc eo0 fa1 in1 fa0 op0 in0 tt0 gd tn0V pc0 kp0 x0 tn1V fw kx0 K12S H02S op1 pc1 tt1 kp1 oh0V ol0 K01V kx1 x1 vb up0 u0 U01 U12 nr0 pra0 a0 oh1V K24S uf0S pra1 ol1 H24S af0 ad0 ac0 up1 bg u1 cnt0 sp0 prc0 pz0 mk0 ev0S prb0 lw0 r0 af1 ad1 ac1 pk0 U23 ev1S ar0+ kw0 hi0S prb1 af2 af3 U34 lo0 tr0 ad3 nr1 cnt1 sp1 ks0 kt0 uf1S prc1 pz1 m0 kd0 a1 mk1 lw1 r1 ac3 pk1 ev3S kw1 hi1V m1 ad2 ac2 ev2S par lo1 tr1 ks1 S23V S34S flip1 S02S flip0 kd1 kt1 tn0S+ thr x0+ pc0+ pra0+ prb0+"
-MIDDLE = "H12S H01V ar1 af0 K01V af1 K12S up0 x1 u0 tn1S a0 pc1 pra1 U01 K24S U12 up1 u1 ad0 nr0 H24S U34 uf1S ac0 ad1 ac1 uf0S cnt0 ev0S prb1 sp0 ev1S pz0 U23 prc0 mk0 lw0 pk0 nr1 kw0 r0 ar0+ cnt1 sp1 a1 hi0S pz1 lo0 mk1 tr0 ks0 kd0 af2 lw1 pk1 kt0 r1 par prc1 kw1 m0 hi1V lo1 tr1 af3 ad3 out2 m1 ks1 kd1 ad2 S02S flip0 ac3 ev3S kt1 out0 ac2 ev2S S23V S34S flip1 out1 tn0S+ pc0+ pra0+ x0+ prb0+ thr"
-LAST = "H12S ar1 K12S H01V K01V x1 tn1S pc1 up0 pra1 K24S u0 U01 a0 av0 up1 U12 nr0 cnt0 H24S u1 uf1S uf0S sp0 ev0S a1 U23 pz0 mk0 U34 av1 ev1S prc0 kw0 yt0 av2 ev2S lw0 nr1 ytr0 pk0 ys0 cnt1 r0 m0 prc1 sp1 pz1 yk0 yq0 S02S av3 mk1 kw1 pk1 eh0 prb1 yx0 lw1 yt1 ev3S ytr1 ys1 ybp0 yq1S yk1 m1 r1 eh1 ybp1 S23S S34V yb0 yx1 yb1"
-FIRST = "zero ga cols tka load ba rot ka kb kc gb fa0 fa1 tkb rr va ff eo1 sa kdma in1 x1 eo0 in0 tn0V op1 tt0 fw pc0 tn1V kp0 op0 pc1 kx0 x0 K01V oh1V tt1 oh0V K12S up0 ol1 ol0 kp1 gc vb H02S pra0 gd pra1 af1 kx1 K24S H24S a0 u0 U01 af0 U12 nr0 ad0 ad1 ac1 up1 u1 cnt0 ac0 sp0 prb0 uf0S prc0 U23 uf1S ev1S pz0 bg U34 a1 mk0 lw0 pk0 kw0 nr1 r0 m0 cnt1 af3 ad3 ac3 prb1 ar0+ sp1 pz1 hi0S lo0 mk1 ev0S S02S af2 tr0 ad2 ac2 ev2S ks0 kt0 lw1 r1 prc1 kw1 ev3S par hi1V thr lo1 pk1 kd0 m1 S34S S23V tr1 ks1 kd1 x0+ flip1 flip0 tn0S+ pc0+ pra0+ prb0+ kt1"
-MIDDLE = "ar1 x1 H12S af1 K12S tn1S H01V af0 K01V up0 pc1 u0 U01 K24S a0 H24S pra1 U12 nr0 up1 u1 ad1 U34 ad0 cnt0 uf0S ac0 sp0 U23 ac1 pz0 mk0 prc0 prb1 lw0 ev1S nr1 kw0 cnt1 a1 uf1S pk0 r0 ev0S sp1 pz1 hi0S lo0 out0 mk1 tr0 ks0 prc1 af2 m0 kw1 hi1V lo1 kd0 lw1 r1 S02S kt0 pk1 m1 af3 ad3 ac3 ev3S tr1 ad2 ac2 ev2S ks1 kt1 flip0 S23V S34S flip1 ar0+ x0+ par tn0S+ thr pc0+ out2 kd1 pra0+ prb0+ out1"
-LAST = "K12S ar1 x1 K01V up0 H01V K24S H12S u0 U01 a0 up1 U12 nr0 u1 av0 H24S av1 tn1S uf1S uf0S U34 ev1S cnt0 sp0 U23 pz0 mk0 nr1 prc0 kw0 pk0 cnt1 pc1 pra1 prb1 yt0 ytr0 sp1 pz1 mk1 ev0S lw0 a1 lw1 m0 ys0 r0 S02S yx0 eh0 pk1 m1 prc1 kw1 av3 av2 yq0 ev3S yk0 yt1 r1 eh1 ytr1 ybp0 ybp1 ev2S S23S S34V yx1 ys1 yk1 yq1S yb0 yb1"
+FIRST = """load io zero ga0 tka cols an eye ba0 tkb nf ba1 ka0 rot ga2 ff ka1 sa0 sa1 ka2 ka3 fa3S ga1 rr eg fa1V eo vc
+    tn2V tt kdma1 pc2 kp gb kdma0 fa0V gc kx fa2S inS
+    K12S x2 op1 K01V op0 up0 vb0 oh1V va dv vb1 vb2 pra0 H02S oh0V ol1 ol0 u0 U01 pra1 K24S a0 ge af0 U12 af1 nr0 ad0 gd
+    up1 ad1 u1 ac0 H24S cnt0 sp0 bg1 prb0 U34 pz0 mk0 ac1 ev0S af2 bg0 lw0 pk0 ev1S U23 uf0S r0 uf1S af3 s0 ad3V prc0
+    kw0 ad2 nr1 cnt1 ac2 m0 hi0V lo0 S02S ev2S tr0 sp1 pz1 mk1 a1 ar0+ prc1 ks0 pk1 par kw1 thr0 thr1 kd0 ev3V m1 hi1V
+    prb1 lo1 lw1 r1 S34S S23S s1 tr1 ks1 kd1 flip0 tq0+ x0+ tn0S+ pc0+ flip1 pra0+ thr2 ku0 kt1S prb0+"""
+MIDDLE = """ar1 H12S H01V K12S af0 K01V af1 x1 K24S up0 tn1V pc1 a0 u0 U01 pra1 H24S up1 ad0 U12 u1 nr0 U23 uf0S ac0 uf1S
+    ad1 ac1 cnt0 sp0 ev1S prc0 af3 pz0 U34 prb1 mk0 lw0 nr1 pk0 r0 s0 ar0+ kw0 cnt1 m0 ev0S hi0S lo0 ad3V af2 tr0 sp1
+    pz1 ad2 ev3V a1 mk1 par ks0 out0 ac2 lw1 r1 kd0 S02S prc1 s1 thr0 thr1 ku0 ev2S kw1 hi1V thr2 pk1 tq0+ m1 lo1 tr1
+    flip0 ks1 tn0S+ S23S kd1 pc0+ pra0+ S34S x0+ prb0+ flip1 kt1S out2 out1"""
+LAST = """K01V ar1 x1 tq1 K12S H01V up0 a0 H12S af1 K24S tn1S af0 u0 up1 U12 ad1 U01 pc1 ad0 H24S ac0 pra1 prb1 nr0 cnt0
+    u1 U23 ev0S uf1S sp0 ac1 a1 uf0S U34 pz0 mk0 nr1 prc0 af2 lw0 ev1S pk0 kw0 r0 m0 S02S yt0 cnt1 s0 sp1 yu0 eh0 ad2
+    af3 pz1 mk1 ac2 ei0 ej0 ytr0 lw1 ys0 pk1 ad3 r1 ac3 yx0 prc1 s1 eh1 ei1 m1 ej1 kw1 ev2S yt1 ybp0 yb0V yk0 yu1 ev3S
+    S24S ybp1 yq0 ytr1 yfp0 ys1 yc0 yb1V yc1 yx1 yfp1 yq1S yf0V yk1 yf1V yg"""
 ORDER = [FIRST, MIDDLE, MIDDLE, LAST]
 
 
@@ -82,8 +68,18 @@ def rank_program(g, core, T, topo):
             c0, c1 = 0, SCRATCH[n][1][-1]
         return (T[n][p0:p1, c0:c1] if st == 1 else T[n][p0:p1, c0:c1:st], [(n, c0, c1)])
 
+    def L(n, h, k=0, per=1, w=1):
+        return A(n, 64 * k, 64 * k + 128) if h == 2 else A(n, 64 * (per * h + k), 64 * (per * h + k + w))
+
+    def Q(n, h, k, w=1):
+        a, b = (slice(0, 2) if h == 2 else h), (k if w == 1 else slice(k, k + w))
+        return (T[n][:, a, b, :], [(n, 256 * j + 64 * k, 256 * j + 64 * (k + w)) for j in ((0, 1) if h == 2 else (h,))])
+
     def Zc(h, c0, c1):
         return (T.Z[:, h, c0:c1], [("Z", 256 * h + c0, 256 * h + c1)])
+
+    def pC(k, w=1):
+        return (T.pY[:, k:k + w, :], [("pY", 0, 64)])
 
     def IX(win, off):
         return (win[0].indirect(off[0]), win[1] + off[1])
@@ -149,9 +145,6 @@ def rank_program(g, core, T, topo):
     def wipe(o, mask, stop=False):
         acc(o, [(cb("Kp"), mask), (cb("Kn"), mask)], stop)
 
-    def pC(k, w=1):
-        return (T.pY[:, k:k + w, :], [("pY", 0, 64)])
-
     def dma(o, i, sem, q="Y"):
         op(q, [lambda: (g.sync if q == "Y" else g.scalar).dma_start(o[0], i[0])], [o], [i], sem, 16)
 
@@ -172,14 +165,18 @@ def rank_program(g, core, T, topo):
         for r in rows[1:]:
             sel(Wm(k, 15, 128, 16), Wm(k, 15, 128, 16), [[-16, 8]], -r, w)
 
-    def rows2list(o, k, n, c, start, stop, whole=False):
-        mm(o, [(Wm(k, 15 - q, 143 - q), A(n, c + q, c + 1024, 16)) for q in range(16)], start, stop, whole)
+    def weave(*makers):
+        chains = []
+        for make in makers:
+            n = len(ops)
+            make()
+            chains.append(ops[n:])
+            del ops[n:]
+        for k in range(max(len(c) for c in chains)):
+            ops.extend(c[k] for c in chains if k < len(c))
 
-    def L(n, h, k=0, per=1, w=1):
-        return A(n, 64 * (per * h + k), 64 * (per * h + k + w))
-
-    def pL(h, k, w=1):
-        return A("pL%d" % h, 64 * k, 64 * (k + w))
+    def rows2list(o, k, n, c, start=True, stop=True):
+        mm(o, [(Wm(k, 15 - q, 143 - q), A(n, c + q, c + 1024, 16)) for q in range(16)], start, stop)
 
     dg = [[-1, 128]]
     zb, z8, nf = A("ZB", 0, 128), A("ZB", 0, 128, 1, 0, 8), A("FF", 256, 512, 1, 0, 8)
@@ -187,119 +184,132 @@ def rank_program(g, core, T, topo):
     def setup(kind, h, e):
         if kind == "load":
             dma(A("EI", 256, 512), X(T.belts[:]), "db")
-            dma(A("FI", 0, 256, 1, 0, 8), X(T.flip[:]), "df", "S")
             dma(A("EI", 0, 256, 1, 0, 64), X(T.kid0[:]), "dk", "S")
             dma(A("EI", 0, 256, 1, 64, 128), X(T.kid1[:]), "dk")
+            dma(A("FI", 0, 256, 1, 0, 8), X(T.flip[:]), "df", "S")
             dma(A("TF0", 0, 2048), X(T.faces[:]), "dp")
         elif kind == "zero":
             ms(A("ZF"), 0.0); ms(A("ZB"), 0.0)
+        elif kind == "io":
             iota(A("IO2"), dg, 0, 1)
+        elif kind == "eye":
             ts(cf("If"), A("IO2"), 0.0, ALU.is_equal)
         elif kind == "tka":
             ms(A("TK", 0, 2048), 0.0)
         elif kind == "tkb":
-            act(A("TK", 2048, 4096), A("TK", 0, 2048))
+            act(A("TK", 4096, 6144), A("TK", 0, 2048))
         elif kind == "cols":
             ms(col(5, 0, 64), 8191.0); ms(col(5, 64, 128), -8193.0); ms(col(6, 0, 64), -4096.0); ms(col(6, 64, 128), 4096.0)
         elif kind == "ga":
-            sel(cf("U16"), A("ZF"), dg, -1, 1.0)
-            sel(cf("U16", 15, 128, 16), A("ZF", 0, 8), [[-16, 8]], 0, 1.0)
-            sel(cf("U16"), cf("U16"), dg, 0, -1.0)
-            sel(cb("GXp", p1=8), z8, [[-1, 8], [0, 16]], 0, BIG)
-            sel(cb("GXn", p1=8), z8, [[-1, 8], [0, 16]], 0, -BIG)
-            for m, o in (("E", 0), ("O", 1)):
+            if h == 0:
+                sel(cf("U16"), A("ZF"), dg, -1, 1.0)
+                sel(cb("GXp", p1=8), z8, [[-1, 8], [0, 16]], 0, BIG)
+                sel(cf("U16", 15, 128, 16), A("ZF", 0, 8), [[-16, 8]], 0, 1.0)
+                sel(cb("GXn", p1=8), z8, [[-1, 8], [0, 16]], 0, -BIG)
+                sel(cf("U16"), cf("U16"), dg, 0, -1.0)
+                return
+            for m, o in (("E", 0), ("O", 1)) if h == 1 else ():
                 for b in range(2):
                     sel(cf("%s%d" % (m, b)), A("ZF"), [[-16, 8], [300, 2], [-2, 8]], -300 * b - o, 0.5)
-            for b in range(2):
+            for b in range(2) if h == 2 else ():
                 sel(cb("GX%d" % b, p1=8), z8, [[-1, 8], [300, 2], [0, 8]], -300 * b, 4096.0)
         elif kind == "sa":
-            for n, s in (("Ib", 1.0), ("nIb", -1.0), ("nhI", -0.5), ("I2", 2.0), ("Kp", BIG / 4096), ("Kn", -BIG / 4096)):
+            for n, s in ((("Ib", 1.0), ("nIb", -1.0), ("nhI", -0.5)), (("I2", 2.0), ("Kp", BIG / 4096), ("Kn", -BIG / 4096)))[h]:
                 act(cb(n), cf("If"), s)
-            for o, c in ((cb("C3"), 397312.0), (cb("C20"), 20.0), (cb("EI8"), 0.125 / 4096), (cb("CC"), C23 / 32),
-                         (A("CT", 128, 256), 4096.0), (A("CT", 64, 128), 4096.0), (A("CT", 0, 64), 8192.0)):
-                act(o, A("ZB", 0, o[1][0][2] - o[1][0][1]), 1.0, c)
-        elif kind == "ba":
-            ts(A("SI", 256, 512), A("EI", 256, 512), 1, ALU.bitwise_and)
-            ts(A("pV1", 0, 256), A("SI", 256, 512), 8191.0, ALU.mult, -4096.0, ALU.add)
-            tt(A("P0"), A("pV1", 0, 256), A("EI", 256, 512), ALU.add)
+            for n, c in ((("C3", 395264.0),), (("C20", 20.0), ("EI8", 0.125 / 4096), ("CC", C23 / 32)))[h]:
+                act(cb(n), zb, 1.0, c)
+        elif kind == "an":
+            ts(A("SI"), A("EI"), 1, ALU.bitwise_and)
+        elif kind == "nf":
             ts(nf, A("FI", 0, 256, 1, 0, 8), 0.0, ALU.is_equal)
+        elif kind == "ba":
+            if h == 0:
+                ts(A("pV1", 0, 256), A("SI", 256, 512), 8191.0, ALU.mult, -4096.0, ALU.add)
+            else:
+                tt(A("P0"), A("pV1", 0, 256), A("EI", 256, 512), ALU.add)
         elif kind == "rot":
             mm(A("pZ", 0, 256), [(cf("U16"), A("P0")), (cb("GXp", p1=8), nf), (cb("GXn", p1=8), nf)])
         elif kind == "rr":
             tt(A("RR"), A("pZ", 0, 256), A("P0"), ALU.add)
         elif kind == "ka":
-            ts(A("SI", 0, 256), A("EI", 0, 256), 1, ALU.bitwise_and)
-            ts(A("pV0", 0, 256), A("SI", 0, 256), col(5), ALU.mult, col(6), ALU.add)
-        elif kind == "kb":
-            tt(A("pV0", 256, 512), A("pV0", 0, 256), A("EI", 0, 256), ALU.add)
-            cp(A("KP", 0, 256), A("pV0", 256, 512))
-        elif kind == "kc":
-            tt(A("KP", 256, 512), A("pV0", 256, 512), A("KP", 0, 256), ALU.subtract)
+            if h == 0:
+                ts(A("pV0", 0, 256), A("SI", 0, 256), col(5), ALU.mult, col(6), ALU.add)
+            elif h == 1:
+                tt(A("pV0", 256, 512), A("pV0", 0, 256), A("EI", 0, 256), ALU.add)
+            elif h == 2:
+                cp(A("KP", 0, 256), A("pV0", 256, 512))
+            else:
+                tt(A("KP", 256, 512), A("pV0", 256, 512), A("KP", 0, 256), ALU.subtract)
         elif kind == "kdma":
+            c = 4096 * h
             for r in range(4):
-                for turn in range(2):
-                    c = 2048 - 2048 * turn
-                    dma((T.TK[r + turn:128:16, c:c + 2048], [("TK", c, c + 2048)]),
-                        A("KP", 256 * (r // 2), 256 * (r // 2) + 256, 1, 64 * (r % 2), 64 * (r % 2) + 64), "kd")
+                dma((T.TK[4 * r + h:128:16, c:c + 2048], [("TK", c, c + 2048)]),
+                    A("KP", 256 * (r // 2), 256 * (r // 2) + 256, 1, 64 * (r % 2), 64 * (r % 2) + 64), "kd", e or "Y")
+        elif kind == "dv":
             dma(A("TF0", 2048, 4096), X(T.faces[:]), "dv")
         elif kind == "ff":
             act(A("FF", 0, 256, 1, 0, 8), nf, -1.0, 1.0)
         elif kind == "eo":
-            bank = "pL%d" % h
             for k, m in enumerate("EO"):
-                mm(A(bank, 64 * k, 64 * k + 64), [(cf("%s%d" % (m, b)), A("RR", 128 * h + b, 128 * h + 128, 2)) for b in range(2)])
-            mm(A(bank, 128, 192), [(cb("GX%d" % b, p1=8), A("FF", 128 * h + b, 128 * h + 128, 2, 0, 8)) for b in range(2)])
+                mm(Q("pL0", 2, k), [(cf("%s%d" % (m, b)), A("RR", b, 256, 2)) for b in range(2)])
+        elif kind == "eg":
+            mm(Q("pL0", 2, 2), [(cb("GX%d" % b, p1=8), A("FF", b, 256, 2, 0, 8)) for b in range(2)])
         elif kind == "in":
-            cp(A("IN0", 192 * h, 192 * h + 192), pL(h, 0, 3), "S")
+            cp(Q("IN0", 2, 0, 3), Q("pL0", 2, 0, 3), e)
         elif kind == "fa":
-            flip(A("TF0", 4096 + 1024 * h, 5120 + 1024 * h), A("TF0", 1024 * h, 1024 * h + 1024))
-        elif kind == "fw":
-            flip(A("TF0", 6144, 8192), A("TF0", 0, 2048), "S")
+            flip(A("TF0", 4096 + 1024 * h, 5120 + 1024 * h), A("TF0", 1024 * (h % 2), 1024 * (h % 2) + 1024), e)
         elif kind == "gb":
-            wrows(0, [1, 3], 1.0)
-            wrows(3, [0, 2], 1.0)
-            wrows(1, [0, 2, 4], 0.5)
+            weave(lambda: wrows(0, [4, 12, 1, 9], 1.0), lambda: wrows(1, [0, 8, 5, 13], 0.5), lambda: wrows(3, [0, 8], 1.0))
         elif kind == "gc":
             iota(Wm(2), [[0, 144]], 0, 0)
-            iota(Wm(2, 15, 128, 16), [[0, 8]], 1, 0)
-            sel(Wm(2, 15, 128, 16), Wm(2, 15, 128, 16), [[-16, 8]], 0, 0.0, ALU.is_ge)
-            sel(Wm(2, 15, 128, 16), Wm(2, 15, 128, 16), [[16, 8]], 15, 0.0, ALU.is_ge, -1)
             op("G", [lambda: g.iota(T.COI[:, 0:1], [[0, 1]], 0, 1)], [A("COI", 0, 1)], [])
+            iota(Wm(2, 15, 128, 16), [[0, 8]], 1, 0)
             iota(cb("C16"), [[16, 128]], 0, 0)
-            for n, c in (("nB4", -4), ("B8I", 1)):
-                iota(cb(n), [[0, 128]], c, 0)
-                sel(cb(n), cb(n), [[-8, 16], [0, 8]], 0, 0.0, ALU.is_ge)
-                sel(cb(n), cb(n), [[8, 16], [0, 8]], 7, 0.0, ALU.is_ge, -1)
+            sel(Wm(2, 15, 128, 16), Wm(2, 15, 128, 16), [[-16, 8]], 0, 0.0, ALU.is_ge)
+            iota(cb("nB4"), [[0, 128]], -4, 0)
+            sel(Wm(2, 15, 128, 16), Wm(2, 15, 128, 16), [[16, 8]], 15, 0.0, ALU.is_ge, -1)
+            iota(cb("B8I"), [[0, 128]], 1, 0)
+        elif kind == "ge":
+            for pat, base, cm in (([[-8, 16], [0, 8]], 0, 1), ([[8, 16], [0, 8]], 7, -1)):
+                for n in ("B8I", "nB4"):
+                    sel(cb(n), cb(n), pat, base, 0.0, ALU.is_ge, cm)
             sel(cb("B8I"), cb("B8I"), dg, 0, 9.0)
         elif kind == "gd":
-            for n, o, w, c in (("IDn", 1, -1.0, 0), ("Dn", 1, 1.0, 0), ("UpI", -1, 1.0, 7)):
+            def shift(n, o, w, c):
                 sel(cb(n), zb, dg, o, w)
                 sel(cb(n, c, 128, 8), A("ZB", 0, 16), [[-8, 16]], c - 7, w)
                 if n != "Dn":
                     sel(cb(n), cb(n), dg, 0, -w)
+            weave(lambda: shift("IDn", 1, -1.0, 0), lambda: shift("UpI", -1, 1.0, 7), lambda: shift("Dn", 1, 1.0, 0))
         elif kind == "va":
             ts(A("CH", 0, 128), cf("If"), 2.0 ** -10 - 1.0, ALU.mult)
             ts(A("CH", 128, 256), cf("If"), 2.0 ** -11 - 0.5, ALU.mult)
+        elif kind == "vc":
             ms(A("ONE", 0, 512, 1, 0, 32), 1.0); ms(col(2), 10.0); ms(col(3), 1.0)
+            ms(A("CT", 0, 64), 8192.0); ms(A("CT", 64, 256), 4096.0)
         elif kind == "vb":
-            ts(A("COI", 4, 5), A("COI", 0, 1), 15, ALU.bitwise_and)
-            ts(col(1), A("COI", 4, 5), 2048.0, ALU.add)
-            ts(A("CM"), cb("C16"), col(1), ALU.add, -2048.0, ALU.add)
+            if h == 0:
+                ts(A("COI", 4, 5), A("COI", 0, 1), 15, ALU.bitwise_and)
+            elif h == 1:
+                ts(col(1), A("COI", 4, 5), 2048.0, ALU.add)
+            else:
+                ts(A("CM"), cb("C16"), col(1), ALU.add, -2048.0, ALU.add)
         elif kind == "bg":
-            dma(A("TK", 4096, 6144), A("TK", 2048, 4096), "dc0")
-            dma(A("TK", 8192, 10240), A("TK", 0, 2048), "dc1")
-            dma(A("TK", 6144, 8192), A("TK", 0, 2048), "dc2")
-            dma(A("TF1", 4096, 6144), A("TF0", 4096, 6144), "dn1")
-            dma(A("TF1", 0, 2048), X(T.faces[:]), "df1")
+            if h == 0:
+                dma(A("TK", 2048, 4096), A("TK", 0, 2048), "dc0")
+                dma(A("TK", 6144, 8192), A("TK", 4096, 6144), "dc1")
+            else:
+                dma(A("TF1", 4096, 6144), A("TF0", 4096, 6144), "dn1")
+                dma(A("TF1", 0, 2048), X(T.faces[:]), "df1")
         elif kind == "tt":
-            ts(L("TT", h), L("IN0", h, 0, 3), 394240.5, ALU.add)
+            ts(A("TT"), Q("pL0", 2, 0), 394240.5, ALU.add)
         elif kind == "kp":
-            mm(L("pZ", h, 4), [(cb("Ib"), L("PC", h, 0, 2)), (cb("nhI"), L("TN", h, 0, 3)), (cb("nIb"), L("TT", h)), (cb("Ib"), cb("C3", 0, 64))])
+            mm(L("pZ", 2, 4), [(cb("Ib"), Q("PC", 2, 0)), (cb("nIb"), Q("TN", 2, 0)), (cb("nIb"), Q("TN", 2, 0)), (cb("nIb"), A("TT")), (cb("Ib"), cb("C3"))])
         elif kind == "kx":
-            cp(L("p16", h), L("pZ", h, 4))
+            cp(A("p16"), L("pZ", 2, 4))
         elif kind == "op":
             for k in range(2):
-                rows2list(A("pV%d" % h, 64 * k, 64 * k + 64), 3 - 3 * k, "TK", 2048 + 1024 * h, True, True)
+                rows2list(A("pV%d" % h, 64 * k, 64 * k + 64), 3 - 3 * k, "TK", 1024 * h)
         elif kind == "oh":
             cp(Zc(h, 0, 128), A("pV%d" % h, 0, 128), e)
         elif kind == "ol":
@@ -331,31 +341,26 @@ def rank_program(g, core, T, topo):
             sel(cf("FT", 8 * b, 8 * b + 8), A("ZF", 0, 8), [[-16, 8]], -8 * b, w / 2)
 
     def kid_rows(t, h, turn, q):
-        c = 4096 + 4096 * turn + 1024 * h
+        c = 2048 + 4096 * turn + 1024 * h
         for gg in range(8):
             p = 16 * gg + turn
-            dma((T.TK[p:p + 4, c:c + 1024], [("TK", c, c + 1024, gg)]), (T["KS%d" % h][0:256 // NT, gg, :], [("KS%d" % h, 0, 1)]),
+            dma((T.TK[p:p + 13:4, c:c + 1024], [("TK", c, c + 1024, gg)]), (T["KS%d" % h][0:256 // NT, gg, :], [("KS%d" % h, 0, 1)]),
                 "kc%d%d" % (t, h), q)
 
     def step(name, t):
-        if name[-1] in "+-":
-            name, t = name[:-1], t + (1 if name[-1] == "+" else -1)
-        if name[:2] == "ar":
-            k = int(name[2])
-            return op("X", [], [L("IN%d" % t, k, 0, 3, 3)], [], "rs%d%d" % (t - 1, k), neng) if t else None
+        if name[-1] == "+":
+            name, t = name[:-1], t + 1
         last = t == RO - 1
         tf, tfn, inb, rb = "TF%d" % (t % 2), "TF%d" % ((t + 1) % 2), "IN%d" % t, "R%d" % t
         if name[0] in "KHUS":
             a, b, e = int(name[1]), int(name[2]), name[3:]
-            h, o = a // 2, 32 * (a % 2)
-            n = 32 * (b - a)
+            h = a // 2
+            k = "KH".find(name[0])
+            x16 = (T.X16[:, h, max(k, 0), 32 * a - 64 * h:32 * b - 64 * h], Q("X16", h, max(k, 0))[1])
             if name[0] == "K":
-                if t == 0:
-                    cp(A("G", 512 * a, 512 * b), IX(A("TK", 0, 4096), A("p16", 32 * a, 32 * b)), e)
-                else:
-                    cp(A("G", 512 * a, 512 * b), IX(A("TK", 2048, 10240), A("X16", 128 * h + o, 128 * h + o + n)), e)
+                cp(A("G", 512 * a, 512 * b), IX(A("TK"), x16) if t else IX(A("TK", 0, 6144), A("p16", 32 * a, 32 * b)), e)
             elif name[0] == "H":
-                cp(A("FW", 512 * a, 512 * b), IX(A(tf, 0, 8192), A("X16", 128 * h + 64 + o, 128 * h + 64 + o + n)), e)
+                cp(A("FW", 512 * a, 512 * b), IX(A(tf, 0, 8192), x16), e)
             elif name[0] == "U":
                 tt(A("D", 512 * a, 512 * b), IX(A(tf, 0, 8192), A("u16", 32 * a, 32 * b)), A("FW", 512 * a, 512 * b), ALU.subtract)
             else:
@@ -366,80 +371,89 @@ def rank_program(g, core, T, topo):
         h = int(kind[-1]) if kind[-1].isdigit() else 0
         kind = kind.rstrip("0123")
         Ib, nIb = cb("Ib"), cb("nIb")
+        src = inb if t else "pL0"
+
+        def go(k, w=1):
+            return Q("pL%d" % h, 0, k, w)
+
+        def fx(k, w=1):
+            return Q("pL%d" % h, 1, k, w)
+
+        def less():
+            return [(nIb, Q("PC", h, 0, 2)), (Ib, Q("TN", h, 0, 2))]
+        pK, pH, tK, tH, tF = Q("PC", h % 3, 0), Q("PC", h % 3, 1), Q("TN", h % 3, 0), Q("TN", h % 3, 1), Q("TN", h % 3, 2)
+        ngo, opn = Q("MK", h % 3, 0), Q("MK", h % 3, 1)
+        pk, np_ = (None, [("pK", 0, 1)]), 256 // NT
+        py, ys = (None, [("pY", 0, 1)]), (T.YS[0:64, :, 32 * (h % 2):32 * (h % 2) + 32], [("YS", h, h + 1)])
         if kind == "out":
-            return outputs_of_the_drawn(h) if t == 1 else None
-        if kind in ("av", "aw", "af", "ad", "ac", "ev"):
+            if t == 1:
+                outputs_of_the_drawn(h)
+        elif kind in ("af", "ad", "ac", "ev"):
             c, bank = 512 * h, A("pV%d" % (h % 2))
             o = A(tf, 8192 + c, 8704 + c)
             terms = [(A("CH", 0, 128), A("FW", c, c + 512)), (A("CH", 128, 256), A("D", c, c + 512)), (cb("CC", p1=32), A("ONE", 0, 512, 1, 0, 32))]
-            if kind in ("av", "aw"):
-                mm(bank, terms[:3 if kind == "av" else 2])
-            elif kind != "ev":
+            if kind != "ev":
                 k = "fdc".index(kind[1])
                 mm(bank, terms[k:k + 1], k == 0, k == 2 or e == "V")
             elif e == "S":
                 act(o, bank, 1.0, 255.0 - C23)
             else:
                 ts(o, bank, C23, ALU.add, C23 - 255.0, ALU.subtract)
-            return
-        pK, pH, tK, tH, tF = L("PC", h, 0, 2), L("PC", h, 1, 2), L("TN", h, 0, 3), L("TN", h, 1, 3), L("TN", h, 2, 3)
-        less = [(nIb, L("PC", h, 0, 2, 2)), (Ib, L("TN", h, 0, 3, 2))]
-        ngo, opn = L("MK", h, 0, 2), L("MK", h, 1, 2)
-        pk, np_ = (None, [("pK", 0, 1)]), 256 // NT
-        ks = (T["KS%d" % h][0:np_, :, :], [("KS%d" % h, 0, 1)])
-        py, ys = (None, [("pY", 0, 1)]), (T.YS[0:64, :, 32 * h:32 * h + 32], [("YS", h, h + 1)])
-        if kind == "x":
-            ts(L("X16", h, 0, 2, 2), L(inb, h, 0, 3, 2), 2048.0, ALU.add)
+        elif kind == "ar":
+            op("X", [], [Q(inb, h, 0, 3)], [], "rs%d%d" % (t - 1, h), neng)
+        elif kind == "x":
+            ts(Q("X16", h, 0, 2), Q(src, h, 0, 2), 2048.0, ALU.add)
         elif kind == "tn":
             if e == "S":
-                act(L("TR", h, 0, 3, 3), L(inb, h, 0, 3, 3), 1.0, 786432.5)
-                act(L("TN", h, 0, 3, 3), L("TR", h, 0, 3, 3), -1.0, 786432.0)
+                act(Q("TN", h, 0, 3), Q("TR", h, 0, 3), -1.0, 786432.0)
             else:
-                ts(L("TN", h, 0, 3, 3), L(inb, h, 0, 3, 3), 2048.0, ALU.is_ge, -4096.0, ALU.mult)
+                ts(Q("TN", h, 0, 3), Q(src, h, 0, 3), 2048.0, ALU.is_ge, -4096.0, ALU.mult)
+        elif kind == "tq":
+            act(Q("TR", h, 0, 3), Q(src, h, 0, 3), 1.0, 786432.5)
         elif kind == "pc":
-            tt(L("PC", h, 0, 2, 2), L(inb, h, 0, 3, 2), L("TN", h, 0, 3, 2), ALU.add)
+            tt(Q("PC", h, 0, 2), Q(src, h, 0, 2), Q("TN", h, 0, 2), ALU.add)
         elif kind == "up":
-            rows2list(L("pZ", h, 4), 0, "G", 1024 * h, True, True)
+            rows2list(L("pZ", h, 4), 0, "G", 1024 * h)
         elif kind == "u":
             ts(L("u16", h), L("pZ", h, 4), 0.5, ALU.mult, 2048.0, ALU.add)
         elif kind == "uf":
             cp(L("UF", h), L("pZ", h, 4), e)
         elif kind == "a":
-            rows2list(pL(h, 0), 1, "G", 1024 * h, False, False)
+            rows2list(go(0), 1, "G", 1024 * h, False, False)
         elif kind == "prc":
             mm(pC(0, 2), [(nIb, Zc(h, 0, 128)), (nIb, Zc(h, 128, 256))], True, False)
             acc(pC(1), [(cb("I2"), pH), (cb("I2"), tH), (Ib, A("CT", 0, 64))])
             acc(pC(0), [(cf("If"), L("UF", h))])
         elif kind == "pra":
-            mm(pL(h, 0, 2), less, True, False, True)
-            acc(pL(h, 1), [(Ib, L("CM", h))])
+            mm(go(0, 2), less(), True, False, True)
+            acc(go(1), [(Ib, L("CM", h))])
         elif kind == "prb":
             if last:
-                acc(pL(h, 4, 3), [(cb("I2"), L("TN", h, 0, 3, 3))])
+                acc(fx(0, 3), [(cb("I2"), Q("TN", h, 0, 3))])
             else:
-                acc(pL(h, 4), [(cb("IDn"), pH), (cb("IDn"), tH)])
-                acc(pL(h, 5), [(cb("UpI"), pK), (cb("UpI"), tK)])
-                wipe(pL(h, 4), tF); wipe(pL(h, 5), tF)
-                acc(pL(h, 4, 2), less)
-                acc(pL(h, 4), [(cb("Dn"), pH), (cb("Dn"), tH)])
-                acc(pL(h, 5), [(Ib, pK), (Ib, tK)])
-                acc(pL(h, 6), [(cb("I2"), tF)])
-            acc(pL(h, 4, 3), [(Ib, A("CT", 64, 256))])
+                acc(fx(0), [(cb("IDn"), pH), (cb("IDn"), tH)])
+                acc(fx(1), [(cb("UpI"), pK), (cb("UpI"), tK)])
+                wipe(fx(0), tF); wipe(fx(1), tF)
+                acc(fx(0, 2), less())
+                acc(fx(0), [(cb("Dn"), pH), (cb("Dn"), tH)])
+                acc(fx(1), [(Ib, pK), (Ib, tK)])
+                acc(fx(2), [(cb("I2"), tF)])
+            acc(fx(0, 3), [(Ib, A("CT", 64, 256))])
         elif kind == "nr":
             ts(A("NR", 1024 * h, 1024 * h + 1024), A("D", 1024 * h, 1024 * h + 1024), C28, ALU.add, C28, ALU.is_equal)
         elif kind == "cnt":
-            rows2list(L("pA", h), 2, "NR", 1024 * h, True, True)
+            rows2list(L("pA", h), 2, "NR", 1024 * h)
         elif kind == "sp":
             ts(L("SP", h), L("pA", h), col(3), ALU.add, col(2), ALU.is_ge)
         elif kind == "pz":
             mm(L("pZ", h, 0, 2), [(cb("B8I"), L("SP", h))])
             mm(L("pZ", h, 1, 2), [(cb("nB4"), L("SP", h)), (Ib, cb("C20", 0, 64))])
         elif kind == "mk":
-            ts(L("MK", h, 0, 2, 2), L("pZ", h, 0, 2, 2), 11.0, ALU.is_lt, 4096.0, ALU.mult)
+            ts(Q("MK", h, 0, 2), L("pZ", h, 0, 2, 2), 11.0, ALU.is_lt, 4096.0, ALU.mult)
         elif kind == "pk":
-            mm(L(PK, h, 6 if PK == "pZ" else 2), [(Ib, cb("C16", 0, 64)), (cb("nhI"), ngo)])
+            mm(L("pZ", h, 6), [(Ib, cb("C16", 0, 64)), (cb("nhI"), ngo)])
         elif kind == "m":
-            ts(L("m16", h), L(PK, h, 6 if PK == "pZ" else 2), col(1), ALU.add)
+            ts(L("m16", h), L("pZ", h, 6), col(1), ALU.add)
         elif kind == "kw":
             wipe(pC(0), ngo); wipe(pC(1), ngo)
             acc(pC(0, 2), [(Ib, Zc(h, 0, 128)), (Ib, Zc(h, 128, 256))], True)
@@ -451,36 +465,45 @@ def rank_program(g, core, T, topo):
             op("P", [lambda cl=cl: g.tensor.transpose(T.pK[0:np_, :, 16 * cl:16 * cl + 16], T.Z[:, h, cl:256:NT], Ib[0])
                      for cl in range(NT)], [pk], [Zc(h, 0, 256), Ib])
         elif kind == "ks":
-            cp(ks, (T.pK[0:np_, :, 0:16 * NT], pk[1]), e or "V")
+            cp((T["KS%d" % h][0:np_, :, :], [("KS%d" % h, 0, 1)]), (T.pK[0:np_, :, 0:16 * NT], pk[1]), e or "V")
         elif kind == "kd":
             kid_rows(t, h, 0, "Y")
         elif kind == "kt":
             kid_rows(t, h, 1, e or "Y")
+        elif kind == "ku":
+            c = 2048 + 1024 * h
+            dma((T.TK[1:128:4, c + 4096:c + 5120], [("TK", c + 4096, c + 5120)]), (T.TK[0:128:4, c:c + 1024], [("TK", c, c + 1024)]),
+                "ku%d%d" % (t, h), e or "Y")
         elif kind == "lw":
             for k in range(2):
-                wipe(pL(h, k), ngo)
+                wipe(go(k), ngo)
             for k in range(3):
-                wipe(pL(h, 4 + k), opn, k == 2)
+                wipe(fx(k), opn, k == 2)
         elif kind == "r":
-            r = L(rb, h, 0, 3, 3)
-            tt(r, pL(h, 4, 3), L(inb, h, 0, 3, 3), ALU.add)
-            tt(L(rb, h, 0, 3, 2), pL(h, 0, 2), L(rb, h, 0, 3, 2), ALU.add)
+            tt(Q(rb, h, 0, 3), fx(0, 3), Q(inb, h, 0, 3), ALU.add)
+        elif kind == "s":
+            tt(Q(rb, h, 0, 2), go(0, 2), Q(rb, h, 0, 2), ALU.add)
             if not last:
-                op("G", [lambda: g.remote_dma(T["IN%d" % (t + 1)][:, 192 * h:192 * h + 192], r[0], T.sem["rs%d%d" % (t, h)],
+                r = Q(rb, h, 0, 3)
+                op("G", [lambda: g.remote_dma(Q("IN%d" % (t + 1), h, 0, 3)[0], r[0], T.sem["rs%d%d" % (t, h)],
                                               T.sem["ls%d%d" % (t, h)], pid, rid, rmask)], [], [r], "ls%d%d" % (t, h), neng)
         elif kind == "flip":
-            flip(A(tfn, 6144 + 1024 * h, 7168 + 1024 * h), A(tfn, 2048 + 1024 * h, 3072 + 1024 * h))
+            flip(A(tfn, 6144 + 1024 * h, 7168 + 1024 * h), A(tfn, 2048 + 1024 * h, 3072 + 1024 * h), e)
         elif kind == "par":
-            mm(A("pA", 384, 448), [(cb("EI8"), L("MK", hh, 1, 2)) for hh in range(2)])
+            mm(A("pA", 384, 448), [(cb("EI8"), Q("MK", hh, 1)) for hh in range(2)])
         elif kind == "thr":
-            act(A("JK"), A("pA", 384, 448), bias=1.0 / 64, acc=col(3))
-            act(col(4), col(3), 0.49995, C23)
-            act(col(2), col(4), 2.0, 10.0 - 2 * C23)
+            if h == 0:
+                act(A("JK"), A("pA", 384, 448), bias=1.0 / 64, acc=col(3))
+            elif h == 1:
+                act(col(4), col(3), 0.49995, C23)
+            else:
+                act(col(2), col(4), 2.0, 10.0 - 2 * C23)
         elif kind == "yx":
             dma(X(T.yx[:, 2048 + 1024 * h:3072 + 1024 * h]), A(tfn, 2048 + 1024 * h, 3072 + 1024 * h), "ox%d" % h)
         elif kind == "yt":
             ts(L("YT", h, 0, 2), pC(0), 4096.0, ALU.is_ge, -8191.0, ALU.mult)
             ts(L("YT", h, 1, 2), pC(1), 4096.0, ALU.is_ge, -8193.0, ALU.mult)
+        elif kind == "yu":
             tt(L("YK", h, 0, 2, 2), pC(0, 2), L("YT", h, 0, 2, 2), ALU.add)
         elif kind == "ytr":
             op("P", [lambda cl=cl: g.tensor.transpose(T.pY[0:64, :, 32 * h + 16 * cl:32 * h + 16 * cl + 16],
@@ -488,32 +511,38 @@ def rank_program(g, core, T, topo):
                      for cl in range(2)], [py], [L("YK", h, 0, 2, 2), cf("If")])
         elif kind == "ys":
             act(ys, (T.pY[0:64, :, 32 * h:32 * h + 32], py[1]), 1.0, col(7, 0, 64))
-        elif kind == "yk":
+        elif kind in ("yk", "yq"):
+            y, p = (T.y0, 0) if kind == "yk" else (T.y1, 32)
             for gg in range(8):
-                dma(X(T.y0[gg, 2048 + 1024 * h:3072 + 1024 * h]), (T.YS[0:32, gg, 32 * h:32 * h + 32], ys[1]), "oy%d" % h)
-        elif kind == "yq":
-            for gg in range(8):
-                dma(X(T.y1[gg, 2048 + 1024 * h:3072 + 1024 * h]), (T.YS[32:64, gg, 32 * h:32 * h + 32], ys[1]), "oy%d" % h, e or "Y")
+                dma(X(y[gg, 2048 + 1024 * h:3072 + 1024 * h]), (T.YS[p:p + 32, gg, 32 * h:32 * h + 32], ys[1]), "oy%d" % h, e or "Y")
         elif kind == "eh":
-            r = L(rb, h, 0, 3, 2)
-            ts(pL(h, 0, 2), r, 2048.0, ALU.is_ge, -4095.5, ALU.mult)
-            tt(L("EH", h, 0, 2, 2), pL(h, 0, 2), r, ALU.add)
+            ts(go(0, 2), Q(rb, h, 0, 2), 2048.0, ALU.is_ge, -4095.5, ALU.mult)
+        elif kind == "ei":
+            tt(L("EH", h, 0, 2, 2), go(0, 2), Q(rb, h, 0, 2), ALU.add)
+        elif kind == "ej":
             for k in range(2):
-                tt(L("FE", h, k, 2), L("EH", h, k, 2), L(inb, h, 2, 3), ALU.mult)
+                tt(L("FE", h, k, 2), L("EH", h, k, 2), Q(inb, h, 2), ALU.mult)
         elif kind == "ybp":
-            bank = "pL%d" % h
+            bank = T["pL%d" % h]
             for b in range(2):
-                mm(A(bank, 256 + b, 384, 2), [(cf("a%d" % b), L("EH", h, 0, 2)), (cf("b%d" % b), L("EH", h, 1, 2)),
-                                              (cf("c%d" % b), L("FE", h, 0, 2)), (cf("d%d" % b), L("FE", h, 1, 2))])
+                mm((bank[:, 0, 2:4, b:64:2], go(2, 2)[1]),
+                   [(cf("a%d" % b), L("EH", h, 0, 2)), (cf("b%d" % b), L("EH", h, 1, 2)),
+                    (cf("c%d" % b), L("FE", h, 0, 2)), (cf("d%d" % b), L("FE", h, 1, 2))])
+        elif kind == "yfp":
+            bank = T["pL%d" % h]
             for b in range(2):
-                mm(A(bank, 384 + b, 512, 2, 0, 8), [(cf("FT", 8 * b, 8 * b + 8), L(rb, h, 2, 3))])
+                mm((bank[0:8, 1, 2:4, b:64:2], fx(2, 2)[1]), [(cf("FT", 8 * b, 8 * b + 8), Q(rb, h, 2))])
         elif kind == "yb":
-            bank = "pL%d" % h
-            ts(A("YB", 128 * h, 128 * h + 128), A(bank, 256, 384), 4096.0, ALU.add)
-            dma(X(T.yb[:, 128 * h:128 * h + 128]), A("YB", 128 * h, 128 * h + 128), "ob%d" % h)
-            cp(A("YF", 128 * h, 128 * h + 128, 1, 0, 8), A(bank, 384, 512, 1, 0, 8))
-            if h == 1:
-                dma(X(T.yf[:]), A("YF", 0, 256, 1, 0, 8), "of")
+            if e == "S":
+                act(A("YB", 128 * h, 128 * h + 128), go(2, 2), 1.0, 4096.0)
+            else:
+                ts(A("YB", 128 * h, 128 * h + 128), go(2, 2), 4096.0, ALU.add)
+        elif kind == "yc":
+            dma(X(T.yb[:, 128 * h:128 * h + 128]), A("YB", 128 * h, 128 * h + 128), "ob%d" % h, e or "Y")
+        elif kind == "yf":
+            cp(A("YF", 128 * h, 128 * h + 128, 1, 0, 8), (T["pL%d" % h][0:8, 1, 2:4, :], fx(2, 2)[1]), e)
+        elif kind == "yg":
+            dma(X(T.yf[:]), A("YF", 0, 256, 1, 0, 8), "of", e or "Y")
         else:
             setup(kind, h, e)
 
@@ -521,7 +550,7 @@ def rank_program(g, core, T, topo):
         for name in ORDER[t].split():
             tag[0] = (name, t)
             step(name, t)
-    emit(g, T, [o for o in ops if o["fns"] or o["e"] == "X"])
+    emit(g, T, ops)
 
 
 def meets(a, b):

@@ -3,52 +3,75 @@ from concourse.mybir import AluOpType as ALU, ActivationFunctionType as ACT
 F, B, I, U, H16 = "float32", "bfloat16", "int32", "uint16", "float16"
 RO = 4
 NT = 4
-MF = ["If", "U16", "E0", "E1", "O0", "O1", "a0", "a1", "b0", "b1", "c0", "c1", "d0", "d1", "FT"]
-MB = ["Ib", "nIb", "I2", "nhI", "Kp", "Kn", "Dn", "IDn", "UpI", "B8I", "nB4", "EI8", "CC",
-      "GX0", "GX1", "GXp", "GXn", "C16", "C20", "C3"]
+MF = ["If"]
+MB = ["Ib", "nIb", "I2", "Ip", "I4k", "nhI", "Kp", "Kn", "Dn", "IDn", "UpI", "B8I", "nB4", "EI8", "CC", "C16", "C20",
+      "a0", "a1", "b0", "b1", "c0", "c1", "d0", "d1", "e0", "e1", "f0", "f1", "FT"]
+MY = ["E", "O", "OE", "SO", "GP", "GN"]
 SCRATCH = {
     "TF0": ("sbuf", [128, 10240], B), "TF1": ("sbuf", [128, 10240], B), "TK": ("sbuf", [128, 8192], B),
     "G": ("sbuf", [128, 2048], B), "FW": ("sbuf", [128, 2048], B), "D": ("sbuf", [128, 2048], B), "NR": ("sbuf", [128, 2048], B),
     "IN0": ("sbuf", [128, 2, 3, 64], F), "IN1": ("sbuf", [128, 2, 3, 64], F), "IN2": ("sbuf", [128, 2, 3, 64], F), "IN3": ("sbuf", [128, 2, 3, 64], F),
     "R0": ("sbuf", [128, 2, 3, 64], F), "R1": ("sbuf", [128, 2, 3, 64], F), "R2": ("sbuf", [128, 2, 3, 64], F), "R3": ("sbuf", [128, 2, 3, 64], F),
-    "TR": ("sbuf", [128, 2, 3, 64], B), "TN": ("sbuf", [128, 2, 3, 64], B), "PC": ("sbuf", [128, 2, 2, 64], H16),
-    "X16": ("sbuf", [128, 2, 2, 64], U), "MK": ("sbuf", [128, 2, 2, 64], B), "UF": ("sbuf", [128, 128], F),
+    "TN": ("sbuf", [128, 2, 3, 64], B), "TE": ("sbuf", [128, 2, 3, 64], B), "T2": ("sbuf", [128, 2, 2, 64], B), "PC": ("sbuf", [128, 2, 2, 64], H16),
+    "X16": ("sbuf", [128, 2, 2, 64], U), "MK": ("sbuf", [128, 2, 3, 64], B),
     "Z": ("sbuf", [128, 2, 256], B), "SP": ("sbuf", [128, 128], B),
-    "p16": ("sbuf", [128, 128], U), "u16": ("sbuf", [128, 128], U), "m16": ("sbuf", [128, 128], U), "TT": ("sbuf", [128, 128], B),
-    "KS0": ("sbuf", [128, 8, 16 * NT], B), "KS1": ("sbuf", [128, 8, 16 * NT], B),
-    "EI": ("sbuf", [128, 512], I), "SI": ("sbuf", [128, 512], I), "FI": ("sbuf", [128, 256], I),
-    "P0": ("sbuf", [128, 256], F), "KP": ("sbuf", [128, 512], B), "FF": ("sbuf", [128, 512], B),
-    "RR": ("sbuf", [128, 256], F), "KF": ("sbuf", [128, 256], F), "IO2": ("sbuf", [128, 128], F),
+    "u16": ("sbuf", [128, 128], U), "m16": ("sbuf", [128, 128], U),
+    "UQ": ("sbuf", [128, 512], B), "WB": ("sbuf", [128, 4096], B), "MG": ("sbuf", [128, 128], B), "ZR": ("sbuf", [128, 512], B), "KS": ("sbuf", [128, 2, 2, 4, 32], B),
+    "EI": ("sbuf", [128, 512], I), "SI": ("sbuf", [128, 1024], I), "FI": ("sbuf", [128, 256], I),
+    "p16": ("sbuf", [128, 128], U), "PS": ("sbuf", [128, 768], H16), "KP": ("sbuf", [128, 512], B), "FF": ("sbuf", [128, 512], B),
+    "KF": ("sbuf", [128, 256], F), "IO2": ("sbuf", [128, 128], F), "YM": ("sbuf", [128, 144 * len(MY)], B),
     "CF": ("sbuf", [128, 128 * len(MF)], F), "CB": ("sbuf", [128, 128 * len(MB)], B), "CH": ("sbuf", [128, 256], H16),
-    "CM": ("sbuf", [128, 128], H16), "CT": ("sbuf", [128, 512], B), "W": ("sbuf", [128, 4 * 144], B),
-    "ZF": ("sbuf", [128, 128], F), "ZB": ("sbuf", [128, 144], B), "ONE": ("sbuf", [128, 512], B),
+    "CM": ("sbuf", [128, 128], H16), "CT": ("sbuf", [128, 64], B), "W": ("sbuf", [128, 4 * 144], B),
+    "ZB": ("sbuf", [128, 160], B), "RL": ("sbuf", [128, 320], B), "BR": ("sbuf", [128, 320], B), "ONE": ("sbuf", [128, 512], B),
     "COL": ("sbuf", [128, 40], F), "COI": ("sbuf", [128, 16], I), "JK": ("sbuf", [128, 64], F),
-    "EH": ("sbuf", [128, 256], F), "FE": ("sbuf", [128, 256], F), "YB": ("sbuf", [128, 256], F), "YF": ("sbuf", [128, 256], F),
-    "YT": ("sbuf", [128, 256], F), "YK": ("sbuf", [128, 256], F), "YS": ("sbuf", [128, 8, 64], F),
+    "YB": ("sbuf", [128, 256], F), "YF": ("sbuf", [128, 256], F),
+    "YT": ("sbuf", [128, 2, 2, 32], F), "YK": ("sbuf", [128, 256], F), "YS": ("sbuf", [128, 256], F),
     "pA": ("psum", [128, 512], F), "pZ": ("psum", [128, 512], F), "pL0": ("psum", [128, 2, 4, 64], F), "pL1": ("psum", [128, 2, 4, 64], F),
-    "pV0": ("psum", [128, 512], F), "pV1": ("psum", [128, 512], F), "pK": ("psum", [128, 8, 128], B), "pY": ("psum", [128, 8, 64], F),
+    "pV0": ("psum", [128, 512], F), "pV1": ("psum", [128, 512], F), "pK": ("psum", [128, 4, 4, 32], F), "pY": ("psum", [128, 8, 64], F),
 }
-DSEM = ["dk", "db", "df", "dp", "dv", "kd", "dc0", "dc1", "df1", "dn1", "dyx", "dy", "ox0", "ox1", "ob0", "ob1", "oy0", "oy1", "of"] \
+DSEM = ["dk", "db", "df", "dp", "dv", "kd", "dc0", "dc1", "df1", "dn1", "dn2", "dn3", "dyx", "dy", "ox0", "ox1", "ox2", "ox3", "ob0", "ob1", "oy0", "oy1", "of"] \
     + ["%s%d%d" % (k, t, h) for k in ("kc", "ku") for t in range(3) for h in range(2)]
 SEMAPHORES = ["sV", "sS", "sP", "sG"] + DSEM + ["%s%d%d" % (k, t, h) for k in ("ls", "rs") for t in range(3) for h in range(2)]
 C23 = 12582912.0
 C28 = 402653184.0
-BIG = 1.5 * 2.0 ** 40
+BIG = 2.0 ** 40
+SB = 2.0 ** -13
 
-FIRST = """load io zero ga0 tka cols an eye ba0 tkb nf ba1 ka0 rot ga2 ff ka1 sa0 sa1 ka2 ka3 fa3S ga1 rr eg fa1V eo vc
-    tn2V tt kdma1 pc2 kp gb kdma0 fa0V gc kx fa2S inS
-    K12S x2 op1 K01V op0 up0 vb0 oh1V va dv vb1 vb2 pra0 H02S oh0V ol1 ol0 u0 U01 pra1 K24S a0 ge af0 U12 af1 nr0 ad0 gd
+FIRST = """load zero io tk0 ga0 tk2 tk1 cols tk3 ga1 an0 ka0 ka1 ka2 ka3 kh0 kh1S kh2 kh3S kl0 kl1S kl2 kl3S ga2 an1 ba0 nf ba1 ba2 eye
+    eo0 xf0 fa0S ffV eo1 eg xf1 in0S in1S gb0 fa1V sa0S tn2 dv fa2V fa3V gb1 gc0 vc pc2 sa1S gc1 ge gd
+    K12S K01V up0 vb0 va vb1 vb2 pra0 H02S op0 oh0V op1 oh1V ol1 ol0 u0 U01 pra1 K24S a0 af0 U12 af1 nr0 ad0 sa3S sa2S
     up1 ad1 u1 ac0 H24S cnt0 sp0 bg1 prb0 U34 pz0 mk0 ac1 ev0S af2 bg0 lw0 pk0 ev1S U23 uf0S r0 uf1S af3 s0 ad3V prc0
     kw0 ad2 nr1 cnt1 ac2 m0 hi0V lo0 S02S ev2S tr0 sp1 pz1 mk1 a1 ar0+ prc1 ks0 pk1 par kw1 thr0 thr1 kd0 ev3V m1 hi1V
-    prb1 lo1 lw1 r1 S34S S23S s1 tr1 ks1 kd1 flip0 tq0+ x0+ tn0S+ pc0+ flip1 pra0+ thr2 ku0 kt1S prb0+"""
-MIDDLE = """ar1 H12S H01V K12S af0 K01V af1 x1 K24S up0 tn1V pc1 a0 u0 U01 pra1 H24S up1 ad0 U12 u1 nr0 U23 uf0S ac0 uf1S
+    prb1 lo1 lw1 r1 S34S S23S s1 tr1 ks1 kd1 flip0 x0+ tn0+ pc0+ flip1 pra0+ thr2 ku0 kt1S prb0+"""
+MIDDLE = """ar1 H12S H01V K12S af0 K01V af1 x1 K24S up0 tn1 pc1 a0 u0 U01 pra1 H24S up1 ad0 U12 u1 nr0 U23 uf0S ac0 uf1S
     ad1 ac1 cnt0 sp0 ev1S prc0 af3 pz0 U34 prb1 mk0 lw0 nr1 pk0 r0 s0 ar0+ kw0 cnt1 m0 ev0S hi0S lo0 ad3V af2 tr0 sp1
-    pz1 ad2 ev3V a1 mk1 par ks0 out0 ac2 lw1 r1 kd0 S02S prc1 s1 thr0 thr1 ku0 ev2S kw1 hi1V thr2 pk1 tq0+ m1 lo1 tr1
-    flip0 ks1 tn0S+ S23S kd1 pc0+ pra0+ S34S x0+ prb0+ flip1 kt1S out2 out1"""
-LAST = """K01V ar1 x1 tq1 K12S H01V up0 a0 H12S af1 K24S tn1S af0 u0 up1 U12 ad1 U01 pc1 ad0 H24S ac0 pra1 prb1 nr0 cnt0
-    u1 U23 ev0S uf1S sp0 ac1 a1 uf0S U34 pz0 mk0 nr1 prc0 af2 lw0 ev1S pk0 kw0 r0 m0 S02S yt0 cnt1 s0 sp1 yu0 eh0 ad2
-    af3 pz1 mk1 ac2 ei0 ej0 ytr0 lw1 ys0 pk1 ad3 r1 ac3 yx0 prc1 s1 eh1 ei1 m1 ej1 kw1 ev2S yt1 ybp0 yb0V yk0 yu1 ev3S
-    S24S ybp1 yq0 ytr1 yfp0 ys1 yc0 yb1V yc1 yx1 yfp1 yq1S yf0V yk1 yf1V yg"""
+    pz1 ad2 ev3V a1 mk1 par ks0 out0 ac2 lw1 r1 kd0 S02S prc1 s1 thr0 thr1 ku0 ev2S kw1 hi1V thr2 pk1 m1 lo1 tr1
+    flip0 ks1 tn0+ S23S kd1 pc0+ pra0+ S34S x0+ prb0+ flip1 kt1S out2 out1"""
+LAST = """K01V ar1 x1 K12S H01V up0 a0 H12S af1 K24S tn1 af0 u0 up1 U12 ad1 U01 pc1 ad0 H24S ac0 pra1 prb1 nr0 cnt0
+    u1 U23 ev0S uf1S sp0 ac1 a1 uf0S U34 pz0 mk0 nr1 prc0 af2 lw0 ev1S pk0 kw0 r0 m0 S02S yt0 cnt1 s0 sp1 yu0 te0 ad2
+    af3 pz1 mk1 ac2 tz0 pe0 ytr0 lw1 ys0 pk1 ad3 r1 ac3 yx0 yx1 prc1 s1 te1 tz1 m1 pe1 kw1 ev2S yt1 ybp0 yb0V yk0 yu1 ev3S
+    S24S ybp1 yq0 ytr1 yfp0 ys1 yc0 yb1V yc1 yx2 yx3 yfp1 yq1S yf0V yk1 yf1V yg"""
+FIRST = """zero load io tk0 sa3S gc0 eye sa0S cols an0 ka0 bm0 sa1S tk1 an1 ka1 dv nf ga0 ka2 ba0 ba2 ga1 ffS bm1 ga2 fa1S ka3 ba1 eg vc eo2 eo1 eo0 vb0 fa2S gb1 gb0 fa3V gc1 vb1 kh0 kh1 in1V fa0S kl0 xk kl1 bg0 xf1 in0V vb2 op0 H02S va K12V bk1 op1 K01V oh0V ge up0 tn2 pc2 oh1S ol0 u0 uf0V U12 K24S pra0 af0 prc0 U01 bg1 a0 up1 nr0 bk0 ad0 gd ol1 cnt0 H24S af1 u1 ad1 sp0 pz0 U34 ac1 ev1S ac0 mk0 ev0S pra1 kw0 U23 hi0S nr1 prb0 sa2S lw0 af3 r0 uf1S lo0 af2 cnt1 pk0 prc1 s0 sp1 tr0 ad2 m0 pz1 mk1 ac2 ks0S ad3V kw1 prb1 kd0 pk1 hi1V lo1 a1 tr1 m1 ev3V ks1V ar0+ S02S ev2S S23S lw1 r1 s1 flip0V kd1 par S34V tn0+ thr0 flip1V thr1 kt1 pc0+ pra0+ thr2 x0+ ku0 prb0+"""
+MIDDLE = """H01V H12S ar1 K01V af1 x1 K12S tn1 K24S af0 pc1 up0 u0 U01 a0 pra1 U12 up1 H24S u1 ad0 nr0 uf1V U23 ad1 ac1 ac0 cnt0 sp0 uf0S U34 prc0 pz0 mk0 ev1S nr1 prb1 af3 pk0 lw0 kw0 ev0S m0 hi0S cnt1 r0 s0 lo0 sp1 ad3V tr0 af2 ev3V pz1 ks0V ar0+ mk1 out0 a1 ad2 S02S lw1 r1 kd0 s1 prc1 pk1 kw1 ac2 hi1V ku0 m1 lo1 tr1 par flip0S ev2S ks1V S23S tn0+ thr0 kd1 kt1 S34V pc0+ out2 out1 pra0+ thr1 prb0+ flip1V x0+ thr2"""
+LAST = """H01V H12S K01V ar1 af1 K12S up0 tn1 x1 u0 U01 af0 a0 K24S up1 H24S U12 pc1 ad0 ad1 u1 uf1S ac0 nr0 ev0S pra1 ac1 uf0S U23 cnt0 prb1 a1 sp0 pz0 af2 prc0 U34 mk0 nr1 ev1S lw0 kw0 cnt1 pk0 r0 yt0 af3 ad2 s0 te0 sp1 m0 yu0 pe0 pz1 mk1 ytr0 lw1 ac2 ys0V S02S r1 ad3 yk0 s1 tz0 pk1 ac3 prc1 ev2S te1 m1 pe1 kw1 yx1 tz1 yt1 ybp0 yfp1 yb0V ev3S yx0 S24S ybp1 yq0 yu1 yfp0 yb1V yc0 yc1 yx3S yf1V yf0V ytr1 ys1S yq1S ygS yx2 yk1"""
+FIRST = """zero cols io tk0 gc0 eye load sa0V an0 sa3S ga1 ka0 nf ga2 ka1 an1 ka2 dvS ga0 ba2 bm0 tk1 kh0 gb1 ffS vb0 eg bm1 eo2 ba0 gc1 sa1S ka3 gb0 kh1S kl0 va ba1 gd fa3V eo1 kl1 fa1S eo0 vc xf1 op1 in1V fa0S fa2S xk K01V op0 in0V K12V H02S tn2 bg0 oh1S pc2 up0 K24S oh0V vb1 ol0 u0 vb2 uf0V U01 af0 H24S prc0 up1 ol1 pra0 ge U12 u1 af1 bk0 ad0 nr0 a0 U34 ac0 cnt0 ev0S sp0 ad1 pz0 prb0 U23 mk0 sa2S ac1 ev1S lw0 nr1 kw0 r0 pk0 hi0S s0 ar0+ lo0 zz0V af2 m0 af3 cnt1 tr0 sp1 pra1 uf1S pz1 prc1 ad2 ks0V mk1 kw1 ad3V ac2 hi1V bg1S pk1 a1 kt0 lo1 ev3V prb1 zz1V S02S tr1 flip0V lw1 m1 ks1V ev2S par r1 s1 S23S kd0 S34V kd1 kt1 tn0+ pc0+ thr0 pra0+ prb0+ thr1 thr2 x0+ flip1V"""
+MIDDLE = """H01S ar1 H12V K01V K12S x1 af0 af1 tn1 pc1 K24S up0 u0 pra1 U01 a0 H24S up1 U12 u1 nr0 U23 ad0 uf1S ad1 ac1 ac0 cnt0 uf0S sp0 ev1S prc0 U34 pz0 prb1 out2 mk0 af3 nr1 lw0 kw0 pk0 ev0S cnt1 r0 ad3V m0 hi0S s0 ar0+ S02S out0 lo0 sp1 a1 prc1 pz1 zz0V af2 ev3V tr0 mk1 lw1 kw1 ks0V pk1 r1 hi1V kd0 kt0 ad2 m1 ac2 ev2S par lo1 S23S tn0+ zz1V tr1 s1 ks1V S34V pc0+ flip0V pra0+ kd1 x0+ kt1S thr0 thr1 flip1V thr2 prb0+ out1"""
+LAST = """ar1 H12S H01V K12S K01V af0 af1 x1 tn1 pc1 K24S up0 u0 U01 a0 pra1 H24S up1 U12 ad0 ac0 u1 uf0V ad1 ac1 ev0S prb1 uf1V nr0 ev1S cnt0 U23 sp0 a1 pz0 U34 mk0 af2 prc0 nr1 kw0 pk0 lw0 cnt1 af3 yt0 m0 yu0 ad2 r0 sp1 s0 pz1 mk1 ytr0 lw1 S02S ac2 ys0V pk1 ad3 te0 ac3 r1 ev2S s1 te1 m1 prc1 tz1 tz0 kw1 pe0 ybp0 yx1 ev3S yt1 yq0 pe1 yx0S yk0 ybp1 yfp1 yu1 yb0V S24S yc0 yb1V ytr1 yx2S yx3S yf1V yfp0 yf0S yc1S ys1V yg yq1S yk1"""
+FIRST = """zero load io tk0 sa3S gc0 eye sa0S cols an0 ka0 bm0 sa1S tk1 an1 ka1 dv nf ga0 ka2 ba0 ba2 ga1 ffS bm1 ga2 fa1S ka3 ba1 eg vc eo2 eo1 eo0 vb0 fa2S gb1 gb0 fa3V gc1 vb1 kh0 kh1 in1V fa0S kl0 xk kl1 bg0 xf1 in0V vb2 op0 H02S va K12V bk1 op1 K01V oh0V ge up0 tn2 pc2 oh1S ol0 u0 uf0V U12 K24S pra0 af0 prc0 U01 bg1 a0 up1 nr0 bk0 ad0 gd ol1 cnt0 H24S af1 u1 ad1 sp0 pz0 U34 ac1 ev1S ac0 mk0 ev0S pra1 kw0 U23 hi0S nr1 prb0 sa2S lw0 af3 r0 uf1S lo0 af2 cnt1 pk0 prc1 s0 sp1 tr0 ad2 m0 pz1 mk1 ac2 ks0S ad3V kw1 prb1 kd0 pk1 hi1V lo1 a1 tr1 m1 ev3V ks1V ar0+ S02S ev2S S23S lw1 r1 s1 flip0V kd1 par S34V tn0+ thr0 flip1V thr1 kt1 pc0+ pra0+ thr2 x0+ ku0 prb0+"""
+MIDDLE = """H01V H12S ar1 K01V af1 x1 K12S tn1 K24S af0 pc1 up0 u0 U01 a0 pra1 U12 up1 H24S u1 ad0 nr0 uf1V U23 ad1 ac1 ac0 cnt0 sp0 uf0S U34 prc0 pz0 mk0 ev1S nr1 prb1 af3 pk0 lw0 kw0 ev0S m0 hi0S cnt1 r0 s0 lo0 sp1 ad3V tr0 af2 ev3V pz1 ks0V ar0+ mk1 out0 a1 ad2 S02S lw1 r1 kd0 s1 prc1 pk1 kw1 ac2 hi1V ku0 m1 lo1 tr1 par flip0S ev2S ks1V S23S tn0+ thr0 kd1 kt1 S34V pc0+ out2 out1 pra0+ thr1 prb0+ flip1V x0+ thr2"""
+LAST = """H01V H12S K01V ar1 af1 K12S up0 tn1 x1 u0 U01 af0 a0 K24S up1 H24S U12 pc1 ad0 ad1 u1 uf1S ac0 nr0 ev0S pra1 ac1 uf0S U23 cnt0 prb1 a1 sp0 pz0 af2 prc0 U34 mk0 nr1 ev1S lw0 kw0 cnt1 pk0 r0 yt0 af3 ad2 s0 te0 sp1 m0 yu0 pe0 pz1 mk1 ytr0 lw1 ac2 ys0V S02S r1 ad3 yk0 s1 tz0 pk1 ac3 prc1 ev2S te1 m1 pe1 kw1 yx1 tz1 yt1 ybp0 yfp1 yb0V ev3S yx0 S24S ybp1 yq0 yu1 yfp0 yb1V yc0 yc1 yx3S yf1V yf0V ytr1 ys1S yq1S ygS yx2 yk1"""
+FIRST = """load zero io ga2 sa3S eye cols sa1S tk0 an0 sa0S ka0 an1 ka1 tk1 nf ga1 ka2 dv ffS kh0 bm0 ka3 bm1 ba2 ga0 gc0 fa2S gb0 ba0 vb0 kh1 fa1S ba1 fa0S vb1 fa3V eo2 eo1 eg kl1 gb1 eo0 kl0 bg0S vc va xf1 op0 xk bk1 op1 H02S in1V in0V oh0S K12V vb2 tn2 K01V K24S H24S up0 ol0 oh1S pc2 af0 u0 gc1 pra0 uf0V ge U12 prc0 gd up1 U01 pra1 gr bk0 u1 a0 nr0 ol1 ad0 ac0 cnt0 sp0 af1 U34 ev0S ad1 ac1 bg1 pz0 mk0 ev1S af2 prb0 U23 nr1 uf1S kw0 hi0S lw0 ad2 af3 r0 cnt1 lo0 s0 sa2S sp1 tr0 prc1 pk0 ks0S pz1 ac2 mk1 ad3V kw1 m0 kv0 hi1V pk1 m1 prb1 lo1 kt0 tr1 S02S a1 kd0 ev3V lw1 ks1V kv1 ev2S r1 s1 S34V ar0+ S23S par flip0V thr0 tn0+ flip1V thr1 kt1 x0+ pc0+ pra0+ kd1 prb0+ thr2"""
+MIDDLE = """H12S H01V K01V ar1 x1 K12S af0 tn1 af1 K24S up0 H24S pc1 pra1 u0 U01 a0 U12 up1 ad0 uf1V ac0 u1 ev0S ad1 uf0S nr0 ac1 cnt0 U23 prc0 sp0 U34 ev1S pz0 mk0 nr1 prb1 af3 ad3V pk0 lw0 m0 kw0 cnt1 hi0S r0 af2 s0 lo0 sp1 tr0 pz1 S02S prc1 a1 ev3V ks0V mk1 lw1 par kw1 kv0 r1 hi1V ad2 lo1 ac2 thr0 s1 pk1 tr1 out0 ks1V ev2S m1 kv1 thr1 kt0 kd0S ar0+ S34V S23S x0+ kd1 tn0+ pc0+ pra0+ prb0+ flip0S kt1 out1 thr2 flip1V out2"""
+LAST = """ar1 H12S K12S H01V K01V af1 up0 tn1 x1 K24S u0 a0 af0 U01 up1 H24S U12 ad0 u1 ac0 pc1 ad1 nr0 pra1 prb1 U23 ac1 cnt0 sp0 uf1S a1 uf0S ev0S U34 pz0 mk0 af2 prc0 lw0 nr1 ev1S pk0 kw0 cnt1 m0 yt0 yu0 sp1 r0 af3 ad2 pz1 ytr0 mk1 lw1 s0 S02S ys0 ac2 r1 te0 pk1 s1 m1 ev2S tz0 pe0 ad3 te1 ac3 ev3S prc1 tz1 yx1 yx0 kw1 pe1 ybp0 yt1 yb0V yfp1 S34S ybp1 yk0 yq0 S23S yu1 yfp0 yc0 yb1V yx3 yc1 ytr1 yf1V yf0V ys1 yg yq1S yk1 yx2"""
+FIRST = """load io eye sa2S zero gc0 tk0 cols an0 ga2 ga1 ga0 vb0 ka0 an1 sa0S ka1 bm0 ka2 nf ka3 ba0 ba2 bm1 ffV ba1 vc fa1V tk1 eo2 gb0 kh0S gc1 vb1 kh1 kl1 kl0 gr sa1S eg eo1 xk fa3V fa2S fa0S eo0 K12S in1V in0V tn2 dv xf1 vb2 va K01S pc2 up0 pra0 ph0 ge rk0 K24V rk1 bk1 H02S u0 hi0V ph1 af0 af1 up1 U01 U12 gd ad0 u1 rv0 lo0 ad1 bg0 br sa3S H24S bsS nr0 ac1 pra1 prc0 U23 cnt0 hi1S sp0 a0 U34 py0 ac0 pz0 mk0 prb0 lw0 mj0 ev1S ev0S nr1 pk0 r0 kw0 m0 s0 cnt1 prb1 af3 ad3V ks0V sp1 pz1 kv0 mk1 a1 py1 ev3V af2 lw1 mj1 lo1 pk1 ad2 S02S rv1 prc1 kw1 r1 m1 flip0S ar0+ s1 ac2 bk0 bg1 kt0 par kd0S ks1V kv1 ev2S S34V S23S kd1 kt1 thr0 flip1V thr1 tn0+ x0+ pc0+ pra0+ thr2 prb0+"""
+MIDDLE = """H12S K12S ar1 out2 ph0 af1 H01V tn1 K01V x1 up0 pc1 a0 u0 hi0V K24S pra1 U01 U12 prb1 up1 af0 u1 lo0 nr0 ad1 ph1 ac1 ad0 H24S U23 cnt0 sp0 ac0 hi1S ev1S pz0 U34 py0 prc0 af3 mj0 kw0 mk0 nr1 lw0 lo1 pk0 cnt1 r0 m0 s0 ev0S ad3V ks0S sp1 prc1 ev3V py1 pz1 mk1 a1 ar0+ lw1 S02S mj1 out0 kw1 par af2 ks1S pk1 thr0 kv0 r1 out1 ad2 kd0 ac2 s1 kt0 ev2S m1 kv1 flip0V thr1 S23S kd1 kt1 thr2 tn0+ S34V x0+ flip1V pc0+ pra0+ prb0+"""
+LAST = """ph0 H12S ar1 K12S H01V af0 tn1 af1 K01V up0 x1 a0 pc1 u0 K24S hi0V lo0 ph1 H24S U12 U01 pra1 up1 ad1 a1 u1 ad0 nr0 U23 ac0 cnt0 sp0 prc0 U34 ev0S py0 prb1 af2 pz0 ac1 ad2 mj0 ev1S kw0 mk0 nr1 pk0 m0 lw0 cnt1 yt0 r0 yu0 hi1S sp1 af3 pz1 ys0 S02S mk1 s0 lo1 ad3 ac2 py1 tz0 mj1 lw1 prc1 yk0 r1 yq0 yx1 kw1 te0 pe0 ev2S ac3 yx0 pk1 yt1 yfp0 ybp0 s1 yu1 ev3S tz1 te1 ys1 m1 yq1 S34S yb0V pe1 yc0 yk1 yfp1 S23V ybp1 yf0S yx3 yb1V yx2 yf1V yc1S yg"""
+FIRST = """load dvS io cols zero gc0 ga2 ga0 ga1 eye vb0 sa2S tk0 an0 ka0 an1 ka1 sa0S ba2 ka2 ba0 ka3 bm0 nf bm1 ffV ba1 vc vb1 tk1 eo2 gb0 gc1 eo0 eg eo1 kh1 kh0 kl0 kl1 fa0S fb0 fa1S fb1 sa1S vaS xk vb2 K01V in1V sa3V xf1 K12S up0 u0 in0S tn2 H12S pc2 rk0 pra0 ph0 ge gr K24S rk1 bk1 ph1 H01V rv0 hi0V af1 af0 up1 U12 ad1 pra1 U01 u1 lo0 gd bg0 H24S nr0 ac1 br ad0 prc0 hi1S bsS ac0 cnt0 sp0 a0 pz0 py0 U34 U23 prb0 mx0 ev1S ev0S nr1 lw0 pk0 r0 kw0 m0 s0 cnt1 prb1 sp1 ks0V kv0 pz1 py1 af3 mx1 ad3V a1 lw1 pk1 rv1 lo1 prc1 kw1 af2 ad2 S02S ev3V r1 gw0 m1 flip0S ar0+ s1 gw1 gw2 gw3 ac2 bk0 bg1 kt0 par kd0 ks1V kv1 ev2S S34V kt1 kd1 thr0 S23S thr1 tn0+ x0+ flip1V pc0+ pra0+ thr2 thr3 prb0+"""
+MIDDLE = """H12S ar1 H01V K01V K12S tn1 x1 ph0 af1 af0 up0 a0 pc1 hi0V u0 pra1 lo0 K24S prb1 up1 ph1 U02 u1 prc0 nr0 ad0 ac0 ad1 cnt0 ac1 H24S ev0S U23 U34 sp0 ev1S hi1S bf0 py0 pz0 bo0 mx0 lo1 nr1 a1 bf1 lw0 pk0 kw0 cnt1 bo1 m0 r0 out0 bd1 ks0S s0 kv0 sp1 pz1 py1 mx1 out1 mg bd0 prc1 lw1 par kw1 bw0S S02S ar0+ kt0 kd0 thr0 thr1 be0S r1 ks1V s1 kv1 bw1S tn0+ be1S flip0V pc0+ x0+ flip1V thr2 thr3 pra0+ prb0+ kd1 kt1 out2"""
+LAST = """ph0 H12S ar1 K12S H01V af0 tn1 af1 K01V up0 x1 a0 pc1 hi0V u0 K24S lo0 pra1 prb1 ph1 up1 H24S U01 U12 u1 ad0 ac0 a1 ad1 nr0 U23 U34 cnt0 ev0S sp0 prc0 pz0 py0 af2 ac1 ad2 mj0 kw0 mk0 nr1 pk0 m0 yt0 lw0 hi1S cnt1 ev1S r0 yu0 sp1 af3 ac2 pz1 ys0 S02S mk1 lo1 s0 ad3 py1 mj1 tz0 lw1 prc1 yk0 r1 yq0 yx1 kw1 te0 ev2S ac3 yx0 pk1 s1 yt1 pe0 yfp0 ybp0 yu1 ev3S tz1 te1 ys1 m1 yq1 S34S yb0V pe1 yk1 yc0 yfp1 S23V ybp1 yf0S yx3 yb1V yx2S yf1V yc1 yg"""
+FIRST = """load dvS io gc0 cols zero eye ga0 ga1 ga2 sa2S tk0 an0 vb0 ka0 bm0 an1 ka1 sa0S bm1 ka2 ba2 nf ka3 vb1 ba0 ffV tk1 eo2 gb0 gc1 eg kh0 kh1 kl0 kl1 fa0S fb0S fa1S fb1 sa1S vaS ba1 vc eo1 eo0 xk vb2 sa3V K01V in1V xf1 K12S up0 u0 in0S tn2 H12S pc2 rk0 pra1 ph1 ph0 pra0 ge gr K24S rk1 bk1 H01V U12 hi0S rv0 af1 af0 ad1S br up1 ac1S U01 lo0 u1 gd bg0 H24S nr0 ad0S prc0 bsS cnt0 sp0 a0 hi1S pz0 py0 U34 U23 prb0 ac0S mx0 ev1S ev0S nr1 lw0 r0 kw0V pk0 m0 cnt1 prb1 sp1 ks0V s0 kv0 py1 pz1 af3 ad3V mx1 a1 pk1 lw1 ac3V rv1 lo1 prc1 kw1V af2 ad2S S02S ev3V r1 m1 flip0S ar0+ s1 ac2S bk0 bg1 kt0 par kd0 ks1V kv1 ev2S S34V kt1 kd1 thr0 S23S thr1 tn0+ x0+ flip1V pc0+ pra0+ thr2 thr3 prb0+ ph0+"""
+MIDDLE = """ar1 H01V K01V x1 H12S K12S tn1 af1 out2 K24S H24S out0 pc1 up0 af0 hi0V u0 lo0 pra1 prb1 U12 U01 ph1 prc0 up1 ad1S ac1S ad0S u1 nr0 U23 U34 ac0S cnt0 a0 ev1S sp0 hi1S pz0 py0 mx0 nr1 lo1 af3 ev0S ad3V pk0 lw0 kw0V r0 ks0V cnt1 m0 s0 prc1 sp1 S02S kv0 py1 pz1 ac3V mx1 af2 a1 pk1 lw1 kw1S ad2S ev3V m1 r1 flip0V ks1S ac2S par ev2S thr0 kv1 s1 ar0+ S23S thr1 tn0+ out1 kd0 kt0 S34V x0+ flip1V pc0+ ph0+ pra0+ prb0+ thr2 thr3 kd1 kt1"""
+LAST = """H12S ar1 K12S H01V af0 tn1 af1 K01V up0 x1 pc1 a0 u0 hi0V K24S ph1 pra1 prb1 up1 H24S U12 U01 u1 lo0 nr0 a1 ad0S ac0S ad1V U23 U34 cnt0 ev0S sp0 prc0 py0 pz0 ac1V af2 mj0 kw0S mk0 nr1 pk0 lw0 cnt1 ad2V m0 yt0 ev1V yu0 r0 sp1 hi1S ac2V af3 pz1 py1 ad3S S02S ys0 lo1 mk1 mj1 s0 prc1 lw1 yk0 ev2V tz0 te0 r1 kw1S pe0 yt1 yq0 yx1 ac3S yx0 pk1 s1 yfp0 ybp0 yu1 ev3S te1 m1 ys1 tz1 pe1 S34S yb0V yk1 yq1 yc0S yfp1 S23V ybp1 yf0S yx3 yb1V yx2 yf1V yc1 yg"""
 ORDER = [FIRST, MIDDLE, MIDDLE, LAST]
 
 
@@ -75,11 +98,17 @@ def rank_program(g, core, T, topo):
         a, b = (slice(0, 2) if h == 2 else h), (k if w == 1 else slice(k, k + w))
         return (T[n][:, a, b, :], [(n, 256 * j + 64 * k, 256 * j + 64 * (k + w)) for j in ((0, 1) if h == 2 else (h,))])
 
-    def Zc(h, c0, c1):
-        return (T.Z[:, h, c0:c1], [("Z", 256 * h + c0, 256 * h + c1)])
+    def Zc(h, k):
+        return (T.Z[:, h, 128 * k:128 * k + 128], [("Z", 256 * h + 128 * k, 256 * h + 128 * k + 128)])
 
-    def pC(k, w=1):
-        return (T.pY[:, k:k + w, :], [("pY", 0, 64)])
+    def TK(turn, c0, c1, rows=slice(0, 128), st=1, key=()):
+        return (T.TK[rows, 4096 * turn + c0:4096 * turn + c1:st], [("TK", 4096 * turn + c0, 4096 * turn + c1) + key])
+
+    def pC(h, k, w=1):
+        return (T.pY[:, 2 * h + k:2 * h + k + w, :], [("pY", 128 * h + 64 * k, 128 * h + 64 * (k + w))])
+
+    def pB(k, r0=0, r1=4):
+        return (T.pK[:, slice(0, 2) if k == 2 else k, r0 if r1 == r0 + 1 else slice(r0, r1), :], [("pK", 0, 512)])
 
     def IX(win, off):
         return (win[0].indirect(off[0]), win[1] + off[1])
@@ -115,13 +144,13 @@ def rank_program(g, core, T, topo):
     def ms(o, c):
         op("V", [lambda: g.vector.memset(o[0], c)], [o], [])
 
-    def act(o, i, scale=1.0, bias=0.0, acc=None):
+    def act(o, i, scale=1.0, bias=0.0, acc=None, func=None):
         if acc is not None:
             op("S", [lambda: g.scalar.activation(o[0], i[0], ACT.Identity, bias=bias, accum_out=acc[0])], [o, acc], [i])
         elif bias == 0.0:
             op("S", [lambda: g.scalar.activation(o[0], i[0], ACT.Copy, scale=scale)], [o], [i])
         else:
-            op("S", [lambda: g.scalar.activation(o[0], i[0], ACT.Identity, bias=sa(bias), scale=scale)], [o], aps(i, bias))
+            op("S", [lambda: g.scalar.activation(o[0], i[0], func or ACT.Identity, bias=sa(bias), scale=scale)], [o], aps(i, bias))
 
     def cp(o, i, e="V"):
         if e == "S":
@@ -129,11 +158,14 @@ def rank_program(g, core, T, topo):
         else:
             op("V", [lambda: g.vector.tensor_copy(o[0], i[0])], [o], [i])
 
-    def flip(o, i, e="V"):
+    def lin(o, i, a, b, e="V"):
         if e == "S":
-            act(o, i, -1.0, 255.0)
+            act(o, i, a, b)
         else:
-            ts(o, i, -1.0, ALU.mult, 255.0, ALU.add)
+            ts(o, i, a, ALU.mult, b, ALU.add)
+
+    def flip(o, i, e="V"):
+        lin(o, i, -1.0, 255.0, e)
 
     def mm(o, terms, start=True, stop=True, whole=False):
         op("P", [lambda l=l, r=r, k=k: g.tensor.matmul(o[0], l[0], r[0], start and k == 0, stop and k == len(terms) - 1)
@@ -161,7 +193,7 @@ def rank_program(g, core, T, topo):
         return A("W", 144 * k + c0, 144 * k + c1, st)
 
     def wrows(k, rows, w):
-        sel(Wm(k), A("ZB"), [[-16, 9], [200, 16]], -rows[0] - 3000, w)
+        sel(Wm(k), A("ZB", 0, 144), [[-16, 9], [200, 16]], -rows[0] - 3000, w)
         for r in rows[1:]:
             sel(Wm(k, 15, 128, 16), Wm(k, 15, 128, 16), [[-16, 8]], -r, w)
 
@@ -179,58 +211,77 @@ def rank_program(g, core, T, topo):
         mm(o, [(Wm(k, 15 - q, 143 - q), A(n, c + q, c + 1024, 16)) for q in range(16)], start, stop)
 
     dg = [[-1, 128]]
-    zb, z8, nf = A("ZB", 0, 128), A("ZB", 0, 128, 1, 0, 8), A("FF", 256, 512, 1, 0, 8)
+    zb, nf = A("ZB", 0, 128), A("FF", 256, 512, 1, 0, 8)
+
+    def Y(n, c0=0, c1=144, p1=128, st=1):
+        k = 144 * MY.index(n); return A("YM", k + c0, k + c1, st, 0, p1)
+
+    def first(k, w=1):
+        return Q("pL%d" % (k == 0), 2, k, w)
 
     def setup(kind, h, e):
         if kind == "load":
-            dma(A("EI", 256, 512), X(T.belts[:]), "db")
             dma(A("EI", 0, 256, 1, 0, 64), X(T.kid0[:]), "dk", "S")
             dma(A("EI", 0, 256, 1, 64, 128), X(T.kid1[:]), "dk")
+            dma(A("EI", 256, 512), X(T.belts[:]), "db")
             dma(A("FI", 0, 256, 1, 0, 8), X(T.flip[:]), "df", "S")
             dma(A("TF0", 0, 2048), X(T.faces[:]), "dp")
         elif kind == "zero":
-            ms(A("ZF"), 0.0); ms(A("ZB"), 0.0)
+            ms(A("ZB"), 0.0)
         elif kind == "io":
             iota(A("IO2"), dg, 0, 1)
         elif kind == "eye":
             ts(cf("If"), A("IO2"), 0.0, ALU.is_equal)
-        elif kind == "tka":
-            ms(A("TK", 0, 2048), 0.0)
-        elif kind == "tkb":
-            act(A("TK", 4096, 6144), A("TK", 0, 2048))
-        elif kind == "cols":
-            ms(col(5, 0, 64), 8191.0); ms(col(5, 64, 128), -8193.0); ms(col(6, 0, 64), -4096.0); ms(col(6, 64, 128), 4096.0)
-        elif kind == "ga":
+        elif kind == "tk":
             if h == 0:
-                sel(cf("U16"), A("ZF"), dg, -1, 1.0)
-                sel(cb("GXp", p1=8), z8, [[-1, 8], [0, 16]], 0, BIG)
-                sel(cf("U16", 15, 128, 16), A("ZF", 0, 8), [[-16, 8]], 0, 1.0)
-                sel(cb("GXn", p1=8), z8, [[-1, 8], [0, 16]], 0, -BIG)
-                sel(cf("U16"), cf("U16"), dg, 0, -1.0)
-                return
-            for m, o in (("E", 0), ("O", 1)) if h == 1 else ():
-                for b in range(2):
-                    sel(cf("%s%d" % (m, b)), A("ZF"), [[-16, 8], [300, 2], [-2, 8]], -300 * b - o, 0.5)
-            for b in range(2) if h == 2 else ():
-                sel(cb("GX%d" % b, p1=8), z8, [[-1, 8], [300, 2], [0, 8]], -300 * b, 4096.0)
+                ms(TK(0, 0, 2048), 0.0)
+            else:
+                cp(TK(1, 0, 2048), TK(0, 0, 2048), "S")
+        elif kind == "bk":
+            dma(TK(h, 2048, 4096), TK(h, 0, 2048), "dc%d" % h, e or "Y")
+        elif kind == "bm":
+            if h == 0:
+                ts(A("SI", 768, 1024), A("EI", 256, 512), 4094, ALU.bitwise_and)
+            else:
+                lin(A("PS", 512, 768), A("SI", 768, 1024), 1.0 / 4096, -1.0)
+        elif kind == "xk":
+            lin(A("p16"), L("pZ", 2, 4), 2048.0, 4096.0)
+        elif kind == "cols":
+            ms(col(5, 0, 64), 8191.0); ms(col(6, 0, 64), -8192.0); ms(col(5, 64, 128), -8193.0); ms(col(6, 64, 128), 0.0)
+        elif kind == "ga":
+            def put(n, o, w, old=False):
+                sel(Y(n), Y(n) if old else A("ZB", 0, 144), [[-16, 9], [300, 2], [-2, 8]], -300 - o, w)
+            if h == 0:
+                put("OE", 1, 1.0); put("E", 0, 1.0); put("OE", 0, -1.0, True)
+            elif h == 1:
+                for n, w in (("GP", BIG), ("GN", -BIG)):
+                    sel(Y(n, p1=8), A("ZB", 0, 144, 1, 0, 8), [[-1, 9], [300, 2], [0, 8]], -300, w)
+            else:
+                put("SO", 2, 1.0); put("O", 1, 1.0)
+                sel(Y("SO", 15, 143, st=16), A("ZB", 0, 8), [[-16, 8]], 0, 1.0)
+                put("SO", 1, -1.0, True)
         elif kind == "sa":
-            for n, s in ((("Ib", 1.0), ("nIb", -1.0), ("nhI", -0.5)), (("I2", 2.0), ("Kp", BIG / 4096), ("Kn", -BIG / 4096)))[h]:
-                act(cb(n), cf("If"), s)
-            for n, c in ((("C3", 395264.0),), (("C20", 20.0), ("EI8", 0.125 / 4096), ("CC", C23 / 32)))[h]:
-                act(cb(n), zb, 1.0, c)
+            for n, s in ((("Ib", 1.0), ("nIb", -1.0), ("I4k", 4096.0)), (("Kp", BIG), ("Kn", -BIG), ("Ip", 4 * SB)), (("nhI", -2048.0), ("I2", 2.0)), ())[h]:
+                if e == "S":
+                    act(cb(n), cf("If"), s)
+                else:
+                    ts(cb(n), cf("If"), s, ALU.mult)
+            for n, c in (("C20", 20.0), ("EI8", 0.125), ("CC", C23 / 32)) if h == 3 else ():
+                if e == "S":
+                    act(cb(n), zb, 1.0, c)
+                else:
+                    ms(cb(n), c)
         elif kind == "an":
-            ts(A("SI"), A("EI"), 1, ALU.bitwise_and)
+            ts(A("SI", 256 * h, 256 * h + 256), A("EI", 256 * h, 256 * h + 256), 1, ALU.bitwise_and)
         elif kind == "nf":
             ts(nf, A("FI", 0, 256, 1, 0, 8), 0.0, ALU.is_equal)
         elif kind == "ba":
             if h == 0:
-                ts(A("pV1", 0, 256), A("SI", 256, 512), 8191.0, ALU.mult, -4096.0, ALU.add)
+                ts(A("SI", 512, 768), A("EI", 256, 512), 1, ALU.arith_shift_right)
+            elif h == 1:
+                lin(A("PS", 0, 256), A("SI", 512, 768), 1.0 / 2048, -1.0)
             else:
-                tt(A("P0"), A("pV1", 0, 256), A("EI", 256, 512), ALU.add)
-        elif kind == "rot":
-            mm(A("pZ", 0, 256), [(cf("U16"), A("P0")), (cb("GXp", p1=8), nf), (cb("GXn", p1=8), nf)])
-        elif kind == "rr":
-            tt(A("RR"), A("pZ", 0, 256), A("P0"), ALU.add)
+                lin(A("PS", 256, 512), A("SI", 256, 512), 2.0, -1.0)
         elif kind == "ka":
             if h == 0:
                 ts(A("pV0", 0, 256), A("SI", 0, 256), col(5), ALU.mult, col(6), ALU.add)
@@ -240,35 +291,45 @@ def rank_program(g, core, T, topo):
                 cp(A("KP", 0, 256), A("pV0", 256, 512))
             else:
                 tt(A("KP", 256, 512), A("pV0", 256, 512), A("KP", 0, 256), ALU.subtract)
-        elif kind == "kdma":
-            c = 4096 * h
-            for r in range(4):
-                dma((T.TK[4 * r + h:128:16, c:c + 2048], [("TK", c, c + 2048)]),
+        elif kind in ("kh", "kl"):
+            for r in (0, 1) if kind == "kh" else (2, 3):
+                dma(TK(h, 0, 2048, slice(4 * r + h, 128, 16), key=(r,)),
                     A("KP", 256 * (r // 2), 256 * (r // 2) + 256, 1, 64 * (r % 2), 64 * (r % 2) + 64), "kd", e or "Y")
         elif kind == "dv":
-            dma(A("TF0", 2048, 4096), X(T.faces[:]), "dv")
+            dma(A("TF0", 2048, 4096), X(T.faces[:]), "dv", e or "Y")
         elif kind == "ff":
-            act(A("FF", 0, 256, 1, 0, 8), nf, -1.0, 1.0)
+            lin(A("FF", 0, 256, 1, 0, 8), nf, -2 * SB / BIG, SB / BIG, e)
         elif kind == "eo":
-            for k, m in enumerate("EO"):
-                mm(Q("pL0", 2, k), [(cf("%s%d" % (m, b)), A("RR", b, 256, 2)) for b in range(2)])
+            def slots(n):
+                return [(Y(n, 8 - 8 * b, 136 - 8 * b), A("PS", 256 * k + b, 256 * k + 256, 2)) for b in range(2) for k in (h & 2, 1)]
+            off = [(Y(n, 8 - 8 * b, 136 - 8 * b, 8), A("FF", 256 + b, 512, 2, 0, 8)) for n in ("GP", "GN") for b in range(2)]
+            mm(first(h) if h < 2 else L("pZ", 2, 4), slots(("OE", "SO")[h % 2]) + off + slots("EO"[h % 2]))
         elif kind == "eg":
-            mm(Q("pL0", 2, 2), [(cb("GX%d" % b, p1=8), A("FF", b, 256, 2, 0, 8)) for b in range(2)])
+            mm(first(2), [(Y("GP", 8 - 8 * b, 136 - 8 * b, 8), A("FF", b, 256, 2, 0, 8)) for b in range(2)])
+        elif kind == "xf":
+            lin(Q("X16", 2, h), first(h), 2048.0, 4096.0)
         elif kind == "in":
-            cp(Q("IN0", 2, 0, 3), Q("pL0", 2, 0, 3), e)
+            cp(Q("IN0", 2, h, 1 + h), first(h, 1 + h), e)
         elif kind == "fa":
             flip(A("TF0", 4096 + 1024 * h, 5120 + 1024 * h), A("TF0", 1024 * (h % 2), 1024 * (h % 2) + 1024), e)
+        elif kind == "fb":
+            dma(A("TF0", 6144 + 1024 * h, 7168 + 1024 * h), A("TF0", 4096 + 1024 * h, 5120 + 1024 * h), "dn%d" % (2 + h), e or "Y")
         elif kind == "gb":
-            weave(lambda: wrows(0, [4, 12, 1, 9], 1.0), lambda: wrows(1, [0, 8, 5, 13], 0.5), lambda: wrows(3, [0, 8], 1.0))
+            if h == 0:
+                weave(lambda: wrows(0, [4, 12, 1, 9], 1.0), lambda: wrows(1, [0, 8, 5, 13], 1.0 / 4096))
+            else:
+                wrows(3, [0, 8], 1.0)
         elif kind == "gc":
+            if h == 0:
+                op("G", [lambda: g.iota(T.COI[:, 0:1], [[0, 1]], 0, 1)], [A("COI", 0, 1)], [])
+                iota(cb("C16"), [[16, 128]], 0, 0)
+                return
             iota(Wm(2), [[0, 144]], 0, 0)
-            op("G", [lambda: g.iota(T.COI[:, 0:1], [[0, 1]], 0, 1)], [A("COI", 0, 1)], [])
+            iota(cb("nB4"), [[0, 128]], -2, 0)
             iota(Wm(2, 15, 128, 16), [[0, 8]], 1, 0)
-            iota(cb("C16"), [[16, 128]], 0, 0)
-            sel(Wm(2, 15, 128, 16), Wm(2, 15, 128, 16), [[-16, 8]], 0, 0.0, ALU.is_ge)
-            iota(cb("nB4"), [[0, 128]], -4, 0)
-            sel(Wm(2, 15, 128, 16), Wm(2, 15, 128, 16), [[16, 8]], 15, 0.0, ALU.is_ge, -1)
             iota(cb("B8I"), [[0, 128]], 1, 0)
+            sel(Wm(2, 15, 128, 16), Wm(2, 15, 128, 16), [[-16, 8]], 0, 0.0, ALU.is_ge)
+            sel(Wm(2, 15, 128, 16), Wm(2, 15, 128, 16), [[16, 8]], 15, 0.0, ALU.is_ge, -1)
         elif kind == "ge":
             for pat, base, cm in (([[-8, 16], [0, 8]], 0, 1), ([[8, 16], [0, 8]], 7, -1)):
                 for n in ("B8I", "nB4"):
@@ -281,76 +342,99 @@ def rank_program(g, core, T, topo):
                 if n != "Dn":
                     sel(cb(n), cb(n), dg, 0, -w)
             weave(lambda: shift("IDn", 1, -1.0, 0), lambda: shift("UpI", -1, 1.0, 7), lambda: shift("Dn", 1, 1.0, 0))
+        elif kind == "gr":
+            for k in range(2):
+                sel(A("RL", 160 * k, 160 * k + 160), A("ZB"), [[-16, 5], [300, 2], [-1, 16]], -64 * k - 300, 1.0)
+        elif kind == "br":
+            mm(A("pA", 0, 320), [(cb("B8I"), A("RL"))])
+        elif kind == "bs":
+            cp(A("BR"), A("pA", 0, 320), e)
+        elif kind == "gw":
+            o = A("WB", 1024 * h, 1024 * h + 1024)
+            if h < 2:
+                iota(o, [[0, 1024]], 0, 0)
+            sel(o, o if h < 2 else A("WB", 1024 * h - 2048, 1024 * h - 1024), [[-16, 4], [0, 16], [-1, 16]], -64 * (h % 2), BIG if h < 2 else -BIG)
         elif kind == "va":
-            ts(A("CH", 0, 128), cf("If"), 2.0 ** -10 - 1.0, ALU.mult)
-            ts(A("CH", 128, 256), cf("If"), 2.0 ** -11 - 0.5, ALU.mult)
+            lin(A("CH", 0, 128), cf("If"), 2.0 ** -10 - 1.0, 0.0, e)
+            lin(A("CH", 128, 256), cf("If"), 2.0 ** -11 - 0.5, 0.0, e)
         elif kind == "vc":
-            ms(A("ONE", 0, 512, 1, 0, 32), 1.0); ms(col(2), 10.0); ms(col(3), 1.0)
-            ms(A("CT", 0, 64), 8192.0); ms(A("CT", 64, 256), 4096.0)
+            ms(A("ONE", 0, 512, 1, 0, 32), 1.0); ms(col(2), -7.5); ms(A("CT"), 2 * SB)
         elif kind == "vb":
             if h == 0:
                 ts(A("COI", 4, 5), A("COI", 0, 1), 15, ALU.bitwise_and)
             elif h == 1:
                 ts(col(1), A("COI", 4, 5), 2048.0, ALU.add)
+                ts(col(8), A("COI", 4, 5), -2048.0, ALU.add)
             else:
-                ts(A("CM"), cb("C16"), col(1), ALU.add, -2048.0, ALU.add)
+                ts(A("CM"), cb("C16"), col(8), ALU.add, 1.0 / 2048, ALU.mult)
         elif kind == "bg":
             if h == 0:
-                dma(A("TK", 2048, 4096), A("TK", 0, 2048), "dc0")
-                dma(A("TK", 6144, 8192), A("TK", 4096, 6144), "dc1")
+                dma(A("TF1", 0, 2048), X(T.faces[:]), "df1", e or "Y")
             else:
-                dma(A("TF1", 4096, 6144), A("TF0", 4096, 6144), "dn1")
-                dma(A("TF1", 0, 2048), X(T.faces[:]), "df1")
-        elif kind == "tt":
-            ts(A("TT"), Q("pL0", 2, 0), 394240.5, ALU.add)
-        elif kind == "kp":
-            mm(L("pZ", 2, 4), [(cb("Ib"), Q("PC", 2, 0)), (cb("nIb"), Q("TN", 2, 0)), (cb("nIb"), Q("TN", 2, 0)), (cb("nIb"), A("TT")), (cb("Ib"), cb("C3"))])
-        elif kind == "kx":
-            cp(A("p16"), L("pZ", 2, 4))
+                dma(A("TF1", 4096, 6144), A("TF0", 4096, 6144), "dn1", e or "Y")
         elif kind == "op":
             for k in range(2):
-                rows2list(A("pV%d" % h, 64 * k, 64 * k + 64), 3 - 3 * k, "TK", 1024 * h)
+                mm(A("pV%d" % h, 64 * k, 64 * k + 64),
+                   [(Wm(3 - 3 * k, 15 - q, 143 - q), TK(0, 1024 * h + q, 1024 * h + 1024, st=16)) for q in range(16)])
         elif kind == "oh":
-            cp(Zc(h, 0, 128), A("pV%d" % h, 0, 128), e)
+            cp(Zc(h, 0), A("pV%d" % h, 0, 128), e)
         elif kind == "ol":
-            tt(Zc(h, 128, 256), A("pV%d" % h, 0, 128), Zc(h, 0, 128), ALU.subtract)
+            tt(Zc(h, 1), A("pV%d" % h, 0, 128), Zc(h, 0), ALU.subtract)
         else:
             raise ValueError(kind)
 
     def outputs_of_the_drawn(k):
         if k == 0:
             cp(A("KF"), A("EI", 0, 256))
-            ms(col(7, 0, 32), 4096.0); ms(col(7, 32, 64), 4097.0)
-            return
-        if k == 1:
+        elif k == 1:
             dma(X(T.yx[:, 0:2048]), A("TF0", 0, 2048), "dyx")
             dma(X(T.y0[:, 0:2048]), A("KF", 0, 256, 1, 0, 64), "dy")
             dma(X(T.y1[:, 0:2048]), A("KF", 0, 256, 1, 64, 128), "dy")
-            return
-        p8 = [[-16, 8], [-1, 8]]
-        pz = [[-16, 8], [-1, 8], [300, 2]]
-        w = 2.0 / 4096
-        for b in range(2):
-            sel(cf("a%d" % b), A("ZF"), pz, -8 * b, 2.0)
-            sel(cf("b%d" % b), A("ZF"), pz, -8 * b - 300, 2.0)
-            sel(cf("c%d" % b), A("ZF"), pz, -8 * b, -w)
-            sel(cf("c%d" % b, 1, 128, 2), cf("c%d" % b, 1, 128, 2), p8, -8 * b, w)
-            sel(cf("d%d" % b), A("ZF"), pz, -8 * b + 1, w)
-            sel(cf("d%d" % b, 0, 128, 16), A("ZF", 0, 8), [[-16, 8]], -8 * b - 7, w)
-            sel(cf("d%d" % b, 1, 128, 2), cf("d%d" % b, 1, 128, 2), p8, -8 * b, -w)
-            sel(cf("FT", 8 * b, 8 * b + 8), A("ZF", 0, 8), [[-16, 8]], -8 * b, w / 2)
+
+    def pairs_to_slots(b):
+        p8, pz, w = [[-16, 8], [-1, 8]], [[-16, 8], [-1, 8], [300, 2]], 4096.0
+        sel(cb("a%d" % b), zb, pz, -8 * b - 300, w)
+        sel(cb("b%d" % b), zb, pz, -8 * b + 1, w)
+        sel(cb("c%d" % b), zb, pz, -8 * b, w)
+        sel(cb("d%d" % b), zb, pz, -8 * b + 1, -w)
+        sel(cb("b%d" % b, 0, 128, 16), A("ZB", 0, 8), [[-16, 8]], -8 * b - 7, w)
+        sel(cb("c%d" % b, 1, 128, 2), cb("c%d" % b, 1, 128, 2), p8, -8 * b, -w)
+        sel(cb("d%d" % b, 0, 128, 16), A("ZB", 0, 8), [[-16, 8]], -8 * b - 7, -w)
+        sel(cb("e%d" % b), zb, [[-16, 8], [0, 16]], -8 * b, BIG)
+        sel(cb("d%d" % b, 1, 128, 2), cb("d%d" % b, 1, 128, 2), p8, -8 * b, w)
+        sel(cb("f%d" % b), zb, [[-16, 8], [0, 16]], -8 * b, -BIG)
+        sel(cb("FT", 8 * b, 8 * b + 8), A("ZB", 0, 8), [[-16, 8]], -8 * b, -1.0)
 
     def kid_rows(t, h, turn, q):
-        c = 2048 + 4096 * turn + 1024 * h
-        for gg in range(8):
-            p = 16 * gg + turn
-            dma((T.TK[p:p + 13:4, c:c + 1024], [("TK", c, c + 1024, gg)]), (T["KS%d" % h][0:256 // NT, gg, :], [("KS%d" % h, 0, 1)]),
-                "kc%d%d" % (t, h), q)
+        c = 2048 + 1024 * h
+        for k in range(2):
+            dma(TK(turn, c, c + 1024, slice(64 * k + turn, 64 * k + 64, 4), key=(10 + k,)),
+                (T.KS[:, h, k, :, :], [("KS", h, h + 1)]), "kc%d%d" % (t, h), q)
+
+    def blocks(n, k, c0):
+        return A(n, 160 * k + 16 - 16 * c0, 160 * k + 144 - 16 * c0)
+
+    def to_blocks(h, summed, stop):
+        for k in range(2):
+            if summed:
+                terms = [(blocks("RL", k, c0), (T.Z[:, h, 128 * p + c0:128 * p + 128:2], Zc(h, p)[1])) for p in range(2) for c0 in range(2)]
+            else:
+                terms = [(blocks("RL", k, c0), (T.Z[:, h, c0:256:2], Zc(h, 0)[1] + Zc(h, 1)[1])) for c0 in range(2)]
+            mm(pB(k, 0, 2 if summed else 4), terms, k == 0, stop and k == 1)
+
+    def old_kids(h, summed, w, stop=False):
+        if summed:
+            for k in range(2):
+                c = 256 * h + 128 * k
+                acc(pB(k, 0, 2), [(w, A("ZR", c, c + 64)), (w, A("ZR", c + 64, c + 128))], stop and k == 1)
+        else:
+            acc(pB(2), [(w, A("ZR", 256 * h, 256 * h + 256))], stop)
 
     def step(name, t):
-        if name[-1] == "+":
-            name, t = name[:-1], t + 1
+        if name[-1] in "+-":
+            name, t = name[:-1], t + (1 if name[-1] == "+" else -1)
         last = t == RO - 1
+        UQ = "uq" in ORDER[t].split()
         tf, tfn, inb, rb = "TF%d" % (t % 2), "TF%d" % ((t + 1) % 2), "IN%d" % t, "R%d" % t
         if name[0] in "KHUS":
             a, b, e = int(name[1]), int(name[2]), name[3:]
@@ -371,7 +455,6 @@ def rank_program(g, core, T, topo):
         h = int(kind[-1]) if kind[-1].isdigit() else 0
         kind = kind.rstrip("0123")
         Ib, nIb = cb("Ib"), cb("nIb")
-        src = inb if t else "pL0"
 
         def go(k, w=1):
             return Q("pL%d" % h, 0, k, w)
@@ -383,53 +466,89 @@ def rank_program(g, core, T, topo):
             return [(nIb, Q("PC", h, 0, 2)), (Ib, Q("TN", h, 0, 2))]
         pK, pH, tK, tH, tF = Q("PC", h % 3, 0), Q("PC", h % 3, 1), Q("TN", h % 3, 0), Q("TN", h % 3, 1), Q("TN", h % 3, 2)
         ngo, opn = Q("MK", h % 3, 0), Q("MK", h % 3, 1)
-        pk, np_ = (None, [("pK", 0, 1)]), 256 // NT
-        py, ys = (None, [("pY", 0, 1)]), (T.YS[0:64, :, 32 * (h % 2):32 * (h % 2) + 32], [("YS", h, h + 1)])
         if kind == "out":
             if t == 1:
                 outputs_of_the_drawn(h)
+            if h == 2:
+                pairs_to_slots(t - 1)
         elif kind in ("af", "ad", "ac", "ev"):
             c, bank = 512 * h, A("pV%d" % (h % 2))
             o = A(tf, 8192 + c, 8704 + c)
             terms = [(A("CH", 0, 128), A("FW", c, c + 512)), (A("CH", 128, 256), A("D", c, c + 512)), (cb("CC", p1=32), A("ONE", 0, 512, 1, 0, 32))]
-            if kind != "ev":
+            if h == 3 and UQ:
+                terms[0:2] = [(A("CH", 128, 256), A("FW", c, c + 512)), (A("CH", 128, 256), A("UQ"))]
+            if kind == "ac" and e == "V":
+                op("X", [], [], [])
+            elif kind != "ev":
                 k = "fdc".index(kind[1])
                 mm(bank, terms[k:k + 1], k == 0, k == 2 or e == "V")
             elif e == "S":
                 act(o, bank, 1.0, 255.0 - C23)
             else:
                 ts(o, bank, C23, ALU.add, C23 - 255.0, ALU.subtract)
+        elif kind in ("bf", "bd", "bo", "bw", "be"):
+            c, bank = 1024 + h, A("pV%d" % h)
+            old, new = A(tf, 2048 + c, 4096, 2), A(tfn, 2048 + c, 4096, 2)
+            if kind == "bw":
+                for k in range(8):
+                    acc(A("pV%d" % h, k, 512, 8), [(A("WB", 2048 * s + 2 * k + h, 2048 * s + 2048, 16), L("MG", 0)) for s in range(2)], k == 7 and e == "V")
+                if e == "S":
+                    acc(bank, [(nIb, old)], True)
+                else:
+                    op("X", [], [], [])
+            elif kind != "be":
+                k = "fdo".index(kind[1])
+                if UQ and k < 2:
+                    mm(A("pV%d" % h, 0, 256), [(A("CH", 128 * k, 128 * k + 128), A(("FW", "D")[k], c, 1536, 2))], k == 0, False, True)
+                    acc(A("pV%d" % h, 256, 512), [(A("CH", 128, 256), (A("FW", c + 512, 2048, 2), A("UQ", h, 512, 2))[k])])
+                else:
+                    mm(bank, [((A("CH", 0, 128), A("FW", c, 2048, 2)), (A("CH", 128, 256), A("D", c, 2048, 2)), (Ib, old))[k]], k == 0, False)
+            elif e == "S":
+                act(new, bank, -1.0)
+            else:
+                tt(new, old, bank, ALU.subtract)
+        elif kind == "mg":
+            ts(L("MG", 0), L("pZ", 1, 0, 3), 6.0, ALU.is_lt, C23 / BIG, ALU.max)
+        elif kind == "mh":
+            lin(L("MG", 1), L("MG", 0), -1.0, 0.0, e)
         elif kind == "ar":
             op("X", [], [Q(inb, h, 0, 3)], [], "rs%d%d" % (t - 1, h), neng)
         elif kind == "x":
-            ts(Q("X16", h, 0, 2), Q(src, h, 0, 2), 2048.0, ALU.add)
+            lin(Q("X16", h, 0, 2), Q(inb, h, 0, 2), 2048.0, 4096.0)
         elif kind == "tn":
-            if e == "S":
-                act(Q("TN", h, 0, 3), Q("TR", h, 0, 3), -1.0, 786432.0)
-            else:
-                ts(Q("TN", h, 0, 3), Q(src, h, 0, 3), 2048.0, ALU.is_ge, -4096.0, ALU.mult)
-        elif kind == "tq":
-            act(Q("TR", h, 0, 3), Q(src, h, 0, 3), 1.0, 786432.5)
+            act(Q("TN", h, 0, 3), Q(inb, h, 0, 3), -1.0, -SB, None, ACT.Sign)
+        elif kind == "te":
+            act(Q("TE", h, 0, 3), Q(rb, h, 0, 3), -1.0, -SB, None, ACT.Sign)
         elif kind == "pc":
-            tt(Q("PC", h, 0, 2), Q(src, h, 0, 2), Q("TN", h, 0, 2), ALU.add)
+            tt(Q("PC", h, 0, 2), Q(inb, h, 0, 2), Q("TN", h, 0, 2), ALU.add)
+        elif kind == "pe":
+            tt(Q("PC", h, 0, 2), Q(rb, h, 0, 2), Q("TE", h, 0, 2), ALU.add)
+        elif kind == "tz":
+            ts(Q("T2", h, 0, 2), Q(rb, h, 0, 2), 0.0, ALU.is_ge, 1.0 / 4096, ALU.mult)
         elif kind == "up":
-            rows2list(L("pZ", h, 4), 0, "G", 1024 * h)
+            rows2list(pC(h, 0), 0, "G", 1024 * h)
         elif kind == "u":
-            ts(L("u16", h), L("pZ", h, 4), 0.5, ALU.mult, 2048.0, ALU.add)
-        elif kind == "uf":
-            cp(L("UF", h), L("pZ", h, 4), e)
+            lin(L("u16", h), pC(h, 0), 0.5, 4096.0)
+        elif kind == "ph":
+            mm(pC(h, 1), [(cb("I4k"), pH), (cb("I4k"), tH)])
         elif kind == "a":
             rows2list(go(0), 1, "G", 1024 * h, False, False)
         elif kind == "prc":
-            mm(pC(0, 2), [(nIb, Zc(h, 0, 128)), (nIb, Zc(h, 128, 256))], True, False)
-            acc(pC(1), [(cb("I2"), pH), (cb("I2"), tH), (Ib, A("CT", 0, 64))])
-            acc(pC(0), [(cf("If"), L("UF", h))])
+            to_blocks(h, last, False)
+            old_kids(h, last, nIb)
+        elif kind == "py":
+            for k in range(2):
+                mm(A("pZ", 128 + 192 * h + 32 * k, 160 + 192 * h + 32 * k), [(blocks("BR", k, c0), A("SP", 64 * h + c0, 64 * h + 64, 2)) for c0 in range(2)])
+        elif kind == "mj":
+            ts(Q("MK", h, 2), L("pZ", h, 2, 3), 6.0, ALU.is_lt)
+        elif kind == "mx":
+            ts(Q("MK", h, 0, 3), L("pZ", h, 0, 3, 3), 6.0, ALU.is_lt)
         elif kind == "pra":
             mm(go(0, 2), less(), True, False, True)
             acc(go(1), [(Ib, L("CM", h))])
         elif kind == "prb":
             if last:
-                acc(fx(0, 3), [(cb("I2"), Q("TN", h, 0, 3))])
+                acc(fx(0, 2), [(cb("I2"), Q("TN", h, 0, 2))])
             else:
                 acc(fx(0), [(cb("IDn"), pH), (cb("IDn"), tH)])
                 acc(fx(1), [(cb("UpI"), pK), (cb("UpI"), tK)])
@@ -437,43 +556,69 @@ def rank_program(g, core, T, topo):
                 acc(fx(0, 2), less())
                 acc(fx(0), [(cb("Dn"), pH), (cb("Dn"), tH)])
                 acc(fx(1), [(Ib, pK), (Ib, tK)])
-                acc(fx(2), [(cb("I2"), tF)])
-            acc(fx(0, 3), [(Ib, A("CT", 64, 256))])
+            acc(fx(2), [(cb("Ip"), tF), (Ib, A("CT"))])
         elif kind == "nr":
             ts(A("NR", 1024 * h, 1024 * h + 1024), A("D", 1024 * h, 1024 * h + 1024), C28, ALU.add, C28, ALU.is_equal)
+        elif kind == "nq":
+            ts(A("NR", 512 * h, 512 * h + 512), A("D", 512 * h, 512 * h + 512), C28, ALU.add, C28, ALU.is_equal)
         elif kind == "cnt":
-            rows2list(L("pA", h), 2, "NR", 1024 * h)
+            rows2list(pC(2, h), 2, "NR", 1024 * h)
+        elif kind == "uq":
+            cp(A("UQ"), IX(A(tf, 0, 8192), A("u16", 96, 128)), "S")
+        elif kind == "dq":
+            mm(A("pA"), [(Ib, A("UQ")), (nIb, A("FW", 1536, 2048))])
+        elif kind == "nz":
+            ts(A("NR", 1536, 2048), A("pA"), C28, ALU.add, C28, ALU.is_equal)
         elif kind == "sp":
-            ts(L("SP", h), L("pA", h), col(3), ALU.add, col(2), ALU.is_ge)
+            act(L("SP", h), pC(2, h), 0.875, col(2), None, ACT.Sign)
         elif kind == "pz":
-            mm(L("pZ", h, 0, 2), [(cb("B8I"), L("SP", h))])
-            mm(L("pZ", h, 1, 2), [(cb("nB4"), L("SP", h)), (Ib, cb("C20", 0, 64))])
+            mm(L("pZ", h, 0, 3), [(cb("B8I"), L("SP", h))])
+            mm(L("pZ", h, 1, 3), [(cb("nB4"), L("SP", h))])
         elif kind == "mk":
-            ts(Q("MK", h, 0, 2), L("pZ", h, 0, 2, 2), 11.0, ALU.is_lt, 4096.0, ALU.mult)
+            ts(Q("MK", h, 0, 2), L("pZ", h, 0, 3, 2), 6.0, ALU.is_lt)
         elif kind == "pk":
             mm(L("pZ", h, 6), [(Ib, cb("C16", 0, 64)), (cb("nhI"), ngo)])
         elif kind == "m":
             ts(L("m16", h), L("pZ", h, 6), col(1), ALU.add)
         elif kind == "kw":
-            wipe(pC(0), ngo); wipe(pC(1), ngo)
-            acc(pC(0, 2), [(Ib, Zc(h, 0, 128)), (Ib, Zc(h, 128, 256))], True)
+            for r in range(2 if last else 4):
+                wipe(pB(2, r, r + 1), Q("MK", h, 2), r == 3 and e == "V")
+            if last:
+                acc(pB(2, 0, 1), [(cb("I4k"), A("CT"))])
+            if e == "V" and not last:
+                op("X", [], [], [])
+            else:
+                old_kids(h, last, Ib, True)
         elif kind == "hi":
-            cp(Zc(h, 0, 128), pC(0, 2), e)
+            cp(Zc(h, 0), pC(h, 0, 2), e)
         elif kind == "lo":
-            tt(Zc(h, 128, 256), pC(0, 2), Zc(h, 0, 128), ALU.subtract)
+            tt(Zc(h, 1), pC(h, 0, 2), Zc(h, 0), ALU.subtract)
         elif kind == "tr":
-            op("P", [lambda cl=cl: g.tensor.transpose(T.pK[0:np_, :, 16 * cl:16 * cl + 16], T.Z[:, h, cl:256:NT], Ib[0])
-                     for cl in range(NT)], [pk], [Zc(h, 0, 256), Ib])
+            to_blocks(h, False, True)
         elif kind == "ks":
-            cp((T["KS%d" % h][0:np_, :, :], [("KS%d" % h, 0, 1)]), (T.pK[0:np_, :, 0:16 * NT], pk[1]), e or "V")
+            zr = A("ZR", 256 * h, 256 * h + 256)
+            if e == "V":
+                tt(zr, pB(2), zr, ALU.add)
+            else:
+                cp(zr, pB(2), e)
+        elif kind == "kv":
+            for c in range(4):
+                i = A("ZR", 256 * h + c, 256 * h + 256, 4)
+                op("V", [lambda c=c, i=i: g.vector.transpose(T.KS[:, h, :, c, :], i[0])], [(None, [("KS", h, h + 1, c)])], [i])
+        elif kind == "rk":
+            for k in range(2):
+                dma((T.KS[:, h, k, :, :], [("KS", h, h + 1)]), TK(0, 1024 * h, 1024 * h + 1024, slice(64 * k, 64 * k + 64, 4)), "ku0%d" % h, e or "Y")
+        elif kind == "rv":
+            for c in range(4):
+                o = A("ZR", 256 * h + c, 256 * h + 256, 4)
+                op("V", [lambda c=c, o=o: g.vector.transpose(o[0], T.KS[:, h, :, c, :])], [(None, [o[1][0] + (c,)])], [(None, [("KS", h, h + 1)])])
         elif kind == "kd":
-            kid_rows(t, h, 0, "Y")
+            kid_rows(t, h, 0, e or "Y")
         elif kind == "kt":
             kid_rows(t, h, 1, e or "Y")
         elif kind == "ku":
             c = 2048 + 1024 * h
-            dma((T.TK[1:128:4, c + 4096:c + 5120], [("TK", c + 4096, c + 5120)]), (T.TK[0:128:4, c:c + 1024], [("TK", c, c + 1024)]),
-                "ku%d%d" % (t, h), e or "Y")
+            dma(TK(1, c, c + 1024, slice(1, 128, 4)), TK(0, c, c + 1024, slice(0, 128, 4)), "ku%d%d" % (t, h), e or "Y")
         elif kind == "lw":
             for k in range(2):
                 wipe(go(k), ngo)
@@ -489,54 +634,47 @@ def rank_program(g, core, T, topo):
                                               T.sem["ls%d%d" % (t, h)], pid, rid, rmask)], [], [r], "ls%d%d" % (t, h), neng)
         elif kind == "flip":
             flip(A(tfn, 6144 + 1024 * h, 7168 + 1024 * h), A(tfn, 2048 + 1024 * h, 3072 + 1024 * h), e)
+        elif kind == "fq":
+            flip(A(tfn, 6144 + 512 * h, 6656 + 512 * h), A(tfn, 2048 + 512 * h, 2560 + 512 * h), e)
         elif kind == "par":
-            mm(A("pA", 384, 448), [(cb("EI8"), Q("MK", hh, 1)) for hh in range(2)])
+            mm(pC(3, 0), [(cb("EI8"), Q("MK", hh, 1)) for hh in range(2)])
         elif kind == "thr":
             if h == 0:
-                act(A("JK"), A("pA", 384, 448), bias=1.0 / 64, acc=col(3))
+                act(A("JK"), pC(3, 0), bias=-9.5 / 64, acc=col(3))
             elif h == 1:
-                act(col(4), col(3), 0.49995, C23)
+                act(col(4), col(3), 0.5, C23)
+            elif h == 2:
+                act(col(9), col(4), -2.0, 2 * C23 - 8.0)
             else:
-                act(col(2), col(4), 2.0, 10.0 - 2 * C23)
+                act(col(2), col(3), 1.0, col(9))
         elif kind == "yx":
-            dma(X(T.yx[:, 2048 + 1024 * h:3072 + 1024 * h]), A(tfn, 2048 + 1024 * h, 3072 + 1024 * h), "ox%d" % h)
+            dma(X(T.yx[:, 2048 + 512 * h:2560 + 512 * h]), A(tfn, 2048 + 512 * h, 2560 + 512 * h), "ox%d" % h, e or "Y")
         elif kind == "yt":
-            ts(L("YT", h, 0, 2), pC(0), 4096.0, ALU.is_ge, -8191.0, ALU.mult)
-            ts(L("YT", h, 1, 2), pC(1), 4096.0, ALU.is_ge, -8193.0, ALU.mult)
-        elif kind == "yu":
-            tt(L("YK", h, 0, 2, 2), pC(0, 2), L("YT", h, 0, 2, 2), ALU.add)
-        elif kind == "ytr":
-            op("P", [lambda cl=cl: g.tensor.transpose(T.pY[0:64, :, 32 * h + 16 * cl:32 * h + 16 * cl + 16],
-                                                      T.YK[:, 128 * h + cl:128 * h + 128:2], cf("If")[0])
-                     for cl in range(2)], [py], [L("YK", h, 0, 2, 2), cf("If")])
-        elif kind == "ys":
-            act(ys, (T.pY[0:64, :, 32 * h:32 * h + 32], py[1]), 1.0, col(7, 0, 64))
-        elif kind in ("yk", "yq"):
-            y, p = (T.y0, 0) if kind == "yk" else (T.y1, 32)
-            for gg in range(8):
-                dma(X(y[gg, 2048 + 1024 * h:3072 + 1024 * h]), (T.YS[p:p + 32, gg, 32 * h:32 * h + 32], ys[1]), "oy%d" % h, e or "Y")
-        elif kind == "eh":
-            ts(go(0, 2), Q(rb, h, 0, 2), 2048.0, ALU.is_ge, -4095.5, ALU.mult)
-        elif kind == "ei":
-            tt(L("EH", h, 0, 2, 2), go(0, 2), Q(rb, h, 0, 2), ALU.add)
-        elif kind == "ej":
             for k in range(2):
-                tt(L("FE", h, k, 2), L("EH", h, k, 2), Q(inb, h, 2), ALU.mult)
+                ts((T.YT[:, :, k, :], [("YT", k, k + 1)]), pB(2, k, k + 1), 0.0, ALU.is_lt, 8191.0 + 2 * k, ALU.mult)
+        elif kind == "yu":
+            tt(L("YK", h, 0, 2, 2), pB(2, 0, 2), (T.YT[:], [("YT", 0, 2)]), ALU.add)
+        elif kind == "ys":
+            o, i = A("YS", 128 * h, 128 * h + 128), L("YK", h, 0, 2, 2)
+            op("V", [lambda: g.vector.transpose(o[0], i[0])], [o], [i])
+        elif kind in ("yk", "yq"):
+            y, c = (T.y0, 128 * h) if kind == "yk" else (T.y1, 128 * h + 32)
+            for k in range(2):
+                dma(X(y[4 * k:4 * k + 4, 2048 + 1024 * h:3072 + 1024 * h]), A("YS", c + 64 * k, c + 64 * k + 32), "oy%d" % h, e or "Y")
         elif kind == "ybp":
             bank = T["pL%d" % h]
+
+            def back(k, n):
+                return [(cb(n), Q("PC", h, k)), (cb(n), Q("T2", h, k))]
             for b in range(2):
                 mm((bank[:, 0, 2:4, b:64:2], go(2, 2)[1]),
-                   [(cf("a%d" % b), L("EH", h, 0, 2)), (cf("b%d" % b), L("EH", h, 1, 2)),
-                    (cf("c%d" % b), L("FE", h, 0, 2)), (cf("d%d" % b), L("FE", h, 1, 2))])
+                   back(0, "c%d" % b) + back(1, "d%d" % b) + [(cb("e%d" % b), tF), (cb("f%d" % b), tF)] + back(0, "a%d" % b) + back(1, "b%d" % b))
         elif kind == "yfp":
             bank = T["pL%d" % h]
             for b in range(2):
-                mm((bank[0:8, 1, 2:4, b:64:2], fx(2, 2)[1]), [(cf("FT", 8 * b, 8 * b + 8), Q(rb, h, 2))])
+                mm((bank[0:8, 1, 2:4, b:64:2], fx(2, 2)[1]), [(cb("FT", 8 * b, 8 * b + 8), Q("TE", h, 2))])
         elif kind == "yb":
-            if e == "S":
-                act(A("YB", 128 * h, 128 * h + 128), go(2, 2), 1.0, 4096.0)
-            else:
-                ts(A("YB", 128 * h, 128 * h + 128), go(2, 2), 4096.0, ALU.add)
+            lin(A("YB", 128 * h, 128 * h + 128), go(2, 2), 1.0, 4096.0, e)
         elif kind == "yc":
             dma(X(T.yb[:, 128 * h:128 * h + 128]), A("YB", 128 * h, 128 * h + 128), "ob%d" % h, e or "Y")
         elif kind == "yf":

from concourse.mybir import AluOpType as ALU, ActivationFunctionType as ACT

F, B, I, U, H16 = "float32", "bfloat16", "int32", "uint16", "float16"
RO = 4
NT = 4
MF = ["If"]
MB = ["Ib", "nIb", "I2", "Ip", "I4k", "nhI", "Kp", "Kn", "Dn", "IDn", "UpI", "B8I", "nB4", "EI8", "CC", "C16", "C20",
      "a0", "a1", "b0", "b1", "c0", "c1", "d0", "d1", "e0", "e1", "f0", "f1", "FT"]
MY = ["E", "O", "OE", "SO", "GP", "GN"]
SCRATCH = {
    "TF0": ("sbuf", [128, 10240], B), "TF1": ("sbuf", [128, 10240], B), "TK": ("sbuf", [128, 8192], B),
    "G": ("sbuf", [128, 2048], B), "FW": ("sbuf", [128, 2048], B), "D": ("sbuf", [128, 2048], B), "NR": ("sbuf", [128, 2048], B),
    "IN0": ("sbuf", [128, 2, 3, 64], F), "IN1": ("sbuf", [128, 2, 3, 64], F), "IN2": ("sbuf", [128, 2, 3, 64], F), "IN3": ("sbuf", [128, 2, 3, 64], F),
    "R0": ("sbuf", [128, 2, 3, 64], F), "R1": ("sbuf", [128, 2, 3, 64], F), "R2": ("sbuf", [128, 2, 3, 64], F), "R3": ("sbuf", [128, 2, 3, 64], F),
    "TN": ("sbuf", [128, 2, 3, 64], B), "TE": ("sbuf", [128, 2, 3, 64], B), "T2": ("sbuf", [128, 2, 2, 64], B), "PC": ("sbuf", [128, 2, 2, 64], H16),
    "X16": ("sbuf", [128, 2, 2, 64], U), "MK": ("sbuf", [128, 2, 3, 64], B),
    "Z": ("sbuf", [128, 2, 256], B), "SP": ("sbuf", [128, 128], B),
    "u16": ("sbuf", [128, 128], U), "m16": ("sbuf", [128, 128], U),
    "UQ": ("sbuf", [128, 512], B), "WB": ("sbuf", [128, 4096], B), "MG": ("sbuf", [128, 128], B), "ZR": ("sbuf", [128, 512], B), "KS": ("sbuf", [128, 2, 2, 4, 32], B),
    "EI": ("sbuf", [128, 512], I), "SI": ("sbuf", [128, 1024], I), "FI": ("sbuf", [128, 256], I),
    "p16": ("sbuf", [128, 128], U), "PS": ("sbuf", [128, 768], H16), "KP": ("sbuf", [128, 512], B), "FF": ("sbuf", [128, 512], B),
    "KF": ("sbuf", [128, 256], F), "IO2": ("sbuf", [128, 128], F), "YM": ("sbuf", [128, 144 * len(MY)], B),
    "CF": ("sbuf", [128, 128 * len(MF)], F), "CB": ("sbuf", [128, 128 * len(MB)], B), "CH": ("sbuf", [128, 256], H16),
    "CM": ("sbuf", [128, 128], H16), "CT": ("sbuf", [128, 64], B), "W": ("sbuf", [128, 4 * 144], B),
    "ZB": ("sbuf", [128, 160], B), "RL": ("sbuf", [128, 320], B), "BR": ("sbuf", [128, 320], B), "ONE": ("sbuf", [128, 512], B),
    "COL": ("sbuf", [128, 40], F), "COI": ("sbuf", [128, 16], I), "JK": ("sbuf", [128, 64], F),
    "YB": ("sbuf", [128, 256], F), "YF": ("sbuf", [128, 256], F),
    "YT": ("sbuf", [128, 2, 2, 32], F), "YK": ("sbuf", [128, 256], F), "YS": ("sbuf", [128, 256], F),
    "pA": ("psum", [128, 512], F), "pZ": ("psum", [128, 512], F), "pL0": ("psum", [128, 2, 4, 64], F), "pL1": ("psum", [128, 2, 4, 64], F),
    "pV0": ("psum", [128, 512], F), "pV1": ("psum", [128, 512], F), "pK": ("psum", [128, 4, 4, 32], F), "pY": ("psum", [128, 8, 64], F),
}
DSEM = ["dk", "db", "df", "dp", "dv", "kd", "dc0", "dc1", "df1", "dn1", "dn2", "dn3", "dyx", "dy", "ox0", "ox1", "ox2", "ox3", "ob0", "ob1", "oy0", "oy1", "of"] \
    + ["%s%d%d" % (k, t, h) for k in ("kc", "ku") for t in range(3) for h in range(2)]
SEMAPHORES = ["sV", "sS", "sP", "sG"] + DSEM + ["%s%d%d" % (k, t, h) for k in ("ls", "rs") for t in range(3) for h in range(2)]
C23 = 12582912.0
C28 = 402653184.0
BIG = 2.0 ** 40
SB = 2.0 ** -13

FIRST = """load zero io tk0 ga0 tk2 tk1 cols tk3 ga1 an0 ka0 ka1 ka2 ka3 kh0 kh1S kh2 kh3S kl0 kl1S kl2 kl3S ga2 an1 ba0 nf ba1 ba2 eye
    eo0 xf0 fa0S ffV eo1 eg xf1 in0S in1S gb0 fa1V sa0S tn2 dv fa2V fa3V gb1 gc0 vc pc2 sa1S gc1 ge gd
    K12S K01V up0 vb0 va vb1 vb2 pra0 H02S op0 oh0V op1 oh1V ol1 ol0 u0 U01 pra1 K24S a0 af0 U12 af1 nr0 ad0 sa3S sa2S
    up1 ad1 u1 ac0 H24S cnt0 sp0 bg1 prb0 U34 pz0 mk0 ac1 ev0S af2 bg0 lw0 pk0 ev1S U23 uf0S r0 uf1S af3 s0 ad3V prc0
    kw0 ad2 nr1 cnt1 ac2 m0 hi0V lo0 S02S ev2S tr0 sp1 pz1 mk1 a1 ar0+ prc1 ks0 pk1 par kw1 thr0 thr1 kd0 ev3V m1 hi1V
    prb1 lo1 lw1 r1 S34S S23S s1 tr1 ks1 kd1 flip0 x0+ tn0+ pc0+ flip1 pra0+ thr2 ku0 kt1S prb0+"""
MIDDLE = """ar1 H12S H01V K12S af0 K01V af1 x1 K24S up0 tn1 pc1 a0 u0 U01 pra1 H24S up1 ad0 U12 u1 nr0 U23 uf0S ac0 uf1S
    ad1 ac1 cnt0 sp0 ev1S prc0 af3 pz0 U34 prb1 mk0 lw0 nr1 pk0 r0 s0 ar0+ kw0 cnt1 m0 ev0S hi0S lo0 ad3V af2 tr0 sp1
    pz1 ad2 ev3V a1 mk1 par ks0 out0 ac2 lw1 r1 kd0 S02S prc1 s1 thr0 thr1 ku0 ev2S kw1 hi1V thr2 pk1 m1 lo1 tr1
    flip0 ks1 tn0+ S23S kd1 pc0+ pra0+ S34S x0+ prb0+ flip1 kt1S out2 out1"""
LAST = """K01V ar1 x1 K12S H01V up0 a0 H12S af1 K24S tn1 af0 u0 up1 U12 ad1 U01 pc1 ad0 H24S ac0 pra1 prb1 nr0 cnt0
    u1 U23 ev0S uf1S sp0 ac1 a1 uf0S U34 pz0 mk0 nr1 prc0 af2 lw0 ev1S pk0 kw0 r0 m0 S02S yt0 cnt1 s0 sp1 yu0 te0 ad2
    af3 pz1 mk1 ac2 tz0 pe0 ytr0 lw1 ys0 pk1 ad3 r1 ac3 yx0 yx1 prc1 s1 te1 tz1 m1 pe1 kw1 ev2S yt1 ybp0 yb0V yk0 yu1 ev3S
    S24S ybp1 yq0 ytr1 yfp0 ys1 yc0 yb1V yc1 yx2 yx3 yfp1 yq1S yf0V yk1 yf1V yg"""
FIRST = """zero load io tk0 sa3S gc0 eye sa0S cols an0 ka0 bm0 sa1S tk1 an1 ka1 dv nf ga0 ka2 ba0 ba2 ga1 ffS bm1 ga2 fa1S ka3 ba1 eg vc eo2 eo1 eo0 vb0 fa2S gb1 gb0 fa3V gc1 vb1 kh0 kh1 in1V fa0S kl0 xk kl1 bg0 xf1 in0V vb2 op0 H02S va K12V bk1 op1 K01V oh0V ge up0 tn2 pc2 oh1S ol0 u0 uf0V U12 K24S pra0 af0 prc0 U01 bg1 a0 up1 nr0 bk0 ad0 gd ol1 cnt0 H24S af1 u1 ad1 sp0 pz0 U34 ac1 ev1S ac0 mk0 ev0S pra1 kw0 U23 hi0S nr1 prb0 sa2S lw0 af3 r0 uf1S lo0 af2 cnt1 pk0 prc1 s0 sp1 tr0 ad2 m0 pz1 mk1 ac2 ks0S ad3V kw1 prb1 kd0 pk1 hi1V lo1 a1 tr1 m1 ev3V ks1V ar0+ S02S ev2S S23S lw1 r1 s1 flip0V kd1 par S34V tn0+ thr0 flip1V thr1 kt1 pc0+ pra0+ thr2 x0+ ku0 prb0+"""
MIDDLE = """H01V H12S ar1 K01V af1 x1 K12S tn1 K24S af0 pc1 up0 u0 U01 a0 pra1 U12 up1 H24S u1 ad0 nr0 uf1V U23 ad1 ac1 ac0 cnt0 sp0 uf0S U34 prc0 pz0 mk0 ev1S nr1 prb1 af3 pk0 lw0 kw0 ev0S m0 hi0S cnt1 r0 s0 lo0 sp1 ad3V tr0 af2 ev3V pz1 ks0V ar0+ mk1 out0 a1 ad2 S02S lw1 r1 kd0 s1 prc1 pk1 kw1 ac2 hi1V ku0 m1 lo1 tr1 par flip0S ev2S ks1V S23S tn0+ thr0 kd1 kt1 S34V pc0+ out2 out1 pra0+ thr1 prb0+ flip1V x0+ thr2"""
LAST = """H01V H12S K01V ar1 af1 K12S up0 tn1 x1 u0 U01 af0 a0 K24S up1 H24S U12 pc1 ad0 ad1 u1 uf1S ac0 nr0 ev0S pra1 ac1 uf0S U23 cnt0 prb1 a1 sp0 pz0 af2 prc0 U34 mk0 nr1 ev1S lw0 kw0 cnt1 pk0 r0 yt0 af3 ad2 s0 te0 sp1 m0 yu0 pe0 pz1 mk1 ytr0 lw1 ac2 ys0V S02S r1 ad3 yk0 s1 tz0 pk1 ac3 prc1 ev2S te1 m1 pe1 kw1 yx1 tz1 yt1 ybp0 yfp1 yb0V ev3S yx0 S24S ybp1 yq0 yu1 yfp0 yb1V yc0 yc1 yx3S yf1V yf0V ytr1 ys1S yq1S ygS yx2 yk1"""
FIRST = """zero cols io tk0 gc0 eye load sa0V an0 sa3S ga1 ka0 nf ga2 ka1 an1 ka2 dvS ga0 ba2 bm0 tk1 kh0 gb1 ffS vb0 eg bm1 eo2 ba0 gc1 sa1S ka3 gb0 kh1S kl0 va ba1 gd fa3V eo1 kl1 fa1S eo0 vc xf1 op1 in1V fa0S fa2S xk K01V op0 in0V K12V H02S tn2 bg0 oh1S pc2 up0 K24S oh0V vb1 ol0 u0 vb2 uf0V U01 af0 H24S prc0 up1 ol1 pra0 ge U12 u1 af1 bk0 ad0 nr0 a0 U34 ac0 cnt0 ev0S sp0 ad1 pz0 prb0 U23 mk0 sa2S ac1 ev1S lw0 nr1 kw0 r0 pk0 hi0S s0 ar0+ lo0 zz0V af2 m0 af3 cnt1 tr0 sp1 pra1 uf1S pz1 prc1 ad2 ks0V mk1 kw1 ad3V ac2 hi1V bg1S pk1 a1 kt0 lo1 ev3V prb1 zz1V S02S tr1 flip0V lw1 m1 ks1V ev2S par r1 s1 S23S kd0 S34V kd1 kt1 tn0+ pc0+ thr0 pra0+ prb0+ thr1 thr2 x0+ flip1V"""
MIDDLE = """H01S ar1 H12V K01V K12S x1 af0 af1 tn1 pc1 K24S up0 u0 pra1 U01 a0 H24S up1 U12 u1 nr0 U23 ad0 uf1S ad1 ac1 ac0 cnt0 uf0S sp0 ev1S prc0 U34 pz0 prb1 out2 mk0 af3 nr1 lw0 kw0 pk0 ev0S cnt1 r0 ad3V m0 hi0S s0 ar0+ S02S out0 lo0 sp1 a1 prc1 pz1 zz0V af2 ev3V tr0 mk1 lw1 kw1 ks0V pk1 r1 hi1V kd0 kt0 ad2 m1 ac2 ev2S par lo1 S23S tn0+ zz1V tr1 s1 ks1V S34V pc0+ flip0V pra0+ kd1 x0+ kt1S thr0 thr1 flip1V thr2 prb0+ out1"""
LAST = """ar1 H12S H01V K12S K01V af0 af1 x1 tn1 pc1 K24S up0 u0 U01 a0 pra1 H24S up1 U12 ad0 ac0 u1 uf0V ad1 ac1 ev0S prb1 uf1V nr0 ev1S cnt0 U23 sp0 a1 pz0 U34 mk0 af2 prc0 nr1 kw0 pk0 lw0 cnt1 af3 yt0 m0 yu0 ad2 r0 sp1 s0 pz1 mk1 ytr0 lw1 S02S ac2 ys0V pk1 ad3 te0 ac3 r1 ev2S s1 te1 m1 prc1 tz1 tz0 kw1 pe0 ybp0 yx1 ev3S yt1 yq0 pe1 yx0S yk0 ybp1 yfp1 yu1 yb0V S24S yc0 yb1V ytr1 yx2S yx3S yf1V yfp0 yf0S yc1S ys1V yg yq1S yk1"""
FIRST = """zero load io tk0 sa3S gc0 eye sa0S cols an0 ka0 bm0 sa1S tk1 an1 ka1 dv nf ga0 ka2 ba0 ba2 ga1 ffS bm1 ga2 fa1S ka3 ba1 eg vc eo2 eo1 eo0 vb0 fa2S gb1 gb0 fa3V gc1 vb1 kh0 kh1 in1V fa0S kl0 xk kl1 bg0 xf1 in0V vb2 op0 H02S va K12V bk1 op1 K01V oh0V ge up0 tn2 pc2 oh1S ol0 u0 uf0V U12 K24S pra0 af0 prc0 U01 bg1 a0 up1 nr0 bk0 ad0 gd ol1 cnt0 H24S af1 u1 ad1 sp0 pz0 U34 ac1 ev1S ac0 mk0 ev0S pra1 kw0 U23 hi0S nr1 prb0 sa2S lw0 af3 r0 uf1S lo0 af2 cnt1 pk0 prc1 s0 sp1 tr0 ad2 m0 pz1 mk1 ac2 ks0S ad3V kw1 prb1 kd0 pk1 hi1V lo1 a1 tr1 m1 ev3V ks1V ar0+ S02S ev2S S23S lw1 r1 s1 flip0V kd1 par S34V tn0+ thr0 flip1V thr1 kt1 pc0+ pra0+ thr2 x0+ ku0 prb0+"""
MIDDLE = """H01V H12S ar1 K01V af1 x1 K12S tn1 K24S af0 pc1 up0 u0 U01 a0 pra1 U12 up1 H24S u1 ad0 nr0 uf1V U23 ad1 ac1 ac0 cnt0 sp0 uf0S U34 prc0 pz0 mk0 ev1S nr1 prb1 af3 pk0 lw0 kw0 ev0S m0 hi0S cnt1 r0 s0 lo0 sp1 ad3V tr0 af2 ev3V pz1 ks0V ar0+ mk1 out0 a1 ad2 S02S lw1 r1 kd0 s1 prc1 pk1 kw1 ac2 hi1V ku0 m1 lo1 tr1 par flip0S ev2S ks1V S23S tn0+ thr0 kd1 kt1 S34V pc0+ out2 out1 pra0+ thr1 prb0+ flip1V x0+ thr2"""
LAST = """H01V H12S K01V ar1 af1 K12S up0 tn1 x1 u0 U01 af0 a0 K24S up1 H24S U12 pc1 ad0 ad1 u1 uf1S ac0 nr0 ev0S pra1 ac1 uf0S U23 cnt0 prb1 a1 sp0 pz0 af2 prc0 U34 mk0 nr1 ev1S lw0 kw0 cnt1 pk0 r0 yt0 af3 ad2 s0 te0 sp1 m0 yu0 pe0 pz1 mk1 ytr0 lw1 ac2 ys0V S02S r1 ad3 yk0 s1 tz0 pk1 ac3 prc1 ev2S te1 m1 pe1 kw1 yx1 tz1 yt1 ybp0 yfp1 yb0V ev3S yx0 S24S ybp1 yq0 yu1 yfp0 yb1V yc0 yc1 yx3S yf1V yf0V ytr1 ys1S yq1S ygS yx2 yk1"""
FIRST = """load zero io ga2 sa3S eye cols sa1S tk0 an0 sa0S ka0 an1 ka1 tk1 nf ga1 ka2 dv ffS kh0 bm0 ka3 bm1 ba2 ga0 gc0 fa2S gb0 ba0 vb0 kh1 fa1S ba1 fa0S vb1 fa3V eo2 eo1 eg kl1 gb1 eo0 kl0 bg0S vc va xf1 op0 xk bk1 op1 H02S in1V in0V oh0S K12V vb2 tn2 K01V K24S H24S up0 ol0 oh1S pc2 af0 u0 gc1 pra0 uf0V ge U12 prc0 gd up1 U01 pra1 gr bk0 u1 a0 nr0 ol1 ad0 ac0 cnt0 sp0 af1 U34 ev0S ad1 ac1 bg1 pz0 mk0 ev1S af2 prb0 U23 nr1 uf1S kw0 hi0S lw0 ad2 af3 r0 cnt1 lo0 s0 sa2S sp1 tr0 prc1 pk0 ks0S pz1 ac2 mk1 ad3V kw1 m0 kv0 hi1V pk1 m1 prb1 lo1 kt0 tr1 S02S a1 kd0 ev3V lw1 ks1V kv1 ev2S r1 s1 S34V ar0+ S23S par flip0V thr0 tn0+ flip1V thr1 kt1 x0+ pc0+ pra0+ kd1 prb0+ thr2"""
MIDDLE = """H12S H01V K01V ar1 x1 K12S af0 tn1 af1 K24S up0 H24S pc1 pra1 u0 U01 a0 U12 up1 ad0 uf1V ac0 u1 ev0S ad1 uf0S nr0 ac1 cnt0 U23 prc0 sp0 U34 ev1S pz0 mk0 nr1 prb1 af3 ad3V pk0 lw0 m0 kw0 cnt1 hi0S r0 af2 s0 lo0 sp1 tr0 pz1 S02S prc1 a1 ev3V ks0V mk1 lw1 par kw1 kv0 r1 hi1V ad2 lo1 ac2 thr0 s1 pk1 tr1 out0 ks1V ev2S m1 kv1 thr1 kt0 kd0S ar0+ S34V S23S x0+ kd1 tn0+ pc0+ pra0+ prb0+ flip0S kt1 out1 thr2 flip1V out2"""
LAST = """ar1 H12S K12S H01V K01V af1 up0 tn1 x1 K24S u0 a0 af0 U01 up1 H24S U12 ad0 u1 ac0 pc1 ad1 nr0 pra1 prb1 U23 ac1 cnt0 sp0 uf1S a1 uf0S ev0S U34 pz0 mk0 af2 prc0 lw0 nr1 ev1S pk0 kw0 cnt1 m0 yt0 yu0 sp1 r0 af3 ad2 pz1 ytr0 mk1 lw1 s0 S02S ys0 ac2 r1 te0 pk1 s1 m1 ev2S tz0 pe0 ad3 te1 ac3 ev3S prc1 tz1 yx1 yx0 kw1 pe1 ybp0 yt1 yb0V yfp1 S34S ybp1 yk0 yq0 S23S yu1 yfp0 yc0 yb1V yx3 yc1 ytr1 yf1V yf0V ys1 yg yq1S yk1 yx2"""
FIRST = """load io eye sa2S zero gc0 tk0 cols an0 ga2 ga1 ga0 vb0 ka0 an1 sa0S ka1 bm0 ka2 nf ka3 ba0 ba2 bm1 ffV ba1 vc fa1V tk1 eo2 gb0 kh0S gc1 vb1 kh1 kl1 kl0 gr sa1S eg eo1 xk fa3V fa2S fa0S eo0 K12S in1V in0V tn2 dv xf1 vb2 va K01S pc2 up0 pra0 ph0 ge rk0 K24V rk1 bk1 H02S u0 hi0V ph1 af0 af1 up1 U01 U12 gd ad0 u1 rv0 lo0 ad1 bg0 br sa3S H24S bsS nr0 ac1 pra1 prc0 U23 cnt0 hi1S sp0 a0 U34 py0 ac0 pz0 mk0 prb0 lw0 mj0 ev1S ev0S nr1 pk0 r0 kw0 m0 s0 cnt1 prb1 af3 ad3V ks0V sp1 pz1 kv0 mk1 a1 py1 ev3V af2 lw1 mj1 lo1 pk1 ad2 S02S rv1 prc1 kw1 r1 m1 flip0S ar0+ s1 ac2 bk0 bg1 kt0 par kd0S ks1V kv1 ev2S S34V S23S kd1 kt1 thr0 flip1V thr1 tn0+ x0+ pc0+ pra0+ thr2 prb0+"""
MIDDLE = """H12S K12S ar1 out2 ph0 af1 H01V tn1 K01V x1 up0 pc1 a0 u0 hi0V K24S pra1 U01 U12 prb1 up1 af0 u1 lo0 nr0 ad1 ph1 ac1 ad0 H24S U23 cnt0 sp0 ac0 hi1S ev1S pz0 U34 py0 prc0 af3 mj0 kw0 mk0 nr1 lw0 lo1 pk0 cnt1 r0 m0 s0 ev0S ad3V ks0S sp1 prc1 ev3V py1 pz1 mk1 a1 ar0+ lw1 S02S mj1 out0 kw1 par af2 ks1S pk1 thr0 kv0 r1 out1 ad2 kd0 ac2 s1 kt0 ev2S m1 kv1 flip0V thr1 S23S kd1 kt1 thr2 tn0+ S34V x0+ flip1V pc0+ pra0+ prb0+"""
LAST = """ph0 H12S ar1 K12S H01V af0 tn1 af1 K01V up0 x1 a0 pc1 u0 K24S hi0V lo0 ph1 H24S U12 U01 pra1 up1 ad1 a1 u1 ad0 nr0 U23 ac0 cnt0 sp0 prc0 U34 ev0S py0 prb1 af2 pz0 ac1 ad2 mj0 ev1S kw0 mk0 nr1 pk0 m0 lw0 cnt1 yt0 r0 yu0 hi1S sp1 af3 pz1 ys0 S02S mk1 s0 lo1 ad3 ac2 py1 tz0 mj1 lw1 prc1 yk0 r1 yq0 yx1 kw1 te0 pe0 ev2S ac3 yx0 pk1 yt1 yfp0 ybp0 s1 yu1 ev3S tz1 te1 ys1 m1 yq1 S34S yb0V pe1 yc0 yk1 yfp1 S23V ybp1 yf0S yx3 yb1V yx2 yf1V yc1S yg"""
FIRST = """load dvS io cols zero gc0 ga2 ga0 ga1 eye vb0 sa2S tk0 an0 ka0 an1 ka1 sa0S ba2 ka2 ba0 ka3 bm0 nf bm1 ffV ba1 vc vb1 tk1 eo2 gb0 gc1 eo0 eg eo1 kh1 kh0 kl0 kl1 fa0S fb0 fa1S fb1 sa1S vaS xk vb2 K01V in1V sa3V xf1 K12S up0 u0 in0S tn2 H12S pc2 rk0 pra0 ph0 ge gr K24S rk1 bk1 ph1 H01V rv0 hi0V af1 af0 up1 U12 ad1 pra1 U01 u1 lo0 gd bg0 H24S nr0 ac1 br ad0 prc0 hi1S bsS ac0 cnt0 sp0 a0 pz0 py0 U34 U23 prb0 mx0 ev1S ev0S nr1 lw0 pk0 r0 kw0 m0 s0 cnt1 prb1 sp1 ks0V kv0 pz1 py1 af3 mx1 ad3V a1 lw1 pk1 rv1 lo1 prc1 kw1 af2 ad2 S02S ev3V r1 gw0 m1 flip0S ar0+ s1 gw1 gw2 gw3 ac2 bk0 bg1 kt0 par kd0 ks1V kv1 ev2S S34V kt1 kd1 thr0 S23S thr1 tn0+ x0+ flip1V pc0+ pra0+ thr2 thr3 prb0+"""
MIDDLE = """H12S ar1 H01V K01V K12S tn1 x1 ph0 af1 af0 up0 a0 pc1 hi0V u0 pra1 lo0 K24S prb1 up1 ph1 U02 u1 prc0 nr0 ad0 ac0 ad1 cnt0 ac1 H24S ev0S U23 U34 sp0 ev1S hi1S bf0 py0 pz0 bo0 mx0 lo1 nr1 a1 bf1 lw0 pk0 kw0 cnt1 bo1 m0 r0 out0 bd1 ks0S s0 kv0 sp1 pz1 py1 mx1 out1 mg bd0 prc1 lw1 par kw1 bw0S S02S ar0+ kt0 kd0 thr0 thr1 be0S r1 ks1V s1 kv1 bw1S tn0+ be1S flip0V pc0+ x0+ flip1V thr2 thr3 pra0+ prb0+ kd1 kt1 out2"""
LAST = """ph0 H12S ar1 K12S H01V af0 tn1 af1 K01V up0 x1 a0 pc1 hi0V u0 K24S lo0 pra1 prb1 ph1 up1 H24S U01 U12 u1 ad0 ac0 a1 ad1 nr0 U23 U34 cnt0 ev0S sp0 prc0 pz0 py0 af2 ac1 ad2 mj0 kw0 mk0 nr1 pk0 m0 yt0 lw0 hi1S cnt1 ev1S r0 yu0 sp1 af3 ac2 pz1 ys0 S02S mk1 lo1 s0 ad3 py1 mj1 tz0 lw1 prc1 yk0 r1 yq0 yx1 kw1 te0 ev2S ac3 yx0 pk1 s1 yt1 pe0 yfp0 ybp0 yu1 ev3S tz1 te1 ys1 m1 yq1 S34S yb0V pe1 yk1 yc0 yfp1 S23V ybp1 yf0S yx3 yb1V yx2S yf1V yc1 yg"""
FIRST = """load dvS io gc0 cols zero eye ga0 ga1 ga2 sa2S tk0 an0 vb0 ka0 bm0 an1 ka1 sa0S bm1 ka2 ba2 nf ka3 vb1 ba0 ffV tk1 eo2 gb0 gc1 eg kh0 kh1 kl0 kl1 fa0S fb0S fa1S fb1 sa1S vaS ba1 vc eo1 eo0 xk vb2 sa3V K01V in1V xf1 K12S up0 u0 in0S tn2 H12S pc2 rk0 pra1 ph1 ph0 pra0 ge gr K24S rk1 bk1 H01V U12 hi0S rv0 af1 af0 ad1S br up1 ac1S U01 lo0 u1 gd bg0 H24S nr0 ad0S prc0 bsS cnt0 sp0 a0 hi1S pz0 py0 U34 U23 prb0 ac0S mx0 ev1S ev0S nr1 lw0 r0 kw0V pk0 m0 cnt1 prb1 sp1 ks0V s0 kv0 py1 pz1 af3 ad3V mx1 a1 pk1 lw1 ac3V rv1 lo1 prc1 kw1V af2 ad2S S02S ev3V r1 m1 flip0S ar0+ s1 ac2S bk0 bg1 kt0 par kd0 ks1V kv1 ev2S S34V kt1 kd1 thr0 S23S thr1 tn0+ x0+ flip1V pc0+ pra0+ thr2 thr3 prb0+ ph0+"""
MIDDLE = """ar1 H01V K01V x1 H12S K12S tn1 af1 out2 K24S H24S out0 pc1 up0 af0 hi0V u0 lo0 pra1 prb1 U12 U01 ph1 prc0 up1 ad1S ac1S ad0S u1 nr0 U23 U34 ac0S cnt0 a0 ev1S sp0 hi1S pz0 py0 mx0 nr1 lo1 af3 ev0S ad3V pk0 lw0 kw0V r0 ks0V cnt1 m0 s0 prc1 sp1 S02S kv0 py1 pz1 ac3V mx1 af2 a1 pk1 lw1 kw1S ad2S ev3V m1 r1 flip0V ks1S ac2S par ev2S thr0 kv1 s1 ar0+ S23S thr1 tn0+ out1 kd0 kt0 S34V x0+ flip1V pc0+ ph0+ pra0+ prb0+ thr2 thr3 kd1 kt1"""
LAST = """H12S ar1 K12S H01V af0 tn1 af1 K01V up0 x1 pc1 a0 u0 hi0V K24S ph1 pra1 prb1 up1 H24S U12 U01 u1 lo0 nr0 a1 ad0S ac0S ad1V U23 U34 cnt0 ev0S sp0 prc0 py0 pz0 ac1V af2 mj0 kw0S mk0 nr1 pk0 lw0 cnt1 ad2V m0 yt0 ev1V yu0 r0 sp1 hi1S ac2V af3 pz1 py1 ad3S S02S ys0 lo1 mk1 mj1 s0 prc1 lw1 yk0 ev2V tz0 te0 r1 kw1S pe0 yt1 yq0 yx1 ac3S yx0 pk1 s1 yfp0 ybp0 yu1 ev3S te1 m1 ys1 tz1 pe1 S34S yb0V yk1 yq1 yc0S yfp1 S23V ybp1 yf0S yx3 yb1V yx2 yf1V yc1 yg"""
ORDER = [FIRST, MIDDLE, MIDDLE, LAST]


def rank_program(g, core, T, topo):
    rank = T.rank_of(core)
    if rank is None:
        return
    nxt = T.cores[(rank + 1) % len(T.cores)]
    rid, pid, _se = topo.addr(nxt)
    rmask = topo.mask(core, nxt)
    neng = len(topo.engines(core, nxt))
    ops = []
    tag = [""]

    def A(n, c0=None, c1=None, st=1, p0=0, p1=128):
        if c0 is None:
            c0, c1 = 0, SCRATCH[n][1][-1]
        return (T[n][p0:p1, c0:c1] if st == 1 else T[n][p0:p1, c0:c1:st], [(n, c0, c1)])

    def L(n, h, k=0, per=1, w=1):
        return A(n, 64 * k, 64 * k + 128) if h == 2 else A(n, 64 * (per * h + k), 64 * (per * h + k + w))

    def Q(n, h, k, w=1):
        a, b = (slice(0, 2) if h == 2 else h), (k if w == 1 else slice(k, k + w))
        return (T[n][:, a, b, :], [(n, 256 * j + 64 * k, 256 * j + 64 * (k + w)) for j in ((0, 1) if h == 2 else (h,))])

    def Zc(h, k):
        return (T.Z[:, h, 128 * k:128 * k + 128], [("Z", 256 * h + 128 * k, 256 * h + 128 * k + 128)])

    def TK(turn, c0, c1, rows=slice(0, 128), st=1, key=()):
        return (T.TK[rows, 4096 * turn + c0:4096 * turn + c1:st], [("TK", 4096 * turn + c0, 4096 * turn + c1) + key])

    def pC(h, k, w=1):
        return (T.pY[:, 2 * h + k:2 * h + k + w, :], [("pY", 128 * h + 64 * k, 128 * h + 64 * (k + w))])

    def pB(k, r0=0, r1=4):
        return (T.pK[:, slice(0, 2) if k == 2 else k, r0 if r1 == r0 + 1 else slice(r0, r1), :], [("pK", 0, 512)])

    def IX(win, off):
        return (win[0].indirect(off[0]), win[1] + off[1])

    def cf(n, c0=0, c1=128, st=1, p1=128):
        k = 128 * MF.index(n); return A("CF", k + c0, k + c1, st, 0, p1)

    def cb(n, c0=0, c1=128, st=1, p0=0, p1=128):
        k = 128 * MB.index(n); return A("CB", k + c0, k + c1, st, p0, p1)

    def col(k, p0=0, p1=128):
        return A("COL", 4 * k, 4 * k + 1, 1, p0, p1)

    def op(e, fns, outs, ins, sem=None, n=1):
        ops.append({"e": e, "fns": fns, "w": [r for a in outs for r in a[1]], "r": [r for a in ins for r in a[1]],
                    "sem": sem, "n": n, "tag": tag[0]})

    def sa(x):
        return x[0] if isinstance(x, tuple) else x

    def aps(*xs):
        return [x for x in xs if isinstance(x, tuple)]

    def ts(o, i, s1, o0, s2=None, o1=None):
        if o1 is None:
            op("V", [lambda: g.vector.tensor_scalar(o[0], i[0], sa(s1), None, o0)], [o], aps(i, s1))
        else:
            op("V", [lambda: g.vector.tensor_scalar(o[0], i[0], sa(s1), sa(s2), o0, o1)], [o], aps(i, s1, s2))

    def tt(o, a, b, o0):
        op("V", [lambda: g.vector.tensor_tensor(o[0], a[0], b[0], o0)], [o], [a, b])

    def ms(o, c):
        op("V", [lambda: g.vector.memset(o[0], c)], [o], [])

    def act(o, i, scale=1.0, bias=0.0, acc=None, func=None):
        if acc is not None:
            op("S", [lambda: g.scalar.activation(o[0], i[0], ACT.Identity, bias=bias, accum_out=acc[0])], [o, acc], [i])
        elif bias == 0.0:
            op("S", [lambda: g.scalar.activation(o[0], i[0], ACT.Copy, scale=scale)], [o], [i])
        else:
            op("S", [lambda: g.scalar.activation(o[0], i[0], func or ACT.Identity, bias=sa(bias), scale=scale)], [o], aps(i, bias))

    def cp(o, i, e="V"):
        if e == "S":
            act(o, i)
        else:
            op("V", [lambda: g.vector.tensor_copy(o[0], i[0])], [o], [i])

    def lin(o, i, a, b, e="V"):
        if e == "S":
            act(o, i, a, b)
        else:
            ts(o, i, a, ALU.mult, b, ALU.add)

    def flip(o, i, e="V"):
        lin(o, i, -1.0, 255.0, e)

    def mm(o, terms, start=True, stop=True, whole=False):
        op("P", [lambda l=l, r=r, k=k: g.tensor.matmul(o[0], l[0], r[0], start and k == 0, stop and k == len(terms) - 1)
                 for k, (l, r) in enumerate(terms)], [o] + ([(None, [(o[1][0][0], 0, 512)])] if whole else []), [a for lr in terms for a in lr])

    def acc(o, terms, stop=False):
        mm(o, terms, False, stop, stop)

    def wipe(o, mask, stop=False):
        acc(o, [(cb("Kp"), mask), (cb("Kn"), mask)], stop)

    def dma(o, i, sem, q="Y"):
        op(q, [lambda: (g.sync if q == "Y" else g.scalar).dma_start(o[0], i[0])], [o], [i], sem, 16)

    def X(ap):
        return (ap, [])

    def iota(o, pat, base, cm):
        op("G", [lambda: g.iota(o[0], pat, base, cm, allow_small_or_imprecise_dtypes=True)], [o], [])

    def sel(o, i, pat, base, fill, cmp=ALU.not_equal, cm=1):
        op("G", [lambda: g.affine_select(o[0], i[0], pat, cmp, fill, base, cm)], [o], [i])

    def Wm(k, c0=0, c1=144, st=1):
        return A("W", 144 * k + c0, 144 * k + c1, st)

    def wrows(k, rows, w):
        sel(Wm(k), A("ZB", 0, 144), [[-16, 9], [200, 16]], -rows[0] - 3000, w)
        for r in rows[1:]:
            sel(Wm(k, 15, 128, 16), Wm(k, 15, 128, 16), [[-16, 8]], -r, w)

    def weave(*makers):
        chains = []
        for make in makers:
            n = len(ops)
            make()
            chains.append(ops[n:])
            del ops[n:]
        for k in range(max(len(c) for c in chains)):
            ops.extend(c[k] for c in chains if k < len(c))

    def rows2list(o, k, n, c, start=True, stop=True):
        mm(o, [(Wm(k, 15 - q, 143 - q), A(n, c + q, c + 1024, 16)) for q in range(16)], start, stop)

    dg = [[-1, 128]]
    zb, nf = A("ZB", 0, 128), A("FF", 256, 512, 1, 0, 8)

    def Y(n, c0=0, c1=144, p1=128, st=1):
        k = 144 * MY.index(n); return A("YM", k + c0, k + c1, st, 0, p1)

    def first(k, w=1):
        return Q("pL%d" % (k == 0), 2, k, w)

    def setup(kind, h, e):
        if kind == "load":
            dma(A("EI", 0, 256, 1, 0, 64), X(T.kid0[:]), "dk", "S")
            dma(A("EI", 0, 256, 1, 64, 128), X(T.kid1[:]), "dk")
            dma(A("EI", 256, 512), X(T.belts[:]), "db")
            dma(A("FI", 0, 256, 1, 0, 8), X(T.flip[:]), "df", "S")
            dma(A("TF0", 0, 2048), X(T.faces[:]), "dp")
        elif kind == "zero":
            ms(A("ZB"), 0.0)
        elif kind == "io":
            iota(A("IO2"), dg, 0, 1)
        elif kind == "eye":
            ts(cf("If"), A("IO2"), 0.0, ALU.is_equal)
        elif kind == "tk":
            if h == 0:
                ms(TK(0, 0, 2048), 0.0)
            else:
                cp(TK(1, 0, 2048), TK(0, 0, 2048), "S")
        elif kind == "bk":
            dma(TK(h, 2048, 4096), TK(h, 0, 2048), "dc%d" % h, e or "Y")
        elif kind == "bm":
            if h == 0:
                ts(A("SI", 768, 1024), A("EI", 256, 512), 4094, ALU.bitwise_and)
            else:
                lin(A("PS", 512, 768), A("SI", 768, 1024), 1.0 / 4096, -1.0)
        elif kind == "xk":
            lin(A("p16"), L("pZ", 2, 4), 2048.0, 4096.0)
        elif kind == "cols":
            ms(col(5, 0, 64), 8191.0); ms(col(6, 0, 64), -8192.0); ms(col(5, 64, 128), -8193.0); ms(col(6, 64, 128), 0.0)
        elif kind == "ga":
            def put(n, o, w, old=False):
                sel(Y(n), Y(n) if old else A("ZB", 0, 144), [[-16, 9], [300, 2], [-2, 8]], -300 - o, w)
            if h == 0:
                put("OE", 1, 1.0); put("E", 0, 1.0); put("OE", 0, -1.0, True)
            elif h == 1:
                for n, w in (("GP", BIG), ("GN", -BIG)):
                    sel(Y(n, p1=8), A("ZB", 0, 144, 1, 0, 8), [[-1, 9], [300, 2], [0, 8]], -300, w)
            else:
                put("SO", 2, 1.0); put("O", 1, 1.0)
                sel(Y("SO", 15, 143, st=16), A("ZB", 0, 8), [[-16, 8]], 0, 1.0)
                put("SO", 1, -1.0, True)
        elif kind == "sa":
            for n, s in ((("Ib", 1.0), ("nIb", -1.0), ("I4k", 4096.0)), (("Kp", BIG), ("Kn", -BIG), ("Ip", 4 * SB)), (("nhI", -2048.0), ("I2", 2.0)), ())[h]:
                if e == "S":
                    act(cb(n), cf("If"), s)
                else:
                    ts(cb(n), cf("If"), s, ALU.mult)
            for n, c in (("C20", 20.0), ("EI8", 0.125), ("CC", C23 / 32)) if h == 3 else ():
                if e == "S":
                    act(cb(n), zb, 1.0, c)
                else:
                    ms(cb(n), c)
        elif kind == "an":
            ts(A("SI", 256 * h, 256 * h + 256), A("EI", 256 * h, 256 * h + 256), 1, ALU.bitwise_and)
        elif kind == "nf":
            ts(nf, A("FI", 0, 256, 1, 0, 8), 0.0, ALU.is_equal)
        elif kind == "ba":
            if h == 0:
                ts(A("SI", 512, 768), A("EI", 256, 512), 1, ALU.arith_shift_right)
            elif h == 1:
                lin(A("PS", 0, 256), A("SI", 512, 768), 1.0 / 2048, -1.0)
            else:
                lin(A("PS", 256, 512), A("SI", 256, 512), 2.0, -1.0)
        elif kind == "ka":
            if h == 0:
                ts(A("pV0", 0, 256), A("SI", 0, 256), col(5), ALU.mult, col(6), ALU.add)
            elif h == 1:
                tt(A("pV0", 256, 512), A("pV0", 0, 256), A("EI", 0, 256), ALU.add)
            elif h == 2:
                cp(A("KP", 0, 256), A("pV0", 256, 512))
            else:
                tt(A("KP", 256, 512), A("pV0", 256, 512), A("KP", 0, 256), ALU.subtract)
        elif kind in ("kh", "kl"):
            for r in (0, 1) if kind == "kh" else (2, 3):
                dma(TK(h, 0, 2048, slice(4 * r + h, 128, 16), key=(r,)),
                    A("KP", 256 * (r // 2), 256 * (r // 2) + 256, 1, 64 * (r % 2), 64 * (r % 2) + 64), "kd", e or "Y")
        elif kind == "dv":
            dma(A("TF0", 2048, 4096), X(T.faces[:]), "dv", e or "Y")
        elif kind == "ff":
            lin(A("FF", 0, 256, 1, 0, 8), nf, -2 * SB / BIG, SB / BIG, e)
        elif kind == "eo":
            def slots(n):
                return [(Y(n, 8 - 8 * b, 136 - 8 * b), A("PS", 256 * k + b, 256 * k + 256, 2)) for b in range(2) for k in (h & 2, 1)]
            off = [(Y(n, 8 - 8 * b, 136 - 8 * b, 8), A("FF", 256 + b, 512, 2, 0, 8)) for n in ("GP", "GN") for b in range(2)]
            mm(first(h) if h < 2 else L("pZ", 2, 4), slots(("OE", "SO")[h % 2]) + off + slots("EO"[h % 2]))
        elif kind == "eg":
            mm(first(2), [(Y("GP", 8 - 8 * b, 136 - 8 * b, 8), A("FF", b, 256, 2, 0, 8)) for b in range(2)])
        elif kind == "xf":
            lin(Q("X16", 2, h), first(h), 2048.0, 4096.0)
        elif kind == "in":
            cp(Q("IN0", 2, h, 1 + h), first(h, 1 + h), e)
        elif kind == "fa":
            flip(A("TF0", 4096 + 1024 * h, 5120 + 1024 * h), A("TF0", 1024 * (h % 2), 1024 * (h % 2) + 1024), e)
        elif kind == "fb":
            dma(A("TF0", 6144 + 1024 * h, 7168 + 1024 * h), A("TF0", 4096 + 1024 * h, 5120 + 1024 * h), "dn%d" % (2 + h), e or "Y")
        elif kind == "gb":
            if h == 0:
                weave(lambda: wrows(0, [4, 12, 1, 9], 1.0), lambda: wrows(1, [0, 8, 5, 13], 1.0 / 4096))
            else:
                wrows(3, [0, 8], 1.0)
        elif kind == "gc":
            if h == 0:
                op("G", [lambda: g.iota(T.COI[:, 0:1], [[0, 1]], 0, 1)], [A("COI", 0, 1)], [])
                iota(cb("C16"), [[16, 128]], 0, 0)
                return
            iota(Wm(2), [[0, 144]], 0, 0)
            iota(cb("nB4"), [[0, 128]], -2, 0)
            iota(Wm(2, 15, 128, 16), [[0, 8]], 1, 0)
            iota(cb("B8I"), [[0, 128]], 1, 0)
            sel(Wm(2, 15, 128, 16), Wm(2, 15, 128, 16), [[-16, 8]], 0, 0.0, ALU.is_ge)
            sel(Wm(2, 15, 128, 16), Wm(2, 15, 128, 16), [[16, 8]], 15, 0.0, ALU.is_ge, -1)
        elif kind == "ge":
            for pat, base, cm in (([[-8, 16], [0, 8]], 0, 1), ([[8, 16], [0, 8]], 7, -1)):
                for n in ("B8I", "nB4"):
                    sel(cb(n), cb(n), pat, base, 0.0, ALU.is_ge, cm)
            sel(cb("B8I"), cb("B8I"), dg, 0, 9.0)
        elif kind == "gd":
            def shift(n, o, w, c):
                sel(cb(n), zb, dg, o, w)
                sel(cb(n, c, 128, 8), A("ZB", 0, 16), [[-8, 16]], c - 7, w)
                if n != "Dn":
                    sel(cb(n), cb(n), dg, 0, -w)
            weave(lambda: shift("IDn", 1, -1.0, 0), lambda: shift("UpI", -1, 1.0, 7), lambda: shift("Dn", 1, 1.0, 0))
        elif kind == "gr":
            for k in range(2):
                sel(A("RL", 160 * k, 160 * k + 160), A("ZB"), [[-16, 5], [300, 2], [-1, 16]], -64 * k - 300, 1.0)
        elif kind == "br":
            mm(A("pA", 0, 320), [(cb("B8I"), A("RL"))])
        elif kind == "bs":
            cp(A("BR"), A("pA", 0, 320), e)
        elif kind == "gw":
            o = A("WB", 1024 * h, 1024 * h + 1024)
            if h < 2:
                iota(o, [[0, 1024]], 0, 0)
            sel(o, o if h < 2 else A("WB", 1024 * h - 2048, 1024 * h - 1024), [[-16, 4], [0, 16], [-1, 16]], -64 * (h % 2), BIG if h < 2 else -BIG)
        elif kind == "va":
            lin(A("CH", 0, 128), cf("If"), 2.0 ** -10 - 1.0, 0.0, e)
            lin(A("CH", 128, 256), cf("If"), 2.0 ** -11 - 0.5, 0.0, e)
        elif kind == "vc":
            ms(A("ONE", 0, 512, 1, 0, 32), 1.0); ms(col(2), -7.5); ms(A("CT"), 2 * SB)
        elif kind == "vb":
            if h == 0:
                ts(A("COI", 4, 5), A("COI", 0, 1), 15, ALU.bitwise_and)
            elif h == 1:
                ts(col(1), A("COI", 4, 5), 2048.0, ALU.add)
                ts(col(8), A("COI", 4, 5), -2048.0, ALU.add)
            else:
                ts(A("CM"), cb("C16"), col(8), ALU.add, 1.0 / 2048, ALU.mult)
        elif kind == "bg":
            if h == 0:
                dma(A("TF1", 0, 2048), X(T.faces[:]), "df1", e or "Y")
            else:
                dma(A("TF1", 4096, 6144), A("TF0", 4096, 6144), "dn1", e or "Y")
        elif kind == "op":
            for k in range(2):
                mm(A("pV%d" % h, 64 * k, 64 * k + 64),
                   [(Wm(3 - 3 * k, 15 - q, 143 - q), TK(0, 1024 * h + q, 1024 * h + 1024, st=16)) for q in range(16)])
        elif kind == "oh":
            cp(Zc(h, 0), A("pV%d" % h, 0, 128), e)
        elif kind == "ol":
            tt(Zc(h, 1), A("pV%d" % h, 0, 128), Zc(h, 0), ALU.subtract)
        else:
            raise ValueError(kind)

    def outputs_of_the_drawn(k):
        if k == 0:
            cp(A("KF"), A("EI", 0, 256))
        elif k == 1:
            dma(X(T.yx[:, 0:2048]), A("TF0", 0, 2048), "dyx")
            dma(X(T.y0[:, 0:2048]), A("KF", 0, 256, 1, 0, 64), "dy")
            dma(X(T.y1[:, 0:2048]), A("KF", 0, 256, 1, 64, 128), "dy")

    def pairs_to_slots(b):
        p8, pz, w = [[-16, 8], [-1, 8]], [[-16, 8], [-1, 8], [300, 2]], 4096.0
        sel(cb("a%d" % b), zb, pz, -8 * b - 300, w)
        sel(cb("b%d" % b), zb, pz, -8 * b + 1, w)
        sel(cb("c%d" % b), zb, pz, -8 * b, w)
        sel(cb("d%d" % b), zb, pz, -8 * b + 1, -w)
        sel(cb("b%d" % b, 0, 128, 16), A("ZB", 0, 8), [[-16, 8]], -8 * b - 7, w)
        sel(cb("c%d" % b, 1, 128, 2), cb("c%d" % b, 1, 128, 2), p8, -8 * b, -w)
        sel(cb("d%d" % b, 0, 128, 16), A("ZB", 0, 8), [[-16, 8]], -8 * b - 7, -w)
        sel(cb("e%d" % b), zb, [[-16, 8], [0, 16]], -8 * b, BIG)
        sel(cb("d%d" % b, 1, 128, 2), cb("d%d" % b, 1, 128, 2), p8, -8 * b, w)
        sel(cb("f%d" % b), zb, [[-16, 8], [0, 16]], -8 * b, -BIG)
        sel(cb("FT", 8 * b, 8 * b + 8), A("ZB", 0, 8), [[-16, 8]], -8 * b, -1.0)

    def kid_rows(t, h, turn, q):
        c = 2048 + 1024 * h
        for k in range(2):
            dma(TK(turn, c, c + 1024, slice(64 * k + turn, 64 * k + 64, 4), key=(10 + k,)),
                (T.KS[:, h, k, :, :], [("KS", h, h + 1)]), "kc%d%d" % (t, h), q)

    def blocks(n, k, c0):
        return A(n, 160 * k + 16 - 16 * c0, 160 * k + 144 - 16 * c0)

    def to_blocks(h, summed, stop):
        for k in range(2):
            if summed:
                terms = [(blocks("RL", k, c0), (T.Z[:, h, 128 * p + c0:128 * p + 128:2], Zc(h, p)[1])) for p in range(2) for c0 in range(2)]
            else:
                terms = [(blocks("RL", k, c0), (T.Z[:, h, c0:256:2], Zc(h, 0)[1] + Zc(h, 1)[1])) for c0 in range(2)]
            mm(pB(k, 0, 2 if summed else 4), terms, k == 0, stop and k == 1)

    def old_kids(h, summed, w, stop=False):
        if summed:
            for k in range(2):
                c = 256 * h + 128 * k
                acc(pB(k, 0, 2), [(w, A("ZR", c, c + 64)), (w, A("ZR", c + 64, c + 128))], stop and k == 1)
        else:
            acc(pB(2), [(w, A("ZR", 256 * h, 256 * h + 256))], stop)

    def step(name, t):
        if name[-1] in "+-":
            name, t = name[:-1], t + (1 if name[-1] == "+" else -1)
        last = t == RO - 1
        UQ = "uq" in ORDER[t].split()
        tf, tfn, inb, rb = "TF%d" % (t % 2), "TF%d" % ((t + 1) % 2), "IN%d" % t, "R%d" % t
        if name[0] in "KHUS":
            a, b, e = int(name[1]), int(name[2]), name[3:]
            h = a // 2
            k = "KH".find(name[0])
            x16 = (T.X16[:, h, max(k, 0), 32 * a - 64 * h:32 * b - 64 * h], Q("X16", h, max(k, 0))[1])
            if name[0] == "K":
                cp(A("G", 512 * a, 512 * b), IX(A("TK"), x16) if t else IX(A("TK", 0, 6144), A("p16", 32 * a, 32 * b)), e)
            elif name[0] == "H":
                cp(A("FW", 512 * a, 512 * b), IX(A(tf, 0, 8192), x16), e)
            elif name[0] == "U":
                tt(A("D", 512 * a, 512 * b), IX(A(tf, 0, 8192), A("u16", 32 * a, 32 * b)), A("FW", 512 * a, 512 * b), ALU.subtract)
            else:
                flip(A(tfn, 2048 + 512 * a, 2048 + 512 * b), IX(A(tf, 6144 + 1024 * h, 9216 + 1024 * h), A("m16", 32 * a, 32 * b)), e)
            return
        e = name[-1] if name[-1] in "VS" else ""
        kind = name.rstrip("VS")
        h = int(kind[-1]) if kind[-1].isdigit() else 0
        kind = kind.rstrip("0123")
        Ib, nIb = cb("Ib"), cb("nIb")

        def go(k, w=1):
            return Q("pL%d" % h, 0, k, w)

        def fx(k, w=1):
            return Q("pL%d" % h, 1, k, w)

        def less():
            return [(nIb, Q("PC", h, 0, 2)), (Ib, Q("TN", h, 0, 2))]
        pK, pH, tK, tH, tF = Q("PC", h % 3, 0), Q("PC", h % 3, 1), Q("TN", h % 3, 0), Q("TN", h % 3, 1), Q("TN", h % 3, 2)
        ngo, opn = Q("MK", h % 3, 0), Q("MK", h % 3, 1)
        if kind == "out":
            if t == 1:
                outputs_of_the_drawn(h)
            if h == 2:
                pairs_to_slots(t - 1)
        elif kind in ("af", "ad", "ac", "ev"):
            c, bank = 512 * h, A("pV%d" % (h % 2))
            o = A(tf, 8192 + c, 8704 + c)
            terms = [(A("CH", 0, 128), A("FW", c, c + 512)), (A("CH", 128, 256), A("D", c, c + 512)), (cb("CC", p1=32), A("ONE", 0, 512, 1, 0, 32))]
            if h == 3 and UQ:
                terms[0:2] = [(A("CH", 128, 256), A("FW", c, c + 512)), (A("CH", 128, 256), A("UQ"))]
            if kind == "ac" and e == "V":
                op("X", [], [], [])
            elif kind != "ev":
                k = "fdc".index(kind[1])
                mm(bank, terms[k:k + 1], k == 0, k == 2 or e == "V")
            elif e == "S":
                act(o, bank, 1.0, 255.0 - C23)
            else:
                ts(o, bank, C23, ALU.add, C23 - 255.0, ALU.subtract)
        elif kind in ("bf", "bd", "bo", "bw", "be"):
            c, bank = 1024 + h, A("pV%d" % h)
            old, new = A(tf, 2048 + c, 4096, 2), A(tfn, 2048 + c, 4096, 2)
            if kind == "bw":
                for k in range(8):
                    acc(A("pV%d" % h, k, 512, 8), [(A("WB", 2048 * s + 2 * k + h, 2048 * s + 2048, 16), L("MG", 0)) for s in range(2)], k == 7 and e == "V")
                if e == "S":
                    acc(bank, [(nIb, old)], True)
                else:
                    op("X", [], [], [])
            elif kind != "be":
                k = "fdo".index(kind[1])
                if UQ and k < 2:
                    mm(A("pV%d" % h, 0, 256), [(A("CH", 128 * k, 128 * k + 128), A(("FW", "D")[k], c, 1536, 2))], k == 0, False, True)
                    acc(A("pV%d" % h, 256, 512), [(A("CH", 128, 256), (A("FW", c + 512, 2048, 2), A("UQ", h, 512, 2))[k])])
                else:
                    mm(bank, [((A("CH", 0, 128), A("FW", c, 2048, 2)), (A("CH", 128, 256), A("D", c, 2048, 2)), (Ib, old))[k]], k == 0, False)
            elif e == "S":
                act(new, bank, -1.0)
            else:
                tt(new, old, bank, ALU.subtract)
        elif kind == "mg":
            ts(L("MG", 0), L("pZ", 1, 0, 3), 6.0, ALU.is_lt, C23 / BIG, ALU.max)
        elif kind == "mh":
            lin(L("MG", 1), L("MG", 0), -1.0, 0.0, e)
        elif kind == "ar":
            op("X", [], [Q(inb, h, 0, 3)], [], "rs%d%d" % (t - 1, h), neng)
        elif kind == "x":
            lin(Q("X16", h, 0, 2), Q(inb, h, 0, 2), 2048.0, 4096.0)
        elif kind == "tn":
            act(Q("TN", h, 0, 3), Q(inb, h, 0, 3), -1.0, -SB, None, ACT.Sign)
        elif kind == "te":
            act(Q("TE", h, 0, 3), Q(rb, h, 0, 3), -1.0, -SB, None, ACT.Sign)
        elif kind == "pc":
            tt(Q("PC", h, 0, 2), Q(inb, h, 0, 2), Q("TN", h, 0, 2), ALU.add)
        elif kind == "pe":
            tt(Q("PC", h, 0, 2), Q(rb, h, 0, 2), Q("TE", h, 0, 2), ALU.add)
        elif kind == "tz":
            ts(Q("T2", h, 0, 2), Q(rb, h, 0, 2), 0.0, ALU.is_ge, 1.0 / 4096, ALU.mult)
        elif kind == "up":
            rows2list(pC(h, 0), 0, "G", 1024 * h)
        elif kind == "u":
            lin(L("u16", h), pC(h, 0), 0.5, 4096.0)
        elif kind == "ph":
            mm(pC(h, 1), [(cb("I4k"), pH), (cb("I4k"), tH)])
        elif kind == "a":
            rows2list(go(0), 1, "G", 1024 * h, False, False)
        elif kind == "prc":
            to_blocks(h, last, False)
            old_kids(h, last, nIb)
        elif kind == "py":
            for k in range(2):
                mm(A("pZ", 128 + 192 * h + 32 * k, 160 + 192 * h + 32 * k), [(blocks("BR", k, c0), A("SP", 64 * h + c0, 64 * h + 64, 2)) for c0 in range(2)])
        elif kind == "mj":
            ts(Q("MK", h, 2), L("pZ", h, 2, 3), 6.0, ALU.is_lt)
        elif kind == "mx":
            ts(Q("MK", h, 0, 3), L("pZ", h, 0, 3, 3), 6.0, ALU.is_lt)
        elif kind == "pra":
            mm(go(0, 2), less(), True, False, True)
            acc(go(1), [(Ib, L("CM", h))])
        elif kind == "prb":
            if last:
                acc(fx(0, 2), [(cb("I2"), Q("TN", h, 0, 2))])
            else:
                acc(fx(0), [(cb("IDn"), pH), (cb("IDn"), tH)])
                acc(fx(1), [(cb("UpI"), pK), (cb("UpI"), tK)])
                wipe(fx(0), tF); wipe(fx(1), tF)
                acc(fx(0, 2), less())
                acc(fx(0), [(cb("Dn"), pH), (cb("Dn"), tH)])
                acc(fx(1), [(Ib, pK), (Ib, tK)])
            acc(fx(2), [(cb("Ip"), tF), (Ib, A("CT"))])
        elif kind == "nr":
            ts(A("NR", 1024 * h, 1024 * h + 1024), A("D", 1024 * h, 1024 * h + 1024), C28, ALU.add, C28, ALU.is_equal)
        elif kind == "nq":
            ts(A("NR", 512 * h, 512 * h + 512), A("D", 512 * h, 512 * h + 512), C28, ALU.add, C28, ALU.is_equal)
        elif kind == "cnt":
            rows2list(pC(2, h), 2, "NR", 1024 * h)
        elif kind == "uq":
            cp(A("UQ"), IX(A(tf, 0, 8192), A("u16", 96, 128)), "S")
        elif kind == "dq":
            mm(A("pA"), [(Ib, A("UQ")), (nIb, A("FW", 1536, 2048))])
        elif kind == "nz":
            ts(A("NR", 1536, 2048), A("pA"), C28, ALU.add, C28, ALU.is_equal)
        elif kind == "sp":
            act(L("SP", h), pC(2, h), 0.875, col(2), None, ACT.Sign)
        elif kind == "pz":
            mm(L("pZ", h, 0, 3), [(cb("B8I"), L("SP", h))])
            mm(L("pZ", h, 1, 3), [(cb("nB4"), L("SP", h))])
        elif kind == "mk":
            ts(Q("MK", h, 0, 2), L("pZ", h, 0, 3, 2), 6.0, ALU.is_lt)
        elif kind == "pk":
            mm(L("pZ", h, 6), [(Ib, cb("C16", 0, 64)), (cb("nhI"), ngo)])
        elif kind == "m":
            ts(L("m16", h), L("pZ", h, 6), col(1), ALU.add)
        elif kind == "kw":
            for r in range(2 if last else 4):
                wipe(pB(2, r, r + 1), Q("MK", h, 2), r == 3 and e == "V")
            if last:
                acc(pB(2, 0, 1), [(cb("I4k"), A("CT"))])
            if e == "V" and not last:
                op("X", [], [], [])
            else:
                old_kids(h, last, Ib, True)
        elif kind == "hi":
            cp(Zc(h, 0), pC(h, 0, 2), e)
        elif kind == "lo":
            tt(Zc(h, 1), pC(h, 0, 2), Zc(h, 0), ALU.subtract)
        elif kind == "tr":
            to_blocks(h, False, True)
        elif kind == "ks":
            zr = A("ZR", 256 * h, 256 * h + 256)
            if e == "V":
                tt(zr, pB(2), zr, ALU.add)
            else:
                cp(zr, pB(2), e)
        elif kind == "kv":
            for c in range(4):
                i = A("ZR", 256 * h + c, 256 * h + 256, 4)
                op("V", [lambda c=c, i=i: g.vector.transpose(T.KS[:, h, :, c, :], i[0])], [(None, [("KS", h, h + 1, c)])], [i])
        elif kind == "rk":
            for k in range(2):
                dma((T.KS[:, h, k, :, :], [("KS", h, h + 1)]), TK(0, 1024 * h, 1024 * h + 1024, slice(64 * k, 64 * k + 64, 4)), "ku0%d" % h, e or "Y")
        elif kind == "rv":
            for c in range(4):
                o = A("ZR", 256 * h + c, 256 * h + 256, 4)
                op("V", [lambda c=c, o=o: g.vector.transpose(o[0], T.KS[:, h, :, c, :])], [(None, [o[1][0] + (c,)])], [(None, [("KS", h, h + 1)])])
        elif kind == "kd":
            kid_rows(t, h, 0, e or "Y")
        elif kind == "kt":
            kid_rows(t, h, 1, e or "Y")
        elif kind == "ku":
            c = 2048 + 1024 * h
            dma(TK(1, c, c + 1024, slice(1, 128, 4)), TK(0, c, c + 1024, slice(0, 128, 4)), "ku%d%d" % (t, h), e or "Y")
        elif kind == "lw":
            for k in range(2):
                wipe(go(k), ngo)
            for k in range(3):
                wipe(fx(k), opn, k == 2)
        elif kind == "r":
            tt(Q(rb, h, 0, 3), fx(0, 3), Q(inb, h, 0, 3), ALU.add)
        elif kind == "s":
            tt(Q(rb, h, 0, 2), go(0, 2), Q(rb, h, 0, 2), ALU.add)
            if not last:
                r = Q(rb, h, 0, 3)
                op("G", [lambda: g.remote_dma(Q("IN%d" % (t + 1), h, 0, 3)[0], r[0], T.sem["rs%d%d" % (t, h)],
                                              T.sem["ls%d%d" % (t, h)], pid, rid, rmask)], [], [r], "ls%d%d" % (t, h), neng)
        elif kind == "flip":
            flip(A(tfn, 6144 + 1024 * h, 7168 + 1024 * h), A(tfn, 2048 + 1024 * h, 3072 + 1024 * h), e)
        elif kind == "fq":
            flip(A(tfn, 6144 + 512 * h, 6656 + 512 * h), A(tfn, 2048 + 512 * h, 2560 + 512 * h), e)
        elif kind == "par":
            mm(pC(3, 0), [(cb("EI8"), Q("MK", hh, 1)) for hh in range(2)])
        elif kind == "thr":
            if h == 0:
                act(A("JK"), pC(3, 0), bias=-9.5 / 64, acc=col(3))
            elif h == 1:
                act(col(4), col(3), 0.5, C23)
            elif h == 2:
                act(col(9), col(4), -2.0, 2 * C23 - 8.0)
            else:
                act(col(2), col(3), 1.0, col(9))
        elif kind == "yx":
            dma(X(T.yx[:, 2048 + 512 * h:2560 + 512 * h]), A(tfn, 2048 + 512 * h, 2560 + 512 * h), "ox%d" % h, e or "Y")
        elif kind == "yt":
            for k in range(2):
                ts((T.YT[:, :, k, :], [("YT", k, k + 1)]), pB(2, k, k + 1), 0.0, ALU.is_lt, 8191.0 + 2 * k, ALU.mult)
        elif kind == "yu":
            tt(L("YK", h, 0, 2, 2), pB(2, 0, 2), (T.YT[:], [("YT", 0, 2)]), ALU.add)
        elif kind == "ys":
            o, i = A("YS", 128 * h, 128 * h + 128), L("YK", h, 0, 2, 2)
            op("V", [lambda: g.vector.transpose(o[0], i[0])], [o], [i])
        elif kind in ("yk", "yq"):
            y, c = (T.y0, 128 * h) if kind == "yk" else (T.y1, 128 * h + 32)
            for k in range(2):
                dma(X(y[4 * k:4 * k + 4, 2048 + 1024 * h:3072 + 1024 * h]), A("YS", c + 64 * k, c + 64 * k + 32), "oy%d" % h, e or "Y")
        elif kind == "ybp":
            bank = T["pL%d" % h]

            def back(k, n):
                return [(cb(n), Q("PC", h, k)), (cb(n), Q("T2", h, k))]
            for b in range(2):
                mm((bank[:, 0, 2:4, b:64:2], go(2, 2)[1]),
                   back(0, "c%d" % b) + back(1, "d%d" % b) + [(cb("e%d" % b), tF), (cb("f%d" % b), tF)] + back(0, "a%d" % b) + back(1, "b%d" % b))
        elif kind == "yfp":
            bank = T["pL%d" % h]
            for b in range(2):
                mm((bank[0:8, 1, 2:4, b:64:2], fx(2, 2)[1]), [(cb("FT", 8 * b, 8 * b + 8), Q("TE", h, 2))])
        elif kind == "yb":
            lin(A("YB", 128 * h, 128 * h + 128), go(2, 2), 1.0, 4096.0, e)
        elif kind == "yc":
            dma(X(T.yb[:, 128 * h:128 * h + 128]), A("YB", 128 * h, 128 * h + 128), "ob%d" % h, e or "Y")
        elif kind == "yf":
            cp(A("YF", 128 * h, 128 * h + 128, 1, 0, 8), (T["pL%d" % h][0:8, 1, 2:4, :], fx(2, 2)[1]), e)
        elif kind == "yg":
            dma(X(T.yf[:]), A("YF", 0, 256, 1, 0, 8), "of", e or "Y")
        else:
            setup(kind, h, e)

    for t in range(RO):
        for name in ORDER[t].split():
            tag[0] = (name, t)
            step(name, t)
    emit(g, T, ops)


def meets(a, b):
    return a[1] < b[2] and b[1] < a[2] and (len(a) < 4 or len(b) < 4 or a[3] == b[3])


def emit(g, T, ops):
    queue = {"V": g.vector, "S": g.scalar, "P": g.tensor, "G": g, "Y": g.sync}
    own = {"V": "sV", "S": "sS", "P": "sP", "G": "sG"}
    total = {}
    for o in ops:
        if o["sem"] is not None:
            total[o["sem"]] = total.get(o["sem"], 0) + o["n"]
    count = {s: 0 for s in own.values()}
    known = {e: {} for e in queue}
    hist = {}
    for i, o in enumerate(ops):
        e = o["e"]
        need = {}
        for kind in ("r", "w"):
            for r in o[kind]:
                psum = SCRATCH[r[0]][0] == "psum"
                for (r2, kind2, o2) in hist.get(r[0], []):
                    if o2["e"] == "P" and e == "P":
                        continue
                    if o2["sem"] is not None and o2["sem"] == o["sem"]:
                        continue
                    if (psum and o2["e"] != e) or (meets(r, r2) and "w" in (kind, kind2)):
                        s, v = o2["tok"]
                        if v > need.get(s, (0, None))[0]:
                            need[s] = (v, o2)
        if e != "X":
            for s, (v, o2) in sorted(need.items(), key=lambda x: -x[1][1]["i"]):
                if known[e].get(s, 0) < v:
                    queue[e].wait_ge(T.sem[s], v)
                    known[e][s] = v
                    for s2, v2 in o2["kn"].items():
                        known[e][s2] = max(known[e].get(s2, 0), v2)
            o["kn"] = dict(known[e])
            for fn in o["fns"]:
                ins = fn()
                if o["sem"] is None:
                    count[own[e]] += 1
                    ins.then_inc(T.sem[own[e]], 1)
            if o["sem"] is None:
                o["tok"] = (own[e], count[own[e]])
            else:
                if o["sem"] in DSEM:
                    ins.then_inc(T.sem[o["sem"]], 16)
                    if total[o["sem"]] > 16:
                        o["kn"] = {}
                o["tok"] = (o["sem"], total[o["sem"]])
        else:
            o["kn"] = {}
            o["tok"] = (o["sem"], o["n"])
        o["i"] = i
        for kind in ("r", "w"):
            for r in o[kind]:
                hist.setdefault(r[0], []).append((r, kind, o))
    for s, v in list(count.items()) + list(total.items()):
        if known["Y"].get(s, 0) < v:
            g.sync.wait_ge(T.sem[s], v)
